import numpy as np, ml_dtypes
CORES = [9,25,41,57]
N = 4
import mx_ref
BF = ml_dtypes.bfloat16
def gcols(t, e):
    v = np.concatenate([t.reshape(8, 16, -1, 4), np.zeros((8, 16, 1, 4), BF)], axis=2)
    return np.ascontiguousarray(np.stack([v[g][:, e[g]] for g in range(8)])).reshape(128, -1)
def tile(rs):
    return np.stack(rs, axis=2).reshape(128, -1).astype(BF)
def pick(q, e):
    c = np.concatenate([q[0].reshape(128, -1, 4), np.zeros((128, 1, 4), np.uint8)], axis=1); s = np.concatenate([q[1], np.ones((16, 1), np.uint8)], axis=1)
    return (np.ascontiguousarray(c[:, e].reshape(128, -1)), np.ascontiguousarray(s[:, e]))
def join(*qs):
    return (np.concatenate([q[0] for q in qs], axis=1), np.concatenate([q[1] for q in qs], axis=1))
def put(q, e, v):
    c, s = q[0].reshape(128, -1, 4).copy(), q[1].copy(); c[:, e] = v[0].reshape(128, -1, 4); s[:, e] = v[1]
    return (c.reshape(128, -1), s)
def pk(c, s):
    return (np.ascontiguousarray(c), mx_ref.live(s))
def emit(q):
    return q[0], q[1]
def packed(v, rng):
    q = [mx_ref.quantize(np.ascontiguousarray(v[r])) for r in range(N)]
    return np.stack([a for a, b in q]), np.stack([mx_ref.plane(b, rng) for a, b in q])
def values_of_codes():
    e, c = np.zeros((128, 128, 4), np.float32), np.zeros((128, 2, 4), np.uint8)
    e[np.arange(128), np.arange(128), 0] = 1
    c[:127, :, 0] = np.arange(256).reshape(2, 128).T[:127]
    return mx_ref.matmul(mx_ref.quantize(e.reshape(128, 512).astype(BF)), (c.reshape(128, 8), np.full((16, 2), 127, np.uint8))).T.reshape(-1).astype(np.float64)
CODE_VALUE, SCALE_VALUE = values_of_codes(), 2.0 ** (np.arange(256) - 127.0)
def decode(q):
    return (CODE_VALUE[q[0]].reshape(16, 8, -1, 4) * SCALE_VALUE[q[1]][:, None, :, None] + 0.0).reshape(128, -1).astype(np.float32)
def f(rng, *shape):
    return mx_ref.flush((rng.standard_normal(shape, dtype=np.float32) * np.exp2(rng.integers(-2, 3, shape[:-1] + (1,)))).astype(BF))
def wide(rng, *shape, cols=0):
    v = rng.standard_normal(shape, dtype=np.float32) * np.exp2(rng.integers(-12, 13, shape)).astype(np.float32)
    if cols: v *= np.repeat(np.exp2(rng.integers(-cols, cols + 1, shape[:-2] + (1, shape[-1] // 4))) * (rng.random(shape[:-2] + (1, shape[-1] // 4)) > 0.0625), 4, axis=-1).astype(np.float32)
    return mx_ref.flush(v.astype(BF))
C, K, M, S, H = 320, 64, 5, 14, 160
PARTNER = [1, 2, 3]
COL = np.stack([M * ((np.arange(K) + 8 * g) % K)[:, None] + np.arange(M) for g in range(8)])
CLOCK = np.stack([(np.arange(C) // M - 8 * g) % K for g in range(8)])
def big(v):
    v = v.astype(np.float32)
    v[np.abs(v) < np.float32(2.0 ** -20)] = 0
    return v.astype(BF)
def numbers_of(rng):
    return {"x": big(f(rng, N, 128, 4 * C)), "u": np.array(f(rng, N, 128, 512)), "v": np.array(f(rng, N, 128, 512))}
def weights(rng, w):
    c, s = packed(np.ascontiguousarray(w.reshape(N, 128, 4, 512).transpose(0, 1, 3, 2)).reshape(N, 128, 2048).astype(BF), rng)
    return {"wc": c, "ws": s}
def layers(rng, still=()):
    w = np.zeros((N, 512, 512), np.float32)
    for r in range(N): w[r, rng.integers(0, 512, (24, 512)), np.arange(512)] = rng.choice([-1.0, 1.0], (24, 512)) * (16 + 20 * rng.random((24, 512)))
    w = w.reshape(N, 8, 16, 4, 512)
    for i in still:
        w[:, :, i] = 0
        w[..., i::16] = 0
    return weights(rng, w.reshape(N, 512, 512))
def setup_inputs(rng):
    return {**numbers_of(rng), **layers(rng)}
def setup_inputs_ties(rng):
    d = numbers_of(rng)
    o = rng.permutation(N)
    x = d["x"].reshape(N, 8, 16, C, 4)
    s = rng.integers(-1, 2, (N, 8, C, 4)).astype(np.float32)
    s[..., 3] -= 1
    s[o[0]] = 0
    s[o[1], :, :, :3] = 1
    for g in range(8): s[o[2], g, :, :3] = [2.0 * (g >> 2 & 1) - 1, 2.0 * (g >> 1 & 1) - 1, 2.0 * (g & 1) - 1]
    x[:, :, 0] = s.astype(BF)
    e = (N, 8, 8, C, 4)
    x[:, :, 8:] = (rng.choice([-1.0, 1.0], e) * (1 + (2 * rng.integers(0, 64, e) + 1) * 2.0 ** -7) * np.exp2(-rng.integers(8, 15, e).astype(np.float64))).astype(np.float32).astype(BF)
    x[:, :, 8, :, 0] = 1.96875
    u = d["u"].reshape(N, 128, 128, 4)
    for b in range(4): u[:, :, b::16] = 0
    for h in range(0, 128, 16):
        for b in range(4): u[:, h, h + b, b] = 1
    return {"x": x.reshape(N, 128, 4 * C), "u": u.reshape(N, 128, 512), "v": d["v"], **layers(rng, [0])}
def setup_inputs_near(rng):
    d = numbers_of(rng)
    o = rng.permutation(N) % 2
    x = d["x"].astype(np.float32).reshape(N, 8, 16, C, 4)
    x[:, :, 0] = 0
    x[:, :, 8:] = 0
    u = d["u"].reshape(N, 128, 128, 4)
    for b in range(4): u[:, :, b::16] = 0
    for r in range(N):
        a = rng.integers(-1, 2, (8, C, 3)).astype(np.float32)
        k = rng.choice([-1.0, 1.0], (8, 1))
        if o[r] == 0:
            s = rng.integers(0, 16, (8, C))
            x[r, :, 0, :, :3] = a
            x[r, :, 0, :, 3] = k
            x[r, :, 8] = ((s[:, :, None] >> np.arange(4)) & 1) * np.exp2(np.arange(4) - 23.0)
            x[r, :, 11, :, 0] = 2.0 ** -10
        else:
            x[r, :, 8, :, :3] = a * np.float32(1.125 * 2.0 ** -24)
            x[r, :, 9, :, :3] = a * np.float32(2.0 ** -24)
            e = rng.integers(0, 4, (8, C))
            x[r, :, 10, :, 3] = k * np.array([1.125, 1.375, 0, 0])[e] * 2.0 ** -24 + 0.0
            x[r, :, 12, :, 3] = k * np.array([0, 0, 1.0, 1.25])[e] * 2.0 ** -24 + 0.0
            for g in rng.permutation(8)[:4]: x[r, g, 10, rng.integers(C), 3] = 2.0 ** 29 * rng.choice([-1.0, 1.0])
        for h in range(0, 128, 16):
            if o[r] == 0:
                for b in range(4): u[r, h, h + b, b] = 1
                u[r, h + 8, h + 3] = 1
                u[r, h + 11, h + 3, 0] = 1
            else:
                for b in range(3):
                    u[r, h + 8, h + b, b] = 1.125 * 2.0 ** -30
                    u[r, h + 9, h + b, b] = -1.25 * 2.0 ** -30
                u[r, h + 10, h + 3, 3] = 1.125 * 2.0 ** -30
                u[r, h + 12, h + 3, 3] = 1.25 * 2.0 ** -30
    return {"x": x.reshape(N, 128, 4 * C).astype(BF), "u": u.reshape(N, 128, 512), "v": d["v"], **layers(rng, [0, 8, 9, 10, 11, 12, 13, 14, 15])}
def setup_inputs_twice(rng):
    d = numbers_of(rng)
    e = (N, 8, 16, C, 4)
    x = rng.choice([-1.0, 1.0], e) * (1 + (2 * rng.integers(0, 64, e) + 1) * 2.0 ** -7) * np.exp2(-rng.integers(13, 15, e).astype(np.float64))
    x[:, :, 0] = 0
    x[:, :, 0, :, 0] = 1.96875 * rng.choice([-1.0, 1.0], (N, 8, C))
    x[:, :, 8] = 0
    x[:, :4, 8, :, 0] = rng.choice([3.25, 0.6875], (N, 4, C))
    x[:, 4:, 8:] = 0
    u = d["u"].reshape(N, 128, 128, 4)
    u[:, :, 3::16] = 0
    for h in range(0, 128, 16): u[:, h + 1:h + 8, h + 3, 0] = 1
    w = np.zeros((N, 512, 512), np.float32)
    i = np.arange(9, 16)
    for g in range(4, 8):
        for b in range(4): w[:, 4 * (16 * (g - 4) + i) + b, 128 * b + 16 * g + i] = 1024.0
    return {"x": x.astype(np.float32).reshape(N, 128, 4 * C).astype(BF), "u": u.reshape(N, 128, 512), "v": d["v"], **weights(rng, w)}
def setup_inputs_ends(rng):
    d = numbers_of(rng)
    e = rng.permutation(N)
    o = e % 4
    x = np.zeros((N, 8, 16, C, 4), np.float32)
    u = d["u"].reshape(N, 128, 128, 4)
    v = rng.choice([-1.0, 1.0], (N, 128, 512))
    w = np.zeros((N, 512, 512), np.float32)
    i = np.arange(128)
    for r in range(N):
        if o[r] == 0: x[r] = -2.0 ** 30 * (1 - 0.125 * rng.integers(0, 2, (8, 1, C, 1)))
        elif o[r] == 1: x[r] = 2.0 ** 30 * rng.choice([-1.0, 1.0], (1, 1, C, 1))
        elif o[r] == 2: x[r] = 2.0 ** -24
        else: x[r] = 2.0 ** 30 * rng.choice([-1.0, 1.0], (8, 16, C, 4))
        if e[r] == 0: x[r][:, :, np.isin(np.arange(C) // M % 8, rng.permutation(8)[:4])] = -2.0 ** 30
        if o[r] == 2:
            for b in range(4): u[r, :, b::16] = 2.0 ** -30
        else:
            for b in range(3): u[r, :, b::16] = (2.0 ** 30 * rng.choice([-1.0, 1.0], (128, 8, 4))).astype(np.float32).astype(BF)
            u[r, :, 3::16] = 2.0 ** 30 if e[r] == 0 or o[r] == 1 else 0.875 * 2.0 ** 30
            for h in range(0, 128, 16): u[r, h:h + 16, h + 3] = 2.0 ** 30
        v[r] *= 2.0 ** 30 if o[r] % 2 == 0 else 2.0 ** -30
        for b in range(4): w[r, 4 * i + b, 128 * b + i] = -1024.0 if o[r] == 1 else 1024.0
    return {"x": x.reshape(N, 128, 4 * C).astype(BF), "u": u.reshape(N, 128, 512), "v": v.astype(np.float32).astype(BF), **weights(rng, w)}
def setup_inputs_spread(rng):
    d = setup_inputs(rng)
    d["x"] = big(wide(rng, N, 128, 4 * C, cols=6))
    return d
def check_inputs(d):
    b = []
    for k, low in (("x", 2.0 ** -24), ("u", 2.0 ** -30), ("v", 2.0 ** -30)):
        a = np.abs(d[k].astype(np.float32))
        if not (np.isfinite(a).all() and ((a == 0) | (a >= low) & (a <= 2.0 ** 30)).all()): b.append("a value of " + k)
    none, least, most = [emit(mx_ref.quantize(np.full((128, 16), k, np.float32).astype(BF)))[1][0, 0] for k in (0.0, 2.0 ** -30, 2.0 ** 30)]
    for r in range(N):
        if ((d["wc"][r] == 0x7F) | (d["wc"][r] == 0xFF)).any(): b.append("wc: a code that is no number")
        s = mx_ref.live(d["ws"][r])
        if ((s != none) & ((s < least) | (s > most))).any(): b.append("ws: a scale out of range")
        with np.errstate(all="ignore"):
            a = np.sum(np.abs(decode(pk(d["wc"][r], d["ws"][r]))).astype(np.float64).reshape(128, 512, 4), axis=(0, 2))
            if not (a <= 1024).all(): b.append("sizes in a column of W")
    return b
def walk(s):
    key = np.take_along_axis(s[3::16] + np.float32(0.0), COL.reshape(8, C), axis=1).reshape(8, K, M)
    pile = np.take_along_axis(COL, np.argsort(-key, axis=2, kind="stable"), axis=2)
    sign = 4 * (s[0::16] > 0) + 2 * (s[1::16] > 0) + (s[2::16] > 0)
    k, h, used = np.arange(K), np.arange(K) % 8, np.zeros((8, K), np.int64)
    when = S * K + np.arange(C) + np.zeros((8, 1), np.int64)
    drawn = []
    for n in range(S):
        for i in range(7): h = np.where(used[h, k] == M, (h + 1) % 8, h)
        c = pile[h, k, used[h, k]]
        used[h, k] += 1
        when[h, c] = K * n + k
        drawn.append((h, c))
        h = sign[h, c]
    before = drawn[-1][1][CLOCK]
    for n in range(1, S): before[drawn[n]] = drawn[n - 1][1]
    q = np.argsort(when, axis=1, kind="stable")
    return q, np.take_along_axis(before, q, axis=1)
def reference(x, u, v, wc, ws):
    qu = [mx_ref.quantize(u[r]) for r in range(N)]
    lay = [pk(wc[r], ws[r]) for r in range(N)]
    now = [x[r] for r in range(N)]
    oq = np.zeros((N, 8, C), np.float32)
    for t in range(3):
        kept, blend = [], []
        for r in range(N):
            qx = mx_ref.quantize(now[r])
            q, p = walk(mx_ref.matmul(qu[r], qx))
            own = decode(qx).astype(BF)
            a = gcols(own, q).astype(np.float32)
            kept.append(a)
            blend.append(mx_ref.quantize(((a + gcols(own, p).astype(np.float32)) * np.float32(0.5)).astype(BF)))
            oq[r] = q
        new = []
        for r in range(N):
            m = join(pick(blend[r ^ PARTNER[t]], np.arange(H)), pick(blend[r], np.arange(H, C)))
            new.append(tile([(mx_ref.matmul(pick(lay[r], np.arange(128 * b, 128 * b + 128)), m) * np.float32(0.0009765625) + kept[r][:, b::4]) * np.float32(0.5) for b in range(4)]))
        now = new
    y = np.zeros((N, 128, C), np.float32)
    oc, osc = np.zeros((N, 128, 4 * C), np.uint8), np.zeros((N, 16, C), np.uint8)
    for r in range(N):
        qx = mx_ref.quantize(now[r])
        y[r] = mx_ref.matmul(mx_ref.quantize(v[r]), qx)
        oc[r], osc[r] = emit(qx)
    return {"y": y, "oq": oq, "oc": oc, "osc": osc}

@@ -1,0 +1,553 @@
+import numpy as np
+from concourse.mybir import dt, AluOpType as Op, ActivationFunctionType as AF
+
+F, B, I, U16 = "float32", "bfloat16", "int32", "uint16"
+C8, U8 = "float8_e4m3fn_x4", "uint8"
+
+
+def _sb(t, *s):
+    return ("sbuf", [128] + list(s), t)
+
+
+SCRATCH = {
+    "xin": _sb(B, 64, 20), "xt": _sb(B, 5, 64, 4), "xl": _sb(B, 1280), "ut": _sb(B, 512), "vt": _sb(B, 512),
+    "xq": _sb(C8, 384), "xs": _sb(U8, 384), "uq": _sb(C8, 128), "us": _sb(U8, 128), "vq": _sb(C8, 128), "vs": _sb(U8, 128),
+    "wq": _sb(C8, 512), "wsc": _sb(U8, 512), "lq": _sb(C8, 320), "lsc": _sb(U8, 320),
+    "sc": _sb(F, 32, 5), "cm": _sb(F, 4, 8, 5), "a2": _sb(F, 2, 8, 5), "rk": _sb(F, 40), "pb": _sb(F, 3, 8, 5),
+    "pac": _sb(F, 40), "pad": _sb(F, 40), "pay": _sb(F, 41), "d1": _sb(F, 40), "ne1": _sb(F, 5, 40), "prb": _sb(F, 40, 5),
+    "rt": _sb(B, 26, 5, 4), "rq": _sb(C8, 168), "rs": _sb(U8, 168),
+    "tb": _sb(F, 51), "tbb": _sb(F, 50), "val": _sb(F, 2, 50), "eq": _sb(F, 50), "ab": _sb(F, 150), "dt3": _sb(F, 150), "so": _sb(F, 14, 150),
+    "phii": _sb(I, 14), "cdf": _sb(I, 64), "phi": _sb(F, 14), "cde": _sb(I, 64), "ca": _sb(I, 64), "pt": _sb(B, 512),
+    "ptq": _sb(C8, 192), "pts": _sb(U8, 192), "nei": _sb(F, 5, 64), "pc": _sb(F, 65), "dp": _sb(F, 64), "uop": _sb(F, 5, 64),
+    "fl": _sb(F, 20), "flm": _sb(F, 20), "inc": _sb(F, 20), "pr": _sb(F, 20), "pk": _sb(F, 65),
+    "v2": _sb(F, 40), "vm": _sb(F, 2, 5, 4, 4), "dg": _sb(B, 1024), "dgq": _sb(C8, 336), "dgs": _sb(U8, 336),
+    "ofp": _sb(U16, 20), "ofq": _sb(U16, 20), "row": _sb(F, 400),
+    "tr": _sb(F, 5, 2, 64), "trl": _sb(F, 2, 320), "te": _sb(F, 20), "to": _sb(F, 20), "off": _sb(U16, 20),
+    "tp": _sb(B, 1280), "tw": _sb(B, 1280), "zp": _sb(B, 1280), "zt": _sb(B, 1280), "at": _sb(B, 1280), "tm": _sb(F, 8, 160), "yb": _sb(F, 320),
+    "zz": _sb(B, 512), "iw": _sb(I, 64, 4), "wm01": _sb(B, 64, 4), "wat": _sb(B, 160, 4), "wbt": _sb(B, 160, 4),
+    "waq": _sb(C8, 160), "was": _sb(U8, 160), "wbq": _sb(C8, 160), "wbs": _sb(U8, 160),
+    "et": _sb(B, 516), "ones": _sb(B, 128), "eqc": _sb(C8, 512), "eqs": _sb(U8, 512),
+    "w3": _sb(B, 3, 128, 4),
+    "cq3": _sb(C8, 384), "cs3": _sb(U8, 384),
+    "ik": _sb(I, 64), "nr": _sb(I, 64, 4), "jr": _sb(I, 16, 4),
+    "n40": _sb(I, 40), "nb40": _sb(I, 40), "msk": _sb(F, 4, 40), "ngf": _sb(F, 4), "ngm": _sb(F, 4),
+    "cti": _sb(I, 50), "ct": _sb(F, 50), "val0": _sb(F, 50),
+    "pi": _sb(I, 8), "s0": _sb(F, 2), "me": _sb(F, 2), "mo": _sb(F, 2), "cqo": _sb(F, 2),
+    "ci2": _sb(F, 40), "cqc": _sb(F, 65), "one5": _sb(F, 8), "cf4": _sb(F, 8), "phr": _sb(F, 320), "lgr": _sb(F, 320),
+}
+for _k in ("send", "stay", "land"):
+    SCRATCH[_k + "c"] = _sb(C8, 480)
+    SCRATCH[_k + "p"] = _sb(U8, 480)
+for _t in range(8):
+    SCRATCH["ps%d" % _t] = ("psum", [128, 512], F)
+SEMAPHORES = ["v", "s", "t", "p", "dx", "du", "dw", "dv", "fin"] + ["%s%d" % (a, i) for a in ("arr", "snd") for i in range(3)]
+
+M1 = 12582912.0
+EPS = 2.0 ** -30
+PARTNER = [1, 2, 3]
+
+
+def rank_program(g, core, T, topo):
+    rank = T.rank_of(core)
+    if rank is None:
+        return
+    queue = {"v": g.vector, "s": g.scalar, "t": g.tensor, "p": g, "y": g.sync}
+    count, known, last, reads = {}, {e: {} for e in queue}, {}, {}
+
+    def need(e, sem, val):
+        if known[e].get(sem, 0) < val:
+            queue[e].wait_ge(T.sem[sem], val)
+            known[e][sem] = val
+
+    def pre(e, rd, wr):
+        for k in rd.split():
+            for s, n in last.get(k, {}).items():
+                need(e, s, n)
+        for k in wr.split():
+            for s, n in list(last.get(k, {}).items()) + list(reads.get(k, {}).items()):
+                need(e, s, n)
+
+    def post(sem, n, rd, wr, more=False):
+        count[sem] = count.get(sem, 0) + n
+        for k in rd.split():
+            reads.setdefault(k, {})[sem] = count[sem]
+        for k in wr.split():
+            old = last.get(k, {}) if more else {}
+            last[k] = {**old, sem: count[sem]}
+            if not more:
+                reads[k] = {}
+
+    def do(e, rd, wr, call, sem=None, n=1, more=False):
+        pre(e, rd, "" if more else wr)
+        if e == "p":
+            need("p", "p", count.get("p", 0))
+        if more:
+            for k in wr.split():
+                for s, c in reads.get(k, {}).items():
+                    if s != e:
+                        need(e, s, c)
+        sem = sem or e
+        call().then_inc(T.sem[sem], n)
+        post(sem, n, rd, wr, more)
+
+    V, S, P, Y = g.vector, g.scalar, g, g.sync
+
+    def tt(wr, rd, out, a, b, op, more=False):
+        do("v", rd, wr, lambda: V.tensor_tensor(out, a, b, op), more=more)
+
+    def ts(wr, rd, out, a, s1, op0, s2=None, op1=None, more=False):
+        if op1 is None:
+            do("v", rd, wr, lambda: V.tensor_scalar(out, a, s1, None, op0), more=more)
+        else:
+            do("v", rd, wr, lambda: V.tensor_scalar(out, a, s1, s2, op0, op1), more=more)
+
+    def scan(wr, rd, out, a, b, more=False, initial=0.0):
+        do("v", rd, wr, lambda: V.tensor_tensor_scan(out, a, b, initial, Op.mult, Op.add), more=more)
+
+    def copy(wr, rd, out, a, more=False):
+        do("v", rd, wr, lambda: V.tensor_copy(out, a), more=more)
+
+    def fill(wr, out, c, more=False):
+        do("v", "", wr, lambda: V.memset(out, c), more=more)
+
+    def quant(wr, rd, q, s, t, more=False):
+        do("v", rd, wr, lambda: V.quantize_mx(q, s, t), more=more)
+
+    def act(wr, rd, out, a, scale=None, more=False, bias=None):
+        if bias is not None:
+            do("s", rd, wr, lambda: S.activation(out, a, AF.Identity, bias=bias), more=more)
+        elif scale is None:
+            do("s", rd, wr, lambda: S.activation(out, a, AF.Copy), more=more)
+        else:
+            do("s", rd, wr, lambda: S.activation(out, a, AF.Copy, scale=scale), more=more)
+
+    def iota(wr, out, pat, base, cm, more=False):
+        do("p", "", wr, lambda: P.iota(out, pat, base, cm), more=more)
+
+    def iotaf(wr, out, pat, base, cm):
+        do("p", "", wr, lambda: P.iota(out, pat, base, cm, allow_small_or_imprecise_dtypes=True))
+
+    def mm(wr, rd, *prods):
+        pre("t", rd, wr)
+        for i, p in enumerate(prods):
+            ins = g.tensor.matmul_mx(*p, i == 0, i == len(prods) - 1)
+        ins.then_inc(T.sem.t, 1)
+        post("t", 1, rd, wr)
+
+    do("y", "", "xin", lambda: Y.dma_start(T.xin[:], T.x[:]), "dx", 16)
+    for G in range(8):
+        gg = 7 - G
+        q = ("s", S) if G % 2 else ("y", Y)
+        do(q[0], "", "ut", lambda: q[1].dma_start(T.ut[:, 16 * G:16 * G + 16], T.u[:, 64 * gg:64 * gg + 16]), "du", 16, more=True)
+    do("s", "", "ut", lambda: S.dma_start(T.ut[:, 128:512], T.u[:, 128:512]), "du", 16, more=True)
+    do("s", "", "wq", lambda: S.dma_start(T.wq[:].bitcast(dt.uint8), T.wc[:]), "dw", 16, more=True)
+    do("s", "", "wq", lambda: S.dma_start(T.wsc[:], T.ws[:]), "dw", 16, more=True)
+    do("y", "", "vt", lambda: Y.dma_start(T.vt[:], T.v[:]), "dv", 16)
+
+    lo, up = slice(0, 64), slice(64, 128)
+    iota("iw", T.iw[:], [[-1, 64], [8, 4]], -56, 1)
+    iota("cti", T.cti[:], [[-8, 10], [0, 5]], 72, 1)
+    iota("pi", T.pi[:, 0:4], [[0, 4]], 0, 1)
+    fill("et0", T.et[:], 0.0)
+    fill("ones", T.ones[:], 1.0)
+    do("p", "ones et0", "et", lambda: P.affine_select(T.et[:, 3:515:4], T.ones[:], [[-1, 128]], Op.is_equal, 0.0, 0, 1))
+    iotaf("v0i", T.val0[:], [[-1, 50]], 49, 0)
+    iotaf("ci2", T.ci2[:], [[0, 8], [1, 5]], -2, 0)
+    for h, sl in ((0, lo), (1, up)):
+        iota("n40", T.n40[sl, :], [[0, 10], [8, 4]], 32 * h, 1, more=True)
+        iota("nr", T.nr[sl, :, :], [[1, 64], [8, 4]], 32 * h, 0, more=True)
+        iota("ik", T.ik[sl, :], [[-1, 64]], 0, 1, more=True)
+    iota("jr", T.jr[:], [[1, 16], [-8, 4]], 0, -1)
+    iotaf("phr", T.phr[:], [[1, 320]], 0, 0)
+    iotaf("lgr", T.lgr[:], [[1, 5], [5, 64]], 0, 0)
+
+    fill("zz", T.zz[:], 0.0)
+    quant("xqz", "zz", T.xq[:, 256:384], T.xs[:, 256:384], T.zz[:])
+    act("rt", "zz", T.rt[:, 0:25, :, :], T.zz[:, 0:500])
+    act("rt", "zz", T.rt[:, 25, :, :], T.zz[:, 0:20], more=True)
+    act("pt0", "zz", T.pt[:], T.zz[:])
+    for i in range(5):
+        if i < 3:
+            copy("xt", "xin", T.xt[:, i, :, :], T.xin[:, :, 4 * i:4 * i + 4], more=True)
+        else:
+            act("xt", "xin", T.xt[:, i, :, :], T.xin[:, :, 4 * i:4 * i + 4], more=True)
+    quant("uq", "ut", T.uq[:], T.us[:], T.ut[:])
+    quant("xq", "xt xqz", T.xq[:, 0:320], T.xs[:, 0:320], T.xt[:])
+
+    def constants0():
+        ts("iw2", "iw", T.iw[:], T.iw[:], 63, Op.bitwise_and)
+        fill("wm01", T.wm01[up], 0.0)
+        fill("pay0", T.pay[:, 40:41], 0.0)
+        ts("wm01", "iw2", T.wm01[lo], T.iw[lo], 0, Op.is_equal, more=True)
+        ts("cti2", "cti", T.cti[:], T.cti[:], 63, Op.bitwise_and)
+        ts("pj", "pi", T.pi[:, 4:6], T.pi[:, 0:2], 7, Op.bitwise_and)
+        fill("code0", T.cde[:], 1)
+
+    def constants3():
+        for c, w in ((0, 64), (64, 64), (128, 32)):
+            act("wat", "wm01", T.wat[:, c:c + w, :], T.wm01[:, 0:w, :], 0.625, more=c > 0)
+            act("wbt", "wm01", T.wbt[:, c:c + w, :], T.wm01[:, 0:w, :], -0.125, more=c > 0)
+        for j in range(3):
+            act("w3z", "zz", T.w3[:, j, :, :], T.zz[:], more=j > 0)
+        for j in range(2):
+            act("dg0", "zz", T.dg[:, 512 * j:512 * j + 512], T.zz[:], more=j > 0)
+        act("row0", "zz", T.row[:], T.zz[:, 0:400])
+
+    def constants1():
+        ts("ct", "cti2", T.ct[:], T.cti[:], -1.0 / 512, Op.mult, 64.0625, Op.add)
+        ts("s0", "pj", T.s0[:], T.pi[:, 4:6], 5.0, Op.mult, 64.0, Op.add)
+        ts("n40b", "n40", T.n40[:], T.n40[:], 63, Op.bitwise_and)
+        ts("ngm", "n40b", T.ngm[:], T.n40[:, 0:4], -1.0 / 512, Op.mult, 102560.0 / 512, Op.add)
+        ts("val0", "v0i", T.val0[:], T.val0[:], 64.4375, Op.add)
+        fill("tb0", T.tb[:, 50:51], 0.0)
+        fill("abk", T.ab[:, 0:150:3], 1 / EPS)
+        fill("dt0", T.dt3[:], 0.0)
+
+    def constants2():
+        for b in range(4):
+            quant("e%d" % b, "et", T.eqc[:, 128 * b:128 * b + 128], T.eqs[:, 128 * b:128 * b + 128], T.et[:, 3 - b:515 - b])
+            yield
+        ts("pj2", "pi", T.pi[:, 6:8], T.pi[:, 0:2], 4, Op.logical_shift_right, 1, Op.bitwise_and)
+        yield
+        ts("nb40", "n40b", T.nb40[:], T.n40[:], 4, Op.logical_shift_right)
+        yield
+        ts("nr2", "nr", T.nr[:], T.nr[:], 63, Op.bitwise_and)
+        yield
+        ts("jr2", "jr", T.jr[:], T.jr[:], 15, Op.bitwise_and)
+        yield
+        copy("ngf", "n40b", T.ngf[:], T.n40[:, 0:4])
+        yield
+        fill("cqc1", T.cqc[:], -160.0)
+        yield
+        fill("one5", T.one5[:], 1.0)
+        yield
+        fill("pc0", T.pc[:], 0.0)
+        yield
+        fill("pk0", T.pk[:, 64:65], 0.0)
+        yield
+        fill("cqc1", T.cqc[:, 15:65:16], 0.0)
+        yield
+        fill("cf4", T.cf4[:, 0:4], 1024.0)
+        yield
+        fill("cf4", T.cf4[:, 4:8], 0.0, more=True)
+        yield
+        fill("cqc1", T.cqc[:, 64:65], 0.0)
+        yield
+        for a in (40, 208):
+            quant("dgqz", "zz", T.dgq[:, a:a + 128], T.dgs[:, a:a + 128], T.zz[:], more=True)
+            yield
+        quant("ptqz", "zz", T.ptq[:, 64:192], T.pts[:, 64:192], T.zz[:])
+        yield
+        for h, sl in ((0, lo), (1, up)):
+            do("v", "w3z", "wt0", lambda: V.memset(T.w3[sl, 0, 64 * h:64 * h + 64, 1], 1.0), more=True)
+            yield
+            ts("wt0", "ik w3z", T.w3[sl, 0, 64 * h:64 * h + 64, 0], T.ik[sl, :], 0, Op.is_lt, more=True)
+            yield
+            for t in range(4):
+                ts("wt1", "nr2 ngf w3z", T.w3[sl, 1, 64 * h:64 * h + 64, t], T.nr[sl, :, t], T.ngf[sl, t:t + 1], Op.is_le, more=True)
+                yield
+                m = 64 * h + 16 * t
+                ts("wt2", "jr2 w3z", T.w3[sl, 2, m:m + 16, t], T.jr[sl, :, t], 0, Op.is_equal, more=True)
+                yield
+        ts("cqc", "n40b cqc1", T.cqc[:, 0:64:16], T.n40[:, 0:4], 5.0, Op.mult, -160.0, Op.add)
+        yield
+        for j in range(3):
+            quant("qwt%d" % j, "wt%d" % j, T.cq3[:, 128 * j:128 * j + 128], T.cs3[:, 128 * j:128 * j + 128], T.w3[:, j, :, :])
+            yield
+            yield
+        for nb in range(4):
+            ts("msk", "nb40", T.msk[:, nb, :], T.nb40[:], nb, Op.is_equal, more=True)
+            yield
+        copy("mo", "pj2", T.mo[:], T.pi[:, 6:8])
+        yield
+        ts("me", "pj2", T.me[:], T.pi[:, 6:8], -1.0, Op.mult, 1.0, Op.add)
+        yield
+        ts("cqo", "pj2", T.cqo[:, 0:1], T.pi[:, 6:7], 80.0, Op.mult, 160.0, Op.add)
+        yield
+        ts("cqo", "pj2", T.cqo[:, 1:2], T.pi[:, 6:7], 16.0, Op.mult, 160.0, Op.add, more=True)
+
+    rest = constants2()
+
+    def fillers(n):
+        for _ in range(n):
+            next(rest, None)
+
+    def W3(j):
+        return T.cq3[:, 128 * j:128 * j + 128], T.cs3[:, 128 * j:128 * j + 128]
+
+    ps = [T["ps%d" % i] for i in range(8)]
+    partner_of = lambda t: T.cores[rank ^ PARTNER[t]]
+
+    for t in range(3):
+        final = t == 2
+        for i in range(5):
+            mm("ps%d" % i, "xq uq", (ps[i][:, 0:128], T.xq[:, 64 * i:64 * i + 128], T.xs[:, 64 * i:64 * i + 128], T.uq[:], T.us[:]))
+        if t == 0:
+            constants0()
+        for i in range(5):
+            if i % 2:
+                act("sc", "ps%d" % i, T.sc[:, :, i], ps[i][:, 0:32], more=i > 0)
+            else:
+                copy("sc", "ps%d" % i, T.sc[:, :, i], ps[i][:, 0:32], more=i > 0)
+        def unpack():
+            for b, k in enumerate((5, 6, 7, 0)):
+                mm("ps%d" % k, "xq e%d" % b, (ps[k][:, 0:320], T.eqc[:, 128 * b:128 * b + 128], T.eqs[:, 128 * b:128 * b + 128], T.xq[:, 0:320], T.xs[:, 0:320]))
+                act("tp", "ps%d" % k, T.tp[:, 320 * b:320 * b + 320], ps[k][:, 0:320], 0.5, more=b > 0)
+            act("tw", "tp", T.tw[:], T.tp[:])
+
+        if t == 0:
+            constants3()
+        else:
+            unpack()
+        key = lambda a, b: T.sc[:, 3:32:4, a:b]
+        for s in range(1, 5):
+            tt("cm", "sc", T.cm[:, s - 1, :, 0:5 - s], key(s, 5), key(0, 5 - s), Op.is_gt, more=True)
+            tt("cm", "sc", T.cm[:, s - 1, :, 5 - s:5], key(0, s), key(5 - s, 5), Op.is_ge, more=True)
+        for b in range(3):
+            ts("pb%d" % b, "sc", T.pb[:, b, :, :], T.sc[:, b:32:4, :], 0.0, Op.is_gt, 32.0 / 2 ** b, Op.mult)
+        tt("a2", "cm", T.a2[:], T.cm[:, 0:2, :, :], T.cm[:, 2:4, :, :], Op.add)
+        tt("pac", "pb0 pb1", T.pac[:], T.pb[:, 0, :, :], T.pb[:, 1, :, :], Op.add)
+        tt("pad", "pb2 ci2", T.pad[:], T.pb[:, 2, :, :], T.ci2[:], Op.add)
+        tt("rk", "a2", T.rk[:], T.a2[:, 0, :, :], T.a2[:, 1, :, :], Op.add)
+        tt("pay", "pac pad", T.pay[:, 0:40], T.pac[:], T.pad[:], Op.add)
+        for r in range(3):
+            ts("ne1%d" % r, "rk", T.ne1[:, r, :], T.rk[:], 4.0 - r, Op.not_equal)
+        tt("d1a", "pay pay0", T.d1[:], T.pay[:, 0:40], T.pay[:, 1:41], Op.subtract)
+        for r in range(3, 5):
+            ts("ne1%d" % r, "rk", T.ne1[:, r, :], T.rk[:], 4.0 - r, Op.not_equal)
+        if t == 0:
+            quant("rqz", "zz", T.rq[:, 40:168], T.rs[:, 40:168], T.zz[:])
+        copy("d1", "pay d1a", T.d1[:, 4:40:5], T.pay[:, 4:40:5])
+        for r in range(5):
+            scan("prb", "ne1%d d1" % r, T.prb[:, :, r], T.ne1[:, r, :], T.d1[:], more=True)
+        if t == 0:
+            quant("wa", "wat", T.waq[:], T.was[:], T.wat[:])
+            quant("wb", "wbt", T.wbq[:], T.wbs[:], T.wbt[:])
+        for e in range(4):
+            ts("rth%d" % e, "prb rt", T.rt[:, e:8:4, :, e], T.prb[:, 4 + 5 * e:40:20, :], M1 * 8, Op.add, M1 * 8, Op.subtract)
+        for e in range(4):
+            tt("rtl%d" % e, "prb rth%d" % e, T.rt[:, 8 + e:16:4, :, e], T.prb[:, 4 + 5 * e:40:20, :], T.rt[:, e:8:4, :, e], Op.subtract)
+        quant("rq", "rqz rth0 rth1 rth2 rth3 rtl0 rtl1 rtl2 rtl3", T.rq[:, 0:130], T.rs[:, 0:130], T.rt[:])
+        for k, w in ((1, 0), (2, 32)):
+            mm("ps%d" % k, "wa wb rq rqz",
+               (ps[k][:, 0:128], T.waq[:, w:w + 128], T.was[:, w:w + 128], T.rq[:, 0:128], T.rs[:, 0:128]),
+               (ps[k][:, 0:128], T.wbq[:, w:w + 128], T.wbs[:, w:w + 128], T.rq[:, 40:168], T.rs[:, 40:168]))
+        fill("abb", T.ab[:, 2:150:3], EPS)
+        if t == 0:
+            constants1()
+        tt("tb1", "ps1 ct", T.tb[:, 10:30], ps[1][:, 0:20], T.ct[:, 10:30], Op.add)
+        tt("tb2", "ps2 ct", T.tb[:, 30:50], ps[2][:, 20:40], T.ct[:, 30:50], Op.add)
+        tt("tb3", "ps2 ct", T.tb[:, 0:10], ps[2][:, 30:40], T.ct[:, 0:10], Op.add)
+        ts("aba", "val0 s0 abk", T.ab[:, 1:150:3], T.val0[:], T.s0[:, 0:1], Op.is_lt, EPS, Op.add)
+        tt("dtb", "tb1 tb2 tb3 tb0 dt0", T.dt3[:, 2:150:3], T.tb[:, 0:50], T.tb[:, 1:51], Op.subtract)
+        tt("tbm", "val0 tb1 tb2 tb3", T.tbb[:], T.val0[:], T.tb[:, 0:50], Op.is_ge)
+        scan("so0", "aba abb dtb", T.so[:, 0, :], T.ab[:], T.dt3[:])
+        tt("tbb", "tbm", T.tbb[:], T.tbb[:], T.tb[:, 0:50], Op.mult)
+        def cd(n):
+            ts("cd%d" % n, "so%d ngm code0" % n, T.cde[:, n + 1:64:16], T.ngm[:], T.so[:, n, 149:150], Op.subtract, 512.0, Op.mult)
+
+        def ca(n):
+            ts("ca%d" % n, "cd%d" % n, T.ca[:, n + 1:64:16], T.cde[:, n + 1:64:16], 63, Op.bitwise_and)
+
+        def po(n):
+            ts("po%d" % n, "ca%d pt0" % n, T.pt[:, 4 * n + 4:256:64], T.ca[:, n + 1:64:16], 0, Op.is_equal)
+
+        def pe(n):
+            tt("pe%d" % n, "po%d pe%d pt0" % (n - 1, n - 1), T.pt[:, 4 * n + 5:256:64], T.pt[:, 4 * n + 1:256:64], T.pt[:, 4 * n:256:64], Op.add)
+
+        for n in range(1, 14):
+            s, so = T.so[:, n - 1, 149:150], "so%d" % (n - 1)
+            vk, vv = ("val0", T.val0[:]) if n == 1 else ("vl%d" % ((n - 1) % 2), T.val[:, (n - 1) % 2, :])
+            if n < 13:
+                ts("eq", so, T.eq[:], T.tb[:, 0:50], s, Op.is_equal, 64.0, Op.mult)
+            ts("aba", vk + " " + so, T.ab[:, 1:150:3], vv, s, Op.is_lt, EPS, Op.add)
+            ts("abb", "tbb " + so, T.ab[:, 2:150:3], T.tbb[:], s, Op.is_equal, EPS, Op.add)
+            cd(n - 1)
+            if n < 13:
+                tt("vl%d" % (n % 2), vk + " eq", T.val[:, n % 2, :], vv, T.eq[:], Op.subtract)
+            else:
+                fillers(2)
+            scan("so%d" % n, "aba abb dtb", T.so[:, n, :], T.ab[:], T.dt3[:])
+            if n >= 2:
+                po(n - 2)
+            if n >= 3:
+                pe(n - 2)
+            ca(n - 1)
+            fillers(4)
+            if t == 0 and n == 5:
+                unpack()
+        fillers(99)
+        cd(13)
+        ts("phii", "so0 so13", T.phii[:], T.so[:, :, 149], -512.0, Op.mult, 102560.0, Op.add)
+        po(12)
+        pe(12)
+        ca(13)
+        ts("phij", "phii", T.phii[:], T.phii[:], 511, Op.bitwise_and)
+        pe(13)
+        po(13)
+        ts("cdf", " ".join("cd%d" % n for n in range(14)), T.cdf[:], T.cde[:], 511, Op.bitwise_and)
+        ts("phi", "phij", T.phi[:], T.phii[:], -160.0, Op.add)
+        for e in range(4):
+            act("pc", "phi pc0", T.pc[:, 16 * e + 2:16 * e + 15], T.phi[:, 0:13], more=e > 0)
+        act("pc", "phi cf4", T.pc[:, 0:64:16], T.cf4[:, 0:4], bias=T.phi[:, 13:14], more=True)
+        act("pc", "phi cf4", T.pc[:, 1:64:16], T.cf4[:, 4:8], bias=T.phi[:, 13:14], more=True)
+        tt("ptu", "pe13 po13 pt0", T.pt[:, 256:452:65], T.pt[:, 57:256:64], T.pt[:, 56:256:64], Op.add)
+        for i in range(3):
+            ts("nea", "cdf", T.nei[:, i, :], T.cdf[:], 64.0 * i, Op.not_equal, more=i > 0)
+        quant("ptq", "ptu ptqz " + " ".join("po%d" % n for n in range(14)) + " " + " ".join("pe%d" % n for n in range(1, 14)), T.ptq[:, 0:128], T.pts[:, 0:128], T.pt[:])
+        mm("ps3", "ptq ptqz qwt0 qwt1", (ps[3][:, 0:128], *W3(0), T.ptq[:, 0:128], T.pts[:, 0:128]),
+           (ps[3][:, 0:128], *W3(1), T.ptq[:, 64:192], T.pts[:, 64:192]))
+        for i in range(3, 5):
+            ts("nea", "cdf", T.nei[:, i, :], T.cdf[:], 64.0 * i, Op.not_equal, more=True)
+        do("v", "nea", "nei", lambda: V.memset(T.nei[:, :, 0:64:16], 0.0))
+        tt("dp", "pc pc0", T.dp[:], T.pc[:, 0:64], T.pc[:, 1:65], Op.subtract)
+        for i in range(5):
+            scan("uop", "nei dp", T.uop[:, i, :], T.nei[:, i, :], T.dp[:], more=True)
+        up5 = T.uop[:, :, 14:64:16]
+
+        def spread(x):
+            j = int(x == "q")
+            for nb in range(4):
+                tt("vm" + x, "v2%s msk" % x, T.vm[:, j, :, nb, :], T.v2[:, 20 * j:20 * j + 20], T.msk[:, nb, 0:20], Op.mult, more=nb > 0)
+
+        def digit(x, j):
+            c, m = 512 * int(x == "q"), T.vm[:, int(x == "q"), :, :, :]
+            if j:
+                ts("dh" + x, "vm%s dg0" % x, T.dg[:, c + 80:c + 160], m, M1 * 32, Op.add, M1 * 32, Op.subtract)
+            else:
+                tt("dl" + x, "vm%s dh%s" % (x, x), T.dg[:, c:c + 80], m, T.dg[:, c + 80:c + 160], Op.subtract)
+
+        def form(x, k):
+            c = 168 * (x == "q")
+            quant("dg" + x, "dh%s dl%s dgqz" % (x, x), T.dgq[:, c:c + 128], T.dgs[:, c:c + 128], T.dg[:, 512 * (x == "q"):512 * (x == "q") + 512])
+            mm("ps%d" % k, "dg%s dgqz qwt2" % x, (ps[k][:, 0:128], *W3(2), T.dgq[:, c:c + 128], T.dgs[:, c:c + 128]),
+               (ps[k][:, 0:128], *W3(2), T.dgq[:, c + 20:c + 148], T.dgs[:, c + 20:c + 148]))
+
+        def blend(b):
+            cs = slice(320 * b, 320 * b + 320)
+            tt("zp%d" % b, "tp tw ofp", T.zp[:, cs], T.tw[:, cs].indirect(T.ofp[:, 0:20]), T.tp[:, cs], Op.add)
+
+        tt("pk", "ps3 cqc", T.pk[:, 0:64], ps[3][:, 0:64], T.cqc[:, 0:64], Op.add)
+        ts("fl", "uop", T.fl[:], up5, 512.0, Op.is_ge)
+        ts("flm", "uop", T.flm[:], up5, 512.0, Op.is_ge, -1024.0, Op.mult)
+        tt("dp", "pk pk0", T.dp[:], T.pk[:, 0:64], T.pk[:, 1:65], Op.subtract)
+        tt("v2p", "uop flm", T.v2[:, 0:20], up5, T.flm[:], Op.add)
+        for e in range(4):
+            scan("inc", "fl one5", T.inc[:, e:20:4], T.one5[:, 0:5], T.fl[:, e:20:4], more=True, initial=-1.0)
+        for i in range(5):
+            scan("uop", "nei dp", T.uop[:, i, :], T.nei[:, i, :], T.dp[:], more=i > 0)
+        tt("pr", "fl inc", T.pr[:], T.fl[:], T.inc[:], Op.mult)
+        spread("p")
+        tt("v2q", "uop pr", T.v2[:, 20:40], up5, T.pr[:], Op.add)
+        digit("p", 1)
+        spread("q")
+        digit("p", 0)
+        digit("q", 1)
+        form("p", 5)
+        digit("q", 0)
+        form("q", 4)
+        ts("ofp", "ps5", T.ofp[:], ps[5][:, 0:20], 160.0, Op.add)
+        blend(0)
+        ci = 1 if final else 0
+        ts("ofq", "ps4 cqo", T.ofq[:], ps[4][:, 0:20], T.cqo[:, ci:ci + 1], Op.add)
+        do("v", "ofq phr row0", "row", lambda: V.tensor_copy(T.row[:].indirect(T.ofq[:, 0:20]), T.phr[:]))
+        blend(1)
+        if final:
+            for a in range(2):
+                do("v", "row", "tr", lambda: V.transpose(T.trl[:, a, :], T.row[:, 16 * a:16 * a + 320]), more=a > 0)
+            blend(2)
+            for a in range(2):
+                ts("te%d" % a, "tr me", T.te[:, a:20:2], T.trl[:, a, 0:320:32], T.me[:, 0:1], Op.mult)
+                ts("to%d" % a, "tr mo", T.to[:, a:20:2], T.trl[:, a, 16:320:32], T.mo[:, 0:1], Op.mult)
+        else:
+            for i in range(5):
+                for a in range(2):
+                    c = i + 80 * a
+                    do("v", "row", "tr", lambda: V.transpose(T.tr[:, i, a, :], T.row[:, c:c + 316:5]), more=i + a > 0)
+            blend(2)
+            for h in range(2):
+                sl = slice(10 * h, 10 * h + 10)
+                ts("te%d" % h, "tr me", T.te[:, sl], T.tr[:, :, :, 32 * h], T.me[:, 0:1], Op.mult)
+                ts("to%d" % h, "tr mo", T.to[:, sl], T.tr[:, :, :, 32 * h + 16], T.mo[:, 0:1], Op.mult)
+        blend(3)
+        tt("ql", "te0 te1 to0 to1", T.to[:], T.te[:], T.to[:], Op.add)
+        copy("off0", "ql", T.off[:], T.to[:])
+
+        def picks(h):
+            o, cs = T.off[:, 10 * h:10 * h + 10], slice(640 * h, 640 * h + 640)
+            for b in range(2):
+                do("v", "off0 zp%d" % b, "zt%d" % h, lambda: V.tensor_copy(T.zt[:, 640 * h + b:640 * h + 640:4], T.zp[:, 320 * b:320 * b + 320].indirect(o)), more=b > 0)
+            for b in range(2, 4):
+                act("zt%d" % h, "off0 zp%d" % b, T.zt[:, 640 * h + b:640 * h + 640:4], T.zp[:, 320 * b:320 * b + 320].indirect(o), more=True)
+            return cs
+
+        def kept(h, b, e):
+            o = T.off[:, 10 * h:10 * h + 10]
+            out, win = T.at[:, 640 * h + b:640 * h + 640:4], T.tp[:, 320 * b:320 * b + 320].indirect(o)
+            if e == "v":
+                ts("at%d%d" % (h, b), "off0 tp", out, win, 2048.0, Op.mult)
+            else:
+                act("at%d%d" % (h, b), "off0 tp", out, win, 2048.0)
+
+        def new(h, b, k, cod):
+            mm("ps%d" % k, "wq " + cod[0], (ps[k][:, 0:160], T.wq[:, 128 * b:128 * b + 128], T.wsc[:, 128 * b:128 * b + 128], cod[1], cod[2]))
+
+        def finish(h, b, k):
+            tt("tm%d%d" % (h, b), "ps%d at%d%d" % (k, h, b), T.tm[:, 4 * h + b, :], ps[k][:, 0:160], T.at[:, 640 * h + b:640 * h + 640:4], Op.add)
+            if final:
+                act("xl%d" % h, "tm%d%d" % (h, b), T.xl[:, 640 * h + b:640 * h + 640:4], T.tm[:, 4 * h + b, :], 2.0 ** -11, more=b > 0)
+            else:
+                act("xt", "tm%d%d" % (h, b), T.xt[:, :, 32 * h:32 * h + 32, b], T.tm[:, 4 * h + b, :], 2.0 ** -11, more=h == 0 or b > 0)
+
+        rc = slice(160 * t, 160 * t + 160)
+        cs = picks(0)
+        quant("sq%d" % t, "zt0", T.sendc[:, rc], T.sendp[:, rc], T.zt[:, cs])
+        dst = partner_of(t)
+        rid, pid, _ = topo.addr(dst)
+        pre("p", "sq%d" % t, "")
+        for a, b in ((T.landc[:, rc].bitcast(dt.uint8), T.sendc[:, rc].bitcast(dt.uint8)), (T.landp[:, rc], T.sendp[:, rc])):
+            g.remote_dma(a, b, T.sem["arr%d" % t], T.sem["snd%d" % t], pid, rid, topo.mask(core, dst))
+        eng = 2 * len(topo.engines(core, dst))
+        last["land%d" % t] = {"arr%d" % t: eng}
+        cs = picks(1)
+        quant("stay%d" % t, "zt1", T.stayc[:, rc], T.stayp[:, rc], T.zt[:, cs])
+        for b in range(4):
+            new(1, b, 4 + b, ("stay%d" % t, T.stayc[:, rc], T.stayp[:, rc]))
+        for h in (1, 0):
+            for b in range(4):
+                kept(h, b, "v" if b < 2 else "s")
+            if h:
+                for b in range(4):
+                    finish(1, b, 4 + b)
+        if t == 0:
+            quant("vq", "vt", T.vq[:], T.vs[:], T.vt[:])
+        if final:
+            quant("lq1", "xl1", T.lq[:, 160:320], T.lsc[:, 160:320], T.xl[:, 640:1280])
+            do("v", "ofq lgr row0", "row", lambda: V.tensor_copy(T.row[:].indirect(T.ofq[:, 0:20]), T.lgr[:]))
+            mm("ps4", "lq1 vq", (ps[4][:, 0:160], T.vq[:], T.vs[:], T.lq[:, 160:320], T.lsc[:, 160:320]))
+            do("y", "row", "", lambda: Y.dma_start(T.oq[0:8:2, :], T.row[0:128:32, 0:320]), "fin", 16)
+            do("y", "row", "", lambda: Y.dma_start(T.oq[1:8:2, :], T.row[16:128:32, 16:336]), "fin", 16)
+            do("y", "lq1", "", lambda: Y.dma_start(T.oc[:, 640:1280], T.lq[:, 160:320].bitcast(dt.uint8)), "fin", 16)
+            copy("yb1", "ps4", T.yb[:, 160:320], ps[4][:, 0:160])
+            do("y", "yb1", "", lambda: Y.dma_start(T.y[:, 160:320], T.yb[:, 160:320]), "fin", 16)
+        for b in range(4):
+            new(0, b, b, ("land%d" % t, T.landc[:, rc], T.landp[:, rc]))
+        for b in range(4):
+            finish(0, b, b)
+        need("p", "snd%d" % t, eng)
+        if not final:
+            quant("xq", "xt xqz", T.xq[:, 0:320], T.xs[:, 0:320], T.xt[:])
+
+    quant("lq0", "xl0", T.lq[:, 0:160], T.lsc[:, 0:160], T.xl[:, 0:640])
+    mm("ps5", "lq0 vq", (ps[5][:, 0:160], T.vq[:], T.vs[:], T.lq[:, 0:160], T.lsc[:, 0:160]))
+    do("y", "lq0", "", lambda: Y.dma_start(T.oc[:, 0:640], T.lq[:, 0:160].bitcast(dt.uint8)), "fin", 16)
+    for k in range(4):
+        q = ("s", S) if k % 2 else ("y", Y)
+        do(q[0], "lq0 lq1", "", lambda: q[1].dma_start(T.osc[4 * k:4 * k + 4, :], T.lsc[32 * k:32 * k + 4, :]), "fin", 16)
+    copy("yb0", "ps5", T.yb[:, 0:160], ps[5][:, 0:160])
+    do("y", "yb0", "", lambda: Y.dma_start(T.y[:, 0:160], T.yb[:, 0:160]), "fin", 16)
+    need("y", "fin", count["fin"])
+    for k in ("v", "s", "t", "p"):
+        need("y", k, count[k])
+    for k in ("dx", "du", "dw", "dv"):
+        need("y", k, count[k])

@@ -13,29 +13,28 @@ SCRATCH = {
     "xin": _sb(B, 64, 20), "xt": _sb(B, 5, 64, 4), "xl": _sb(B, 1280), "ut": _sb(B, 512), "vt": _sb(B, 512),
     "xq": _sb(C8, 384), "xs": _sb(U8, 384), "uq": _sb(C8, 128), "us": _sb(U8, 128), "vq": _sb(C8, 128), "vs": _sb(U8, 128),
     "wq": _sb(C8, 512), "wsc": _sb(U8, 512), "lq": _sb(C8, 320), "lsc": _sb(U8, 320),
-    "sc": _sb(F, 32, 5), "cm": _sb(F, 4, 8, 5), "a2": _sb(F, 2, 8, 5), "rk": _sb(F, 40), "pb": _sb(F, 3, 8, 5),
-    "pac": _sb(F, 40), "pad": _sb(F, 40), "pay": _sb(F, 41), "d1": _sb(F, 40), "ne1": _sb(F, 5, 40), "prb": _sb(F, 40, 5),
-    "rt": _sb(B, 26, 5, 4), "rq": _sb(C8, 168), "rs": _sb(U8, 168),
-    "tb": _sb(F, 51), "tbb": _sb(F, 50), "val": _sb(F, 2, 50), "eq": _sb(F, 50), "ab": _sb(F, 150), "dt3": _sb(F, 150), "so": _sb(F, 14, 150),
-    "phii": _sb(I, 14), "cdf": _sb(I, 64), "phi": _sb(F, 14), "cde": _sb(I, 64), "ca": _sb(I, 64), "pt": _sb(B, 512),
-    "ptq": _sb(C8, 192), "pts": _sb(U8, 192), "nei": _sb(F, 5, 64), "pc": _sb(F, 65), "dp": _sb(F, 64), "uop": _sb(F, 5, 64),
-    "fl": _sb(F, 20), "flm": _sb(F, 20), "inc": _sb(F, 20), "pr": _sb(F, 20), "pk": _sb(F, 65),
-    "v2": _sb(F, 40), "vm": _sb(F, 2, 5, 4, 4), "dg": _sb(B, 1024), "dgq": _sb(C8, 336), "dgs": _sb(U8, 336),
-    "ofp": _sb(U16, 20), "ofq": _sb(U16, 20), "row": _sb(F, 400),
-    "tr": _sb(F, 5, 2, 64), "trl": _sb(F, 2, 320), "te": _sb(F, 20), "to": _sb(F, 20), "off": _sb(U16, 20),
-    "tp": _sb(B, 1280), "tw": _sb(B, 1280), "zp": _sb(B, 1280), "zt": _sb(B, 1280), "at": _sb(B, 1280), "tm": _sb(F, 8, 160), "yb": _sb(F, 320),
-    "zz": _sb(B, 512), "iw": _sb(I, 64, 4), "wm01": _sb(B, 64, 4), "wat": _sb(B, 160, 4), "wbt": _sb(B, 160, 4),
-    "waq": _sb(C8, 160), "was": _sb(U8, 160), "wbq": _sb(C8, 160), "wbs": _sb(U8, 160),
+    "sc": _sb(F, 8, 5, 4), "cm": _sb(B, 4, 8, 5), "a2": _sb(B, 2, 40), "hb": _sb(B, 160), "rk": _sb(B, 40), "pay": _sb(B, 160),
+    "eqr": _sb(B, 5, 40), "prb": _sb(F, 40, 5), "rt": _sb(B, 4, 8, 21), "rq": _sb(C8, 234), "rs": _sb(U8, 234),
+    "rt2": _sb(B, 6, 88), "rq2": _sb(C8, 150), "rs2": _sb(U8, 150),
+    "tb": _sb(F, 56), "tbb": _sb(F, 50), "val": _sb(F, 2, 50), "sq": _sb(F, 2, 50), "ab": _sb(F, 150), "dt3": _sb(F, 150),
+    "so": _sb(F, 14, 150), "tbp": _sb(F, 20), "sqp": _sb(F, 2, 20), "und": _sb(F, 2, 20), "tt4": _sb(F, 2, 4),
+    "cde": _sb(I, 64), "ca": _sb(I, 64), "c13": _sb(I, 4), "pe": _sb(F, 64), "pt": _sb(B, 512),
+    "ptq": _sb(C8, 192), "pts": _sb(U8, 192), "ne": _sb(F, 5, 64), "dp": _sb(F, 64), "uop": _sb(F, 2, 5, 64),
+    "inc": _sb(F, 20), "pr": _sb(F, 20), "v2": _sb(I, 2, 20), "dgi": _sb(I, 5, 20), "dg": _sb(B, 2, 32, 4, 4),
+    "dgq": _sb(C8, 336), "dgs": _sb(U8, 336), "ofp": _sb(U16, 20), "ofq": _sb(U16, 20), "pk": _sb(F, 320), "row": _sb(F, 320),
+    "s5": _sb(F, 5, 64), "xi": _sb(I, 5, 4), "xj": _sb(I, 20), "offa": _sb(U16, 20), "offb": _sb(U16, 20),
+    "tp": _sb(B, 1280), "zt": _sb(B, 1280), "at": _sb(B, 1280), "ak": _sb(B, 1280), "tm": _sb(F, 8, 160),
+    "zz": _sb(B, 512), "zf": _sb(F, 4), "wm": _sb(B, 64, 4), "wat": _sb(B, 160, 4), "wbt": _sb(B, 160, 4), "wct": _sb(B, 192, 4),
+    "waq": _sb(C8, 160), "was": _sb(U8, 160), "wbq": _sb(C8, 160), "wbs": _sb(U8, 160), "wcq": _sb(C8, 192), "wcs": _sb(U8, 192),
     "et": _sb(B, 516), "ones": _sb(B, 128), "eqc": _sb(C8, 512), "eqs": _sb(U8, 512),
-    "w3": _sb(B, 3, 128, 4),
-    "cq3": _sb(C8, 384), "cs3": _sb(U8, 384),
-    "ik": _sb(I, 64), "nr": _sb(I, 64, 4), "jr": _sb(I, 16, 4),
-    "n40": _sb(I, 40), "nb40": _sb(I, 40), "msk": _sb(F, 4, 40), "ngf": _sb(F, 4), "ngm": _sb(F, 4),
-    "cti": _sb(I, 50), "ct": _sb(F, 50), "val0": _sb(F, 50),
-    "pi": _sb(I, 8), "s0": _sb(F, 2), "me": _sb(F, 2), "mo": _sb(F, 2), "cqo": _sb(F, 2),
-    "ci2": _sb(F, 40), "cqc": _sb(F, 65), "one5": _sb(F, 8), "cf4": _sb(F, 8), "phr": _sb(F, 320), "lgr": _sb(F, 320),
+    "w3": _sb(B, 3, 128, 4), "cq3": _sb(C8, 384), "cs3": _sb(U8, 384),
+    "nr": _sb(I, 64, 4), "jr": _sb(I, 16, 4), "n60": _sb(I, 60), "nb60": _sb(I, 60), "msk": _sb(F, 4, 60), "ngf": _sb(F, 4),
+    "i20": _sb(I, 20), "ctp": _sb(F, 20), "ngm": _sb(F, 4), "n5": _sb(F, 4),
+    "cti": _sb(I, 50), "ct": _sb(F, 50), "val1": _sb(F, 50), "pi": _sb(I, 4), "pf": _sb(F, 8), "c0": _sb(F, 2, 10), "ci": _sb(F, 40),
+    "pa2": _sb(B, 160), "pa16": _sb(F, 64), "d16i": _sb(I, 64), "d16": _sb(F, 2, 64),
+    "phr": _sb(F, 320), "ph512": _sb(F, 320), "lgr": _sb(F, 320),
 }
-for _k in ("send", "stay", "land"):
+for _k in ("send", "land"):
     SCRATCH[_k + "c"] = _sb(C8, 480)
     SCRATCH[_k + "p"] = _sb(U8, 480)
 for _t in range(8):
@@ -43,7 +42,9 @@ for _t in range(8):
 SEMAPHORES = ["v", "s", "t", "p", "dx", "du", "dw", "dv", "fin"] + ["%s%d" % (a, i) for a in ("arr", "snd") for i in range(3)]
 
 M1 = 12582912.0
-EPS = 2.0 ** -30
+EPS = 2.0 ** -40
+U = 2.0 ** 26
+LOW = 2.0 ** 18
 PARTNER = [1, 2, 3]
 
 
@@ -101,8 +102,10 @@ def rank_program(g, core, T, topo):
         else:
             do("v", rd, wr, lambda: V.tensor_scalar(out, a, s1, s2, op0, op1), more=more)
 
-    def scan(wr, rd, out, a, b, more=False, initial=0.0):
-        do("v", rd, wr, lambda: V.tensor_tensor_scan(out, a, b, initial, Op.mult, Op.add), more=more)
+    def scan(wr, rd, out, a, b, more=False, ops=(Op.mult, Op.add), initial=0.0):
+        do("v", rd, wr, lambda: V.tensor_tensor_scan(out, a, b, initial, ops[0], ops[1]), more=more)
+
+    LATCH = (Op.add, Op.min)
 
     def copy(wr, rd, out, a, more=False):
         do("v", rd, wr, lambda: V.tensor_copy(out, a), more=more)
@@ -113,19 +116,20 @@ def rank_program(g, core, T, topo):
     def quant(wr, rd, q, s, t, more=False):
         do("v", rd, wr, lambda: V.quantize_mx(q, s, t), more=more)
 
-    def act(wr, rd, out, a, scale=None, more=False, bias=None):
+    def act(wr, rd, out, a, scale=1.0, more=False, bias=None, func=None):
         if bias is not None:
-            do("s", rd, wr, lambda: S.activation(out, a, AF.Identity, bias=bias), more=more)
-        elif scale is None:
-            do("s", rd, wr, lambda: S.activation(out, a, AF.Copy), more=more)
+            do("s", rd, wr, lambda: S.activation(out, a, func or AF.Identity, bias=bias, scale=scale), more=more)
         else:
-            do("s", rd, wr, lambda: S.activation(out, a, AF.Copy, scale=scale), more=more)
+            do("s", rd, wr, lambda: S.activation(out, a, func or AF.Copy, scale=scale), more=more)
 
     def iota(wr, out, pat, base, cm, more=False):
         do("p", "", wr, lambda: P.iota(out, pat, base, cm), more=more)
 
     def iotaf(wr, out, pat, base, cm):
         do("p", "", wr, lambda: P.iota(out, pat, base, cm, allow_small_or_imprecise_dtypes=True))
+
+    def select(wr, rd, out, a, pat, op, c, base, cm, more=False):
+        do("p", rd, wr, lambda: P.affine_select(out, a, pat, op, c, base, cm), more=more)
 
     def mm(wr, rd, *prods):
         pre("t", rd, wr)
@@ -145,27 +149,63 @@ def rank_program(g, core, T, topo):
     do("y", "", "vt", lambda: Y.dma_start(T.vt[:], T.v[:]), "dv", 16)
 
     lo, up = slice(0, 64), slice(64, 128)
-    iota("iw", T.iw[:], [[-1, 64], [8, 4]], -56, 1)
-    iota("cti", T.cti[:], [[-8, 10], [0, 5]], 72, 1)
-    iota("pi", T.pi[:, 0:4], [[0, 4]], 0, 1)
-    fill("et0", T.et[:], 0.0)
-    fill("ones", T.ones[:], 1.0)
-    do("p", "ones et0", "et", lambda: P.affine_select(T.et[:, 3:515:4], T.ones[:], [[-1, 128]], Op.is_equal, 0.0, 0, 1))
-    iotaf("v0i", T.val0[:], [[-1, 50]], 49, 0)
-    iotaf("ci2", T.ci2[:], [[0, 8], [1, 5]], -2, 0)
-    for h, sl in ((0, lo), (1, up)):
-        iota("n40", T.n40[sl, :], [[0, 10], [8, 4]], 32 * h, 1, more=True)
-        iota("nr", T.nr[sl, :, :], [[1, 64], [8, 4]], 32 * h, 0, more=True)
-        iota("ik", T.ik[sl, :], [[-1, 64]], 0, 1, more=True)
-    iota("jr", T.jr[:], [[1, 16], [-8, 4]], 0, -1)
-    iotaf("phr", T.phr[:], [[1, 320]], 0, 0)
-    iotaf("lgr", T.lgr[:], [[1, 5], [5, 64]], 0, 0)
-
+    halves = ((0, lo), (1, up))
     fill("zz", T.zz[:], 0.0)
+    fill("ones", T.ones[:], 1.0)
+    fill("et0", T.et[:], 0.0)
+    fill("wm0", T.wm[up], 0.0)
+    iota("pi", T.pi[:], [[0, 4]], 0, 1)
+    iota("cti", T.cti[:], [[-8, 10], [0, 5]], 72, 1)
+    iotaf("v0i", T.val1[:], [[-1, 50]], 49, 0)
+    iotaf("cii", T.ci[:], [[0, 8], [1, 5]], 0, 0)
+    select("wm1", "zz", T.wm[lo], T.zz[lo, 0:256], [[-1, 64], [8, 4]], Op.not_equal, 1.0, -56, 1)
+    select("wm", "wm1", T.wm[lo], T.wm[lo], [[-1, 64], [8, 4]], Op.not_equal, 1.0, 8, 1)
+    iotaf("c0i", T.c0[:, 0, :], [[1, 10]], -7, 0)
+    for h, sl in halves:
+        iota("n60", T.n60[sl, :], [[0, 15], [-8, 4]], 120 - 32 * h, 1, more=True)
+    iota("i20", T.i20[:], [[64, 5], [0, 4]], 0, 0)
+    select("et", "ones et0", T.et[:, 3:515:4], T.ones[:], [[-1, 128]], Op.is_equal, 0.0, 0, 1)
+    for h, sl in halves:
+        iota("nr", T.nr[sl], [[1, 64], [-8, 4]], 120 - 32 * h, 0, more=True)
+    iota("jr", T.jr[:], [[1, 16], [-8, 4]], 8, -1)
+    iota("d16i", T.d16i[:], [[1, 64]], 128, -1)
+
     quant("xqz", "zz", T.xq[:, 256:384], T.xs[:, 256:384], T.zz[:])
-    act("rt", "zz", T.rt[:, 0:25, :, :], T.zz[:, 0:500])
-    act("rt", "zz", T.rt[:, 25, :, :], T.zz[:, 0:20], more=True)
+    quant("rqz", "zz", T.rq[:, 106:234], T.rs[:, 106:234], T.zz[:])
+    quant("rq2z", "zz", T.rq2[:, 22:150], T.rs2[:, 22:150], T.zz[:])
+    for j in range(2):
+        act("rt0", "zz", T.rt[:, 2 * j:2 * j + 2, :, :], T.zz[:, 0:336], more=j > 0)
+        act("rt20", "zz", T.rt2[:, 3 * j:3 * j + 3, :], T.zz[:, 0:264], more=j > 0)
     act("pt0", "zz", T.pt[:], T.zz[:])
+    for j in range(3):
+        act("w3z", "zz", T.w3[:, j, :, :], T.zz[:], more=j > 0)
+    for h, sl in halves:
+        cs = slice(64 * h, 64 * h + 64)
+        select("wt0", "ones w3z", T.w3[sl, 0, cs, 0], T.ones[sl, 0:64], [[1, 64]], Op.is_gt, 0.0, 0, -1, more=True)
+        select("wt0", "ones w3z", T.w3[sl, 0, cs, 1], T.ones[sl, 0:64], [[-1, 64]], Op.is_ge, 0.0, 0, 1, more=True)
+    iotaf("phr", T.phr[:], [[1, 320]], 0, 0)
+    iotaf("ph512", T.ph512[:], [[512, 320]], 0, 0)
+    iotaf("lgr", T.lgr[:], [[1, 5], [5, 64]], 0, 0)
+    fill("pa2", T.pa2[:], 2.0)
+    fill("zf", T.zf[:], 0.0)
+    fill("tb0", T.tb[:, 50:54], 0.0)
+    fill("tb0", T.tb[:, 54:56], 1024 * U, more=True)
+    fill("pa2", T.pa2[:, 0:160:4], 0.0)
+    fill("abk", T.ab[:, 0:150:3], 1 / EPS)
+    fill("dt0", T.dt3[:], 0.0)
+    fill("dp0", T.dp[:], 0.0)
+    fill("cd0_", T.cde[:], 1)
+    ts("hb0", "cii", T.hb[:, 0:160:4], T.ci[:], -0.4375, Op.add)
+    ts("pj", "pi", T.pi[:, 0:2], T.pi[:, 0:2], 7, Op.bitwise_and)
+    ts("cti2", "cti", T.cti[:], T.cti[:], 63, Op.bitwise_and)
+    ts("g0", "pj", T.pf[:, 0:2], T.pi[:, 0:2], 5.0, Op.mult)
+    ts("g1", "pj", T.pf[:, 2:4], T.pi[:, 0:2], -1.0, Op.mult)
+    ts("ct", "cti2", T.ct[:], T.cti[:], -U / 512, Op.mult, 81.8125 * U, Op.add)
+    ts("v0m", "v0i g0", T.tbb[:], T.val1[:], T.pf[:, 0:1], Op.not_equal)
+    ts("v0n", "v0i v0m", T.val1[:], T.val1[:], 64.4375, Op.add, U, Op.mult)
+    ts("c0a", "c0i g1", T.c0[:, 1, :], T.c0[:, 0, :], T.pf[:, 2:3], Op.is_equal, 128 * U, Op.mult)
+    tt("val1", "v0m v0n", T.val1[:], T.val1[:], T.tbb[:], Op.mult)
+
     for i in range(5):
         if i < 3:
             copy("xt", "xin", T.xt[:, i, :, :], T.xin[:, :, 4 * i:4 * i + 4], more=True)
@@ -175,97 +215,80 @@ def rank_program(g, core, T, topo):
     quant("xq", "xt xqz", T.xq[:, 0:320], T.xs[:, 0:320], T.xt[:])
 
     def constants0():
-        ts("iw2", "iw", T.iw[:], T.iw[:], 63, Op.bitwise_and)
-        fill("wm01", T.wm01[up], 0.0)
-        fill("pay0", T.pay[:, 40:41], 0.0)
-        ts("wm01", "iw2", T.wm01[lo], T.iw[lo], 0, Op.is_equal, more=True)
-        ts("cti2", "cti", T.cti[:], T.cti[:], 63, Op.bitwise_and)
-        ts("pj", "pi", T.pi[:, 4:6], T.pi[:, 0:2], 7, Op.bitwise_and)
-        fill("code0", T.cde[:], 1)
+        ts("c0b", "c0a", T.c0[:, 0, 0:9], T.c0[:, 1, 0:9], 8.0, Op.mult)
+        ts("n60b", "n60", T.n60[:], T.n60[:], 63, Op.bitwise_and)
+        tt("c0c", "c0a c0b", T.c0[:, 0, 1:9], T.c0[:, 0, 1:9], T.c0[:, 1, 0:8], Op.subtract)
+        ts("ngm", "n60b", T.ngm[:], T.n60[:, 0:4], -U / 512, Op.mult, 102560.0 / 512 * U, Op.add)
+        tt("i20b", "n60b i20", T.i20[:], T.i20[:], T.n60[:, 0:20], Op.add)
+        ts("n5", "n60b", T.n5[:], T.n60[:, 0:4], 5.0, Op.mult, -1.0, Op.add)
+        ts("c0", "c0c", T.c0[:, 0, 8:9], T.c0[:, 0, 8:9], 128 * U, Op.add)
 
     def constants3():
-        for c, w in ((0, 64), (64, 64), (128, 32)):
-            act("wat", "wm01", T.wat[:, c:c + w, :], T.wm01[:, 0:w, :], 0.625, more=c > 0)
-            act("wbt", "wm01", T.wbt[:, c:c + w, :], T.wm01[:, 0:w, :], -0.125, more=c > 0)
-        for j in range(3):
-            act("w3z", "zz", T.w3[:, j, :, :], T.zz[:], more=j > 0)
+        for k, c in (("wat", 5 * U), ("wbt", -U / 64)):
+            for a, w in ((0, 64), (64, 64), (128, 32)):
+                act(k, "wm wm0", T[k][:, a:a + w, :], T.wm[:, 0:w, :], c, more=a > 0)
+        act("wct", "zz", T.wct[:, 64:128, :], T.zz[:, 0:256])
+        for a, b, w in ((0, 0, 64), (128, 32, 32), (160, 0, 32)):
+            act("wct", "wm wm0", T.wct[:, a:a + w, :], T.wm[:, b:b + w, :], 5 * U, more=True)
         for j in range(2):
-            act("dg0", "zz", T.dg[:, 512 * j:512 * j + 512], T.zz[:], more=j > 0)
-        act("row0", "zz", T.row[:], T.zz[:, 0:400])
-
-    def constants1():
-        ts("ct", "cti2", T.ct[:], T.cti[:], -1.0 / 512, Op.mult, 64.0625, Op.add)
-        ts("s0", "pj", T.s0[:], T.pi[:, 4:6], 5.0, Op.mult, 64.0, Op.add)
-        ts("n40b", "n40", T.n40[:], T.n40[:], 63, Op.bitwise_and)
-        ts("ngm", "n40b", T.ngm[:], T.n40[:, 0:4], -1.0 / 512, Op.mult, 102560.0 / 512, Op.add)
-        ts("val0", "v0i", T.val0[:], T.val0[:], 64.4375, Op.add)
-        fill("tb0", T.tb[:, 50:51], 0.0)
-        fill("abk", T.ab[:, 0:150:3], 1 / EPS)
-        fill("dt0", T.dt3[:], 0.0)
+            act("dg0", "zz", T.dg[:, j, :, :, :], T.zz[:], more=j > 0)
 
     def constants2():
         for b in range(4):
             quant("e%d" % b, "et", T.eqc[:, 128 * b:128 * b + 128], T.eqs[:, 128 * b:128 * b + 128], T.et[:, 3 - b:515 - b])
             yield
-        ts("pj2", "pi", T.pi[:, 6:8], T.pi[:, 0:2], 4, Op.logical_shift_right, 1, Op.bitwise_and)
-        yield
-        ts("nb40", "n40b", T.nb40[:], T.n40[:], 4, Op.logical_shift_right)
-        yield
+            yield
         ts("nr2", "nr", T.nr[:], T.nr[:], 63, Op.bitwise_and)
+        yield
+        yield
         yield
         ts("jr2", "jr", T.jr[:], T.jr[:], 15, Op.bitwise_and)
         yield
-        copy("ngf", "n40b", T.ngf[:], T.n40[:, 0:4])
+        copy("ngf", "n60b", T.ngf[:], T.n60[:, 0:4])
         yield
-        fill("cqc1", T.cqc[:], -160.0)
+        ts("nb60", "n60b", T.nb60[:], T.n60[:], 4, Op.logical_shift_right)
         yield
-        fill("one5", T.one5[:], 1.0)
+        fill("pa16", T.pa16[:], 1.0)
         yield
-        fill("pc0", T.pc[:], 0.0)
+        ts("d16a", "d16i", T.d16i[:], T.d16i[:], 15, Op.bitwise_and)
         yield
-        fill("pk0", T.pk[:, 64:65], 0.0)
         yield
-        fill("cqc1", T.cqc[:, 15:65:16], 0.0)
+        fill("pa16", T.pa16[:, 0:64:16], 0.0)
         yield
-        fill("cf4", T.cf4[:, 0:4], 1024.0)
-        yield
-        fill("cf4", T.cf4[:, 4:8], 0.0, more=True)
-        yield
-        fill("cqc1", T.cqc[:, 64:65], 0.0)
-        yield
-        for a in (40, 208):
-            quant("dgqz", "zz", T.dgq[:, a:a + 128], T.dgs[:, a:a + 128], T.zz[:], more=True)
-            yield
+        for h, sl in halves:
+            for e in range(4):
+                ts("wt1", "nr2 ngf w3z", T.w3[sl, 1, 64 * h:64 * h + 64, e], T.nr[sl, :, e], T.ngf[sl, e:e + 1], Op.is_gt, -1.0, Op.mult, more=True)
+                yield
+                m = 16 * (7 - 4 * h - e)
+                ts("wt2", "jr2 w3z", T.w3[sl, 2, m:m + 16, e], T.jr[sl, :, e], 0, Op.is_equal, more=True)
+                yield
         quant("ptqz", "zz", T.ptq[:, 64:192], T.pts[:, 64:192], T.zz[:])
         yield
-        for h, sl in ((0, lo), (1, up)):
-            do("v", "w3z", "wt0", lambda: V.memset(T.w3[sl, 0, 64 * h:64 * h + 64, 1], 1.0), more=True)
-            yield
-            ts("wt0", "ik w3z", T.w3[sl, 0, 64 * h:64 * h + 64, 0], T.ik[sl, :], 0, Op.is_lt, more=True)
-            yield
-            for t in range(4):
-                ts("wt1", "nr2 ngf w3z", T.w3[sl, 1, 64 * h:64 * h + 64, t], T.nr[sl, :, t], T.ngf[sl, t:t + 1], Op.is_le, more=True)
-                yield
-                m = 64 * h + 16 * t
-                ts("wt2", "jr2 w3z", T.w3[sl, 2, m:m + 16, t], T.jr[sl, :, t], 0, Op.is_equal, more=True)
-                yield
-        ts("cqc", "n40b cqc1", T.cqc[:, 0:64:16], T.n40[:, 0:4], 5.0, Op.mult, -160.0, Op.add)
         yield
         for j in range(3):
             quant("qwt%d" % j, "wt%d" % j, T.cq3[:, 128 * j:128 * j + 128], T.cs3[:, 128 * j:128 * j + 128], T.w3[:, j, :, :])
             yield
             yield
-        for nb in range(4):
-            ts("msk", "nb40", T.msk[:, nb, :], T.nb40[:], nb, Op.is_equal, more=True)
+        for a in (40, 208):
+            quant("dgqz", "zz", T.dgq[:, a:a + 128], T.dgs[:, a:a + 128], T.zz[:], more=True)
             yield
-        copy("mo", "pj2", T.mo[:], T.pi[:, 6:8])
+            yield
+        for nb in range(4):
+            ts("msk", "nb60", T.msk[:, nb, :], T.nb60[:], nb, Op.is_equal, more=True)
+            yield
+        ts("d16b", "d16a", T.d16[:, 0, :], T.d16i[:], 0, Op.is_equal, 4 * LOW, Op.mult)
         yield
-        ts("me", "pj2", T.me[:], T.pi[:, 6:8], -1.0, Op.mult, 1.0, Op.add)
+        ts("d16c", "d16a", T.d16[:, 1, :], T.d16i[:], 1, Op.is_equal, LOW, Op.mult)
         yield
-        ts("cqo", "pj2", T.cqo[:, 0:1], T.pi[:, 6:7], 80.0, Op.mult, 160.0, Op.add)
+        ts("cb", "d16a", T.pf[:, 4:5], T.d16i[:, 15:16], 0, Op.not_equal, LOW / 512, Op.mult)
         yield
-        ts("cqo", "pj2", T.cqo[:, 1:2], T.pi[:, 6:7], 16.0, Op.mult, 160.0, Op.add, more=True)
+        tt("d16", "d16b d16c", T.d16[:, 0, :], T.d16[:, 0, :], T.d16[:, 1, :], Op.subtract)
+        yield
+        yield
+        ts("cb2", "cb", T.pf[:, 5:6], T.pf[:, 4:5], -0.499, Op.add)
 
+    fill("ne0", T.ne[:, :, 0:64:16], 0.0)
+    fill("ne0", T.ne[:, :, 15:64:16], 1.0, more=True)
     rest = constants2()
 
     def fillers(n):
@@ -286,214 +309,210 @@ def rank_program(g, core, T, topo):
             constants0()
         for i in range(5):
             if i % 2:
-                act("sc", "ps%d" % i, T.sc[:, :, i], ps[i][:, 0:32], more=i > 0)
+                act("sc", "ps%d" % i, T.sc[:, :, i, :], ps[i][:, 0:32], more=i > 0)
             else:
-                copy("sc", "ps%d" % i, T.sc[:, :, i], ps[i][:, 0:32], more=i > 0)
+                copy("sc", "ps%d" % i, T.sc[:, :, i, :], ps[i][:, 0:32], more=i > 0)
+
         def unpack():
-            for b, k in enumerate((5, 6, 7, 0)):
-                mm("ps%d" % k, "xq e%d" % b, (ps[k][:, 0:320], T.eqc[:, 128 * b:128 * b + 128], T.eqs[:, 128 * b:128 * b + 128], T.xq[:, 0:320], T.xs[:, 0:320]))
-                act("tp", "ps%d" % k, T.tp[:, 320 * b:320 * b + 320], ps[k][:, 0:320], 0.5, more=b > 0)
-            act("tw", "tp", T.tw[:], T.tp[:])
+            for b in range(4):
+                mm("ps%d" % b, "xq e%d" % b, (ps[b][:, 0:320], T.eqc[:, 128 * b:128 * b + 128], T.eqs[:, 128 * b:128 * b + 128], T.xq[:, 0:320], T.xs[:, 0:320]))
+                act("tp", "ps%d" % b, T.tp[:, 320 * b:320 * b + 320], ps[b][:, 0:320], 0.5, more=b > 0)
 
         if t == 0:
             constants3()
         else:
             unpack()
-        key = lambda a, b: T.sc[:, 3:32:4, a:b]
+        key = lambda a, b: T.sc[:, :, a:b, 3]
         for s in range(1, 5):
             tt("cm", "sc", T.cm[:, s - 1, :, 0:5 - s], key(s, 5), key(0, 5 - s), Op.is_gt, more=True)
             tt("cm", "sc", T.cm[:, s - 1, :, 5 - s:5], key(0, s), key(5 - s, 5), Op.is_ge, more=True)
-        for b in range(3):
-            ts("pb%d" % b, "sc", T.pb[:, b, :, :], T.sc[:, b:32:4, :], 0.0, Op.is_gt, 32.0 / 2 ** b, Op.mult)
+        for b in range(2):
+            ts("hb", "sc hb0", T.hb[:, 1 + b:160:4], T.sc[:, :, :, b], 0.0, Op.is_gt, more=b > 0)
         tt("a2", "cm", T.a2[:], T.cm[:, 0:2, :, :], T.cm[:, 2:4, :, :], Op.add)
-        tt("pac", "pb0 pb1", T.pac[:], T.pb[:, 0, :, :], T.pb[:, 1, :, :], Op.add)
-        tt("pad", "pb2 ci2", T.pad[:], T.pb[:, 2, :, :], T.ci2[:], Op.add)
-        tt("rk", "a2", T.rk[:], T.a2[:, 0, :, :], T.a2[:, 1, :, :], Op.add)
-        tt("pay", "pac pad", T.pay[:, 0:40], T.pac[:], T.pad[:], Op.add)
-        for r in range(3):
-            ts("ne1%d" % r, "rk", T.ne1[:, r, :], T.rk[:], 4.0 - r, Op.not_equal)
-        tt("d1a", "pay pay0", T.d1[:], T.pay[:, 0:40], T.pay[:, 1:41], Op.subtract)
-        for r in range(3, 5):
-            ts("ne1%d" % r, "rk", T.ne1[:, r, :], T.rk[:], 4.0 - r, Op.not_equal)
-        if t == 0:
-            quant("rqz", "zz", T.rq[:, 40:168], T.rs[:, 40:168], T.zz[:])
-        copy("d1", "pay d1a", T.d1[:, 4:40:5], T.pay[:, 4:40:5])
+        ts("hb", "sc hb0", T.hb[:, 3:160:4], T.sc[:, :, :, 2], 0.0, Op.is_gt, more=True)
+        fill("abb", T.ab[:, 2:150:3], EPS)
+        tt("rk", "a2", T.rk[:], T.a2[:, 0, :], T.a2[:, 1, :], Op.add)
+        scan("pay", "pa2 hb", T.pay[:], T.pa2[:], T.hb[:])
         for r in range(5):
-            scan("prb", "ne1%d d1" % r, T.prb[:, :, r], T.ne1[:, r, :], T.d1[:], more=True)
+            ts("eqr%d" % r, "rk", T.eqr[:, r, :], T.rk[:], 4.0 - r, Op.is_equal, 64.0, Op.mult)
+        for r in range(5):
+            scan("prb", "eqr%d pay" % r, T.prb[:, :, r], T.eqr[:, r, :], T.pay[:, 3:160:4], more=True, ops=LATCH)
+
+        def sym(i):
+            ts("rt2", "pay rt20", T.rt2[:, 0:2, 16 * i:16 * i + 20:5], T.pay[:, 3 + 4 * i:160:20], 3.5 - 8 * i, Op.add, more=i > 0)
+
+        if t == 0:
+            quant("wb", "wbt", T.wbq[:], T.wbs[:], T.wbt[:])
+        sym(0)
+        sym(1)
+        hi, lw = T.rt[:, 0:2, 0:4, 0:20:4], T.rt[:, 2:4, 0:4, 0:20:4]
+        ts("rth", "prb rt0", hi, T.prb[:, 4:40:5, :], M1 * 8, Op.add, M1 * 8, Op.subtract)
         if t == 0:
             quant("wa", "wat", T.waq[:], T.was[:], T.wat[:])
-            quant("wb", "wbt", T.wbq[:], T.wbs[:], T.wbt[:])
-        for e in range(4):
-            ts("rth%d" % e, "prb rt", T.rt[:, e:8:4, :, e], T.prb[:, 4 + 5 * e:40:20, :], M1 * 8, Op.add, M1 * 8, Op.subtract)
-        for e in range(4):
-            tt("rtl%d" % e, "prb rth%d" % e, T.rt[:, 8 + e:16:4, :, e], T.prb[:, 4 + 5 * e:40:20, :], T.rt[:, e:8:4, :, e], Op.subtract)
-        quant("rq", "rqz rth0 rth1 rth2 rth3 rtl0 rtl1 rtl2 rtl3", T.rq[:, 0:130], T.rs[:, 0:130], T.rt[:])
-        for k, w in ((1, 0), (2, 32)):
-            mm("ps%d" % k, "wa wb rq rqz",
-               (ps[k][:, 0:128], T.waq[:, w:w + 128], T.was[:, w:w + 128], T.rq[:, 0:128], T.rs[:, 0:128]),
-               (ps[k][:, 0:128], T.wbq[:, w:w + 128], T.wbs[:, w:w + 128], T.rq[:, 40:168], T.rs[:, 40:168]))
-        fill("abb", T.ab[:, 2:150:3], EPS)
+        sym(2)
+        sym(3)
+        tt("rtl", "prb rth", lw, T.prb[:, 4:40:5, :], hi, Op.subtract)
+        sym(4)
+        quant("rq", "rqz rth rtl", T.rq[:, 0:168], T.rs[:, 0:168], T.rt[:])
+        mm("ps5", "wa wb rq rqz", *[(ps[5][:, 0:128], wq[:, w:w + 128], wsc[:, w:w + 128], T.rq[:, c:c + 128], T.rs[:, c:c + 128])
+                                    for wq, wsc, w, c in ((T.wbq, T.wbs, 0, 0), (T.wbq, T.wbs, 32, 22), (T.waq, T.was, 0, 84), (T.waq, T.was, 32, 106))])
         if t == 0:
-            constants1()
-        tt("tb1", "ps1 ct", T.tb[:, 10:30], ps[1][:, 0:20], T.ct[:, 10:30], Op.add)
-        tt("tb2", "ps2 ct", T.tb[:, 30:50], ps[2][:, 20:40], T.ct[:, 30:50], Op.add)
-        tt("tb3", "ps2 ct", T.tb[:, 0:10], ps[2][:, 30:40], T.ct[:, 0:10], Op.add)
-        ts("aba", "val0 s0 abk", T.ab[:, 1:150:3], T.val0[:], T.s0[:, 0:1], Op.is_lt, EPS, Op.add)
-        tt("dtb", "tb1 tb2 tb3 tb0 dt0", T.dt3[:, 2:150:3], T.tb[:, 0:50], T.tb[:, 1:51], Op.subtract)
-        tt("tbm", "val0 tb1 tb2 tb3", T.tbb[:], T.val0[:], T.tb[:, 0:50], Op.is_ge)
-        scan("so0", "aba abb dtb", T.so[:, 0, :], T.ab[:], T.dt3[:])
-        tt("tbb", "tbm", T.tbb[:], T.tbb[:], T.tb[:, 0:50], Op.mult)
+            quant("wc", "wct", T.wcq[:], T.wcs[:], T.wct[:])
+            ts("ctp", "i20b", T.ctp[:], T.i20[:], -U / 512, Op.mult, 64.3125 * U, Op.add)
+        quant("rq2", "rq2z rt2", T.rq2[:, 0:132], T.rs2[:, 0:132], T.rt2[:])
+        mm("ps6", "wc rq2 rq2z", *[(ps[6][:, 0:128], T.wcq[:, w:w + 128], T.wcs[:, w:w + 128], T.rq2[:, c:c + 128], T.rs2[:, c:c + 128])
+                                   for w, c in ((0, 0), (64, 22))])
+        tt("tb1", "ps5 ct", T.tb[:, 10:50], ps[5][:, 0:40], T.ct[:, 10:50], Op.add)
+        tt("tb2", "ps5 ct", T.tb[:, 0:10], ps[5][:, 30:40], T.ct[:, 0:10], Op.add)
+        fillers(1)
+        scan("so0", "c0 tb1 tb0", T.so[:, 0, 141:150], T.c0[:, 0, 0:9], T.tb[:, 14:55:5], ops=LATCH)
+        tt("dtb", "tb1 tb2 tb0 dt0", T.dt3[:, 2:150:3], T.tb[:, 0:50], T.tb[:, 1:51], Op.subtract)
+        tt("tbm", "val1 tb1 tb2", T.tbb[:], T.val1[:], T.tb[:, 0:50], Op.is_ge)
+        tt("tbp", "ps6 ctp", T.tbp[:], ps[6][:, 0:20], T.ctp[:], Op.add)
+
         def cd(n):
-            ts("cd%d" % n, "so%d ngm code0" % n, T.cde[:, n + 1:64:16], T.ngm[:], T.so[:, n, 149:150], Op.subtract, 512.0, Op.mult)
+            ts("cd%d" % n, "so%d ngm cd0_" % n, T.cde[:, 14 - n:64:16], T.ngm[:], T.so[:, n, 149:150], Op.subtract, 512 / U, Op.mult)
 
-        def ca(n):
-            ts("ca%d" % n, "cd%d" % n, T.ca[:, n + 1:64:16], T.cde[:, n + 1:64:16], 63, Op.bitwise_and)
+        def marks(n):
+            s, so, a = T.so[:, n, 149:150], "so%d" % n, n % 2
+            if 0 < n < 12:
+                j = 10 if n < 3 else 5 if n < 8 else 0
+                act("sq%d" % a, "tb1 tb2 " + so, T.sq[:, a, j:50], T.tb[:, j:50], -1.0, bias=s, func=AF.Square)
+            if n == 0:
+                act("dp", "zf dp0 " + so, T.dp[:, 13:64:16], T.zf[:], bias=s)
+            else:
+                act("dp", "tt%d %s" % (1 - a, so), T.dp[:, 13 - n:64:16], T.tt4[:, 1 - a, :], -1.0, bias=s, more=True)
+            if n < 13:
+                act("sqp%d" % a, "tbp " + so, T.sqp[:, a, :], T.tbp[:], -1.0, bias=s, func=AF.Square)
+                act("tt%d" % a, "zf " + so, T.tt4[:, a, :], T.zf[:], bias=s)
+                act("ne", "sqp%d ne0" % a, T.ne[:, :, 14 - n:64:16], T.sqp[:, a, :], func=AF.Sign, more=n > 0)
 
-        def po(n):
-            ts("po%d" % n, "ca%d pt0" % n, T.pt[:, 4 * n + 4:256:64], T.ca[:, n + 1:64:16], 0, Op.is_equal)
-
-        def pe(n):
-            tt("pe%d" % n, "po%d pe%d pt0" % (n - 1, n - 1), T.pt[:, 4 * n + 5:256:64], T.pt[:, 4 * n + 1:256:64], T.pt[:, 4 * n:256:64], Op.add)
+        def undrawn(n):
+            a = n % 2
+            if n == 0:
+                ts("und0", "sqp0", T.und[:, 0, :], T.sqp[:, 0, :], 1.0, Op.min)
+            else:
+                tt("und%d" % a, "und%d sqp%d" % (1 - a, a), T.und[:, a, :], T.und[:, 1 - a, :], T.sqp[:, a, :], Op.min)
 
         for n in range(1, 14):
             s, so = T.so[:, n - 1, 149:150], "so%d" % (n - 1)
-            vk, vv = ("val0", T.val0[:]) if n == 1 else ("vl%d" % ((n - 1) % 2), T.val[:, (n - 1) % 2, :])
-            if n < 13:
-                ts("eq", so, T.eq[:], T.tb[:, 0:50], s, Op.is_equal, 64.0, Op.mult)
-            ts("aba", vk + " " + so, T.ab[:, 1:150:3], vv, s, Op.is_lt, EPS, Op.add)
-            ts("abb", "tbb " + so, T.ab[:, 2:150:3], T.tbb[:], s, Op.is_equal, EPS, Op.add)
-            cd(n - 1)
-            if n < 13:
-                tt("vl%d" % (n % 2), vk + " eq", T.val[:, n % 2, :], vv, T.eq[:], Op.subtract)
+            j = 10 if n < 5 else 5 if n < 10 else 0
+            vk, vv = ("val1", T.val1) if n < 3 else ("vl%d" % (n % 2), T.val[:, n % 2, :])
+            marks(n - 1)
+            ts("aba", vk + " abk " + so, T.ab[:, 3 * j + 1:150:3], T.val1[:, j:50] if n < 3 else T.val[:, n % 2, j:50], s, Op.is_lt, EPS, Op.add)
+            if n == 1:
+                tt("tbb", "tbm", T.tbb[:], T.tbb[:], T.tb[:, 0:50], Op.mult)
             else:
-                fillers(2)
-            scan("so%d" % n, "aba abb dtb", T.so[:, n, :], T.ab[:], T.dt3[:])
+                ts("abb", "tbb " + so, T.ab[:, 3 * j + 2:150:3], T.tbb[:, j:50], s, Op.is_equal, EPS, Op.add)
+            if 2 <= n < 13:
+                j2 = 10 if n < 4 else 5 if n < 9 else 0
+                old = T.val1[:, j2:50] if n < 3 else T.val[:, n % 2, j2:50]
+                tt("vl%d" % ((n + 1) % 2), vk + " sq%d" % ((n - 1) % 2), T.val[:, (n + 1) % 2, j2:50], old, T.sq[:, (n - 1) % 2, j2:50], Op.min)
+            elif n == 13:
+                cd(12)
+            scan("so%d" % n, "aba abb dtb", T.so[:, n, 3 * j:150], T.ab[:, 3 * j:150], T.dt3[:, 3 * j:150])
+            if n in (3, 8):
+                j2, a = 5 if n == 3 else 0, (n + 1) % 2
+                ts("vl%d" % a, "vl%d" % a, T.val[:, a, j2:j2 + 5], T.val[:, a, 40 + j2:45 + j2], 2.0, Op.mult, more=True)
+            if n < 13:
+                cd(n - 1)
             if n >= 2:
-                po(n - 2)
-            if n >= 3:
-                pe(n - 2)
-            ca(n - 1)
-            fillers(4)
+                undrawn(n - 2)
+            fillers(5)
             if t == 0 and n == 5:
                 unpack()
         fillers(99)
-        cd(13)
-        ts("phii", "so0 so13", T.phii[:], T.so[:, :, 149], -512.0, Op.mult, 102560.0, Op.add)
-        po(12)
-        pe(12)
-        ca(13)
-        ts("phij", "phii", T.phii[:], T.phii[:], 511, Op.bitwise_and)
-        pe(13)
-        po(13)
-        ts("cdf", " ".join("cd%d" % n for n in range(14)), T.cdf[:], T.cde[:], 511, Op.bitwise_and)
-        ts("phi", "phij", T.phi[:], T.phii[:], -160.0, Op.add)
+        s = T.so[:, 13, 149:150]
+        marks(13)
+        ts("ca", " ".join("cd%d" % n for n in range(13)), T.ca[:], T.cde[:], 63, Op.bitwise_and)
+        ts("c13", "so13 ngm", T.c13[:], T.ngm[:], s, Op.subtract, 512 / U, Op.mult)
+        ts("ne13", "so13 tbp ne0", T.ne[:, :, 1:64:16], T.tbp[:], s, Op.not_equal)
+        undrawn(12)
+        ts("po0", "ca pt0", T.pt[:, 0:256:4], T.ca[:], 0, Op.is_equal)
+        ts("c13", "c13", T.c13[:], T.c13[:], 63, Op.bitwise_and)
+        ts("po1", "ca pt0", T.pt[:, 1:252:4], T.ca[:, 1:64], 0, Op.is_equal)
+        scan("pe", "pa16 po0", T.pe[:], T.pa16[:], T.pt[:, 0:256:4])
+
+        def before(i):
+            scan("uopp", "ne ne13 dp", T.uop[:, 0, i, :], T.ne[:, i, :], T.dp[:], more=i > 0)
+
+        before(0)
+        before(1)
+        ts("po0", "c13", T.pt[:, 4:256:64], T.c13[:], 0, Op.is_equal)
+        ts("po1", "c13", T.pt[:, 1:256:64], T.c13[:], 0, Op.is_equal)
         for e in range(4):
-            act("pc", "phi pc0", T.pc[:, 16 * e + 2:16 * e + 15], T.phi[:, 0:13], more=e > 0)
-        act("pc", "phi cf4", T.pc[:, 0:64:16], T.cf4[:, 0:4], bias=T.phi[:, 13:14], more=True)
-        act("pc", "phi cf4", T.pc[:, 1:64:16], T.cf4[:, 4:8], bias=T.phi[:, 13:14], more=True)
-        tt("ptu", "pe13 po13 pt0", T.pt[:, 256:452:65], T.pt[:, 57:256:64], T.pt[:, 56:256:64], Op.add)
-        for i in range(3):
-            ts("nea", "cdf", T.nei[:, i, :], T.cdf[:], 64.0 * i, Op.not_equal, more=i > 0)
-        quant("ptq", "ptu ptqz " + " ".join("po%d" % n for n in range(14)) + " " + " ".join("pe%d" % n for n in range(1, 14)), T.ptq[:, 0:128], T.pts[:, 0:128], T.pt[:])
-        mm("ps3", "ptq ptqz qwt0 qwt1", (ps[3][:, 0:128], *W3(0), T.ptq[:, 0:128], T.pts[:, 0:128]),
-           (ps[3][:, 0:128], *W3(1), T.ptq[:, 64:192], T.pts[:, 64:192]))
-        for i in range(3, 5):
-            ts("nea", "cdf", T.nei[:, i, :], T.cdf[:], 64.0 * i, Op.not_equal, more=True)
-        do("v", "nea", "nei", lambda: V.memset(T.nei[:, :, 0:64:16], 0.0))
-        tt("dp", "pc pc0", T.dp[:], T.pc[:, 0:64], T.pc[:, 1:65], Op.subtract)
-        for i in range(5):
-            scan("uop", "nei dp", T.uop[:, i, :], T.nei[:, i, :], T.dp[:], more=True)
-        up5 = T.uop[:, :, 14:64:16]
+            ts("po3", "c13 pe pt0", T.pt[:, 256 + 65 * e:257 + 65 * e], T.c13[:, e:e + 1], 0, Op.is_equal, T.pe[:, 16 * e + 15:16 * e + 16], Op.add, more=e > 0)
+        before(2)
+        before(3)
+        quant("ptq", "po0 po1 po3 ptqz", T.ptq[:, 0:128], T.pts[:, 0:128], T.pt[:])
+        mm("ps4", "ptq ptqz qwt0 qwt1", (ps[4][:, 0:128], *W3(0), T.ptq[:, 0:128], T.pts[:, 0:128]),
+           (ps[4][:, 0:128], *W3(1), T.ptq[:, 64:192], T.pts[:, 64:192]))
+        before(4)
+        tt("fl und1", "und0 ne13", T.und[:, 1, :], T.und[:, 0, :], T.ne[:, :, 1:64:16], Op.mult)
+
+        def digits(x):
+            for d, m in enumerate((15, 240, 256) if x == "p" else (15, -16)):
+                j = int(x == "q")
+                ts("di" + x, "v2" + x, T.dgi[:, 3 * j + d, :], T.v2[:, j, :], m, Op.bitwise_and, more=d > 0)
 
         def spread(x):
-            j = int(x == "q")
+            j, nd = (1, 2) if x == "q" else (0, 3)
             for nb in range(4):
-                tt("vm" + x, "v2%s msk" % x, T.vm[:, j, :, nb, :], T.v2[:, 20 * j:20 * j + 20], T.msk[:, nb, 0:20], Op.mult, more=nb > 0)
-
-        def digit(x, j):
-            c, m = 512 * int(x == "q"), T.vm[:, int(x == "q"), :, :, :]
-            if j:
-                ts("dh" + x, "vm%s dg0" % x, T.dg[:, c + 80:c + 160], m, M1 * 32, Op.add, M1 * 32, Op.subtract)
-            else:
-                tt("dl" + x, "vm%s dh%s" % (x, x), T.dg[:, c:c + 80], m, T.dg[:, c + 80:c + 160], Op.subtract)
+                tt("dg" + x, "di%s msk dg0" % x, T.dg[:, j, 0:5 * nd, nb, :], T.dgi[:, 3 * j:3 * j + nd, :], T.msk[:, nb, 0:20 * nd], Op.mult, more=nb > 0)
 
         def form(x, k):
-            c = 168 * (x == "q")
-            quant("dg" + x, "dh%s dl%s dgqz" % (x, x), T.dgq[:, c:c + 128], T.dgs[:, c:c + 128], T.dg[:, 512 * (x == "q"):512 * (x == "q") + 512])
-            mm("ps%d" % k, "dg%s dgqz qwt2" % x, (ps[k][:, 0:128], *W3(2), T.dgq[:, c:c + 128], T.dgs[:, c:c + 128]),
-               (ps[k][:, 0:128], *W3(2), T.dgq[:, c + 20:c + 148], T.dgs[:, c + 20:c + 148]))
+            j, nd = (1, 2) if x == "q" else (0, 3)
+            c = 168 * j
+            quant("dq" + x, "dg%s dgqz" % x, T.dgq[:, c:c + 128], T.dgs[:, c:c + 128], T.dg[:, j, :, :, :])
+            mm("ps%d" % k, "dq%s dgqz qwt2" % x, *[(ps[k][:, 0:128], *W3(2), T.dgq[:, c + 20 * d:c + 20 * d + 128], T.dgs[:, c + 20 * d:c + 20 * d + 128]) for d in range(nd)])
 
-        def blend(b):
-            cs = slice(320 * b, 320 * b + 320)
-            tt("zp%d" % b, "tp tw ofp", T.zp[:, cs], T.tw[:, cs].indirect(T.ofp[:, 0:20]), T.tp[:, cs], Op.add)
-
-        tt("pk", "ps3 cqc", T.pk[:, 0:64], ps[3][:, 0:64], T.cqc[:, 0:64], Op.add)
-        ts("fl", "uop", T.fl[:], up5, 512.0, Op.is_ge)
-        ts("flm", "uop", T.flm[:], up5, 512.0, Op.is_ge, -1024.0, Op.mult)
-        tt("dp", "pk pk0", T.dp[:], T.pk[:, 0:64], T.pk[:, 1:65], Op.subtract)
-        tt("v2p", "uop flm", T.v2[:, 0:20], up5, T.flm[:], Op.add)
+        ts("v2p", "uopp", T.v2[:, 0, :], T.uop[:, 0, :, 13:64:16], -512 / U, Op.mult, 102560.0, Op.add)
         for e in range(4):
-            scan("inc", "fl one5", T.inc[:, e:20:4], T.one5[:, 0:5], T.fl[:, e:20:4], more=True, initial=-1.0)
+            scan("inc", "pa16 fl n5", T.inc[:, e:20:4], T.pa16[:, 1:6], T.und[:, 1, e:20:4], more=e > 0, initial=T.n5[:, e:e + 1])
+        digits("p")
+        tt("pr0", "fl inc", T.pr[:], T.und[:, 1, :], T.inc[:], Op.mult)
         for i in range(5):
-            scan("uop", "nei dp", T.uop[:, i, :], T.nei[:, i, :], T.dp[:], more=i > 0)
-        tt("pr", "fl inc", T.pr[:], T.fl[:], T.inc[:], Op.mult)
+            scan("uopq", "ne ne13 ps4", T.uop[:, 1, i, :], T.ne[:, i, :], ps[4][:, 0:64], more=i > 0)
+        ts("pr", "pr0", T.pr[:], T.pr[:], -160.0, Op.add)
         spread("p")
-        tt("v2q", "uop pr", T.v2[:, 20:40], up5, T.pr[:], Op.add)
-        digit("p", 1)
-        spread("q")
-        digit("p", 0)
-        digit("q", 1)
+        tt("v2q", "uopq pr", T.v2[:, 1, :], T.uop[:, 1, :, 15:64:16], T.pr[:], Op.add)
         form("p", 5)
-        digit("q", 0)
-        form("q", 4)
-        ts("ofp", "ps5", T.ofp[:], ps[5][:, 0:20], 160.0, Op.add)
-        blend(0)
-        ci = 1 if final else 0
-        ts("ofq", "ps4 cqo", T.ofq[:], ps[4][:, 0:20], T.cqo[:, ci:ci + 1], Op.add)
-        do("v", "ofq phr row0", "row", lambda: V.tensor_copy(T.row[:].indirect(T.ofq[:, 0:20]), T.phr[:]))
-        blend(1)
-        if final:
-            for a in range(2):
-                do("v", "row", "tr", lambda: V.transpose(T.trl[:, a, :], T.row[:, 16 * a:16 * a + 320]), more=a > 0)
-            blend(2)
-            for a in range(2):
-                ts("te%d" % a, "tr me", T.te[:, a:20:2], T.trl[:, a, 0:320:32], T.me[:, 0:1], Op.mult)
-                ts("to%d" % a, "tr mo", T.to[:, a:20:2], T.trl[:, a, 16:320:32], T.mo[:, 0:1], Op.mult)
-        else:
-            for i in range(5):
-                for a in range(2):
-                    c = i + 80 * a
-                    do("v", "row", "tr", lambda: V.transpose(T.tr[:, i, a, :], T.row[:, c:c + 316:5]), more=i + a > 0)
-            blend(2)
-            for h in range(2):
-                sl = slice(10 * h, 10 * h + 10)
-                ts("te%d" % h, "tr me", T.te[:, sl], T.tr[:, :, :, 32 * h], T.me[:, 0:1], Op.mult)
-                ts("to%d" % h, "tr mo", T.to[:, sl], T.tr[:, :, :, 32 * h + 16], T.mo[:, 0:1], Op.mult)
-        blend(3)
-        tt("ql", "te0 te1 to0 to1", T.to[:], T.te[:], T.to[:], Op.add)
-        copy("off0", "ql", T.off[:], T.to[:])
+        digits("q")
+        spread("q")
+        form("q", 6)
+        copy("ofp", "ps5", T.ofp[:], ps[5][:, 0:20])
+        tt("pk", "ofp phr ph512", T.pk[:], T.phr[:].indirect(T.ofp[:]), T.ph512[:], Op.add)
+        ts("ofq", "ps6", T.ofq[:], ps[6][:, 0:20], 160.0, Op.add)
+        do("v", "ofq pk", "row", lambda: V.tensor_copy(T.row[:].indirect(T.ofq[:]), T.pk[:]))
+        for i in range(5):
+            scan("s5", "d16 row", T.s5[:, i, :], T.d16[:, 0, :], T.row[:, 64 * i:64 * i + 64] if final else T.row[:, i:320:5], more=i > 0, ops=LATCH)
+        parts = [(slice(0, 20), slice(0, 4))] if final else [(slice(10 * h, 10 * h + 10), slice(2 * h, 2 * h + 2)) for h in range(2)]
+        for h, (o, v) in enumerate(parts):
+            ts("offa%d" % h, "s5 cb2", T.offa[:, o], T.s5[:, :, 15 + 16 * v.start:16 * v.stop:16], 1 / 512, Op.mult, T.pf[:, 5:6], Op.add)
+            if h == 0:
+                copy("xi", "s5", T.xi[:], T.s5[:, :, 15:64:16])
+        for h, (o, v) in enumerate(parts):
+            ts("xj", "xi", T.xj[:, o], T.xi[:, :, v], 511, Op.bitwise_and, more=h > 0)
+        copy("offb", "xj", T.offb[:], T.xj[:])
 
         def picks(h):
-            o, cs = T.off[:, 10 * h:10 * h + 10], slice(640 * h, 640 * h + 640)
-            for b in range(2):
-                do("v", "off0 zp%d" % b, "zt%d" % h, lambda: V.tensor_copy(T.zt[:, 640 * h + b:640 * h + 640:4], T.zp[:, 320 * b:320 * b + 320].indirect(o)), more=b > 0)
-            for b in range(2, 4):
-                act("zt%d" % h, "off0 zp%d" % b, T.zt[:, 640 * h + b:640 * h + 640:4], T.zp[:, 320 * b:320 * b + 320].indirect(o), more=True)
-            return cs
+            o = slice(10 * h, 10 * h + 10)
+            for b in range(4):
+                act("at%d%d" % (h, b), "offa%d tp" % (0 if final else h), T.at[:, 640 * h + b:640 * h + 640:4], T.tp[:, 320 * b:320 * b + 320].indirect(T.offa[:, o]))
+            for b in range(4):
+                cs = slice(640 * h + b, 640 * h + 640, 4)
+                tt("zt%d" % h, "offb tp at%d%d" % (h, b), T.zt[:, cs], T.tp[:, 320 * b:320 * b + 320].indirect(T.offb[:, o]), T.at[:, cs], Op.add, more=b > 0)
+            return slice(640 * h, 640 * h + 640)
 
-        def kept(h, b, e):
-            o = T.off[:, 10 * h:10 * h + 10]
-            out, win = T.at[:, 640 * h + b:640 * h + 640:4], T.tp[:, 320 * b:320 * b + 320].indirect(o)
-            if e == "v":
-                ts("at%d%d" % (h, b), "off0 tp", out, win, 2048.0, Op.mult)
-            else:
-                act("at%d%d" % (h, b), "off0 tp", out, win, 2048.0)
+        def kept(h):
+            cs = slice(640 * h, 640 * h + 640)
+            act("ak%d" % h, " ".join("at%d%d" % (h, b) for b in range(4)), T.ak[:, cs], T.at[:, cs], 2048.0)
 
         def new(h, b, k, cod):
             mm("ps%d" % k, "wq " + cod[0], (ps[k][:, 0:160], T.wq[:, 128 * b:128 * b + 128], T.wsc[:, 128 * b:128 * b + 128], cod[1], cod[2]))
 
         def finish(h, b, k):
-            tt("tm%d%d" % (h, b), "ps%d at%d%d" % (k, h, b), T.tm[:, 4 * h + b, :], ps[k][:, 0:160], T.at[:, 640 * h + b:640 * h + 640:4], Op.add)
+            tt("tm%d%d" % (h, b), "ps%d ak%d" % (k, h), T.tm[:, 4 * h + b, :], ps[k][:, 0:160], T.ak[:, 640 * h + b:640 * h + 640:4], Op.add)
             if final:
                 act("xl%d" % h, "tm%d%d" % (h, b), T.xl[:, 640 * h + b:640 * h + 640:4], T.tm[:, 4 * h + b, :], 2.0 ** -11, more=b > 0)
             else:
@@ -501,35 +520,32 @@ def rank_program(g, core, T, topo):
 
         rc = slice(160 * t, 160 * t + 160)
         cs = picks(0)
-        quant("sq%d" % t, "zt0", T.sendc[:, rc], T.sendp[:, rc], T.zt[:, cs])
+        quant("send%d" % t, "zt0", T.sendc[:, rc], T.sendp[:, rc], T.zt[:, cs])
         dst = partner_of(t)
         rid, pid, _ = topo.addr(dst)
-        pre("p", "sq%d" % t, "")
+        pre("p", "send%d" % t, "")
         for a, b in ((T.landc[:, rc].bitcast(dt.uint8), T.sendc[:, rc].bitcast(dt.uint8)), (T.landp[:, rc], T.sendp[:, rc])):
             g.remote_dma(a, b, T.sem["arr%d" % t], T.sem["snd%d" % t], pid, rid, topo.mask(core, dst))
         eng = 2 * len(topo.engines(core, dst))
         last["land%d" % t] = {"arr%d" % t: eng}
         cs = picks(1)
-        quant("stay%d" % t, "zt1", T.stayc[:, rc], T.stayp[:, rc], T.zt[:, cs])
+        kept(1)
+        kept(0)
+        quant("stay", "zt1", T.lq[:, 0:160], T.lsc[:, 0:160], T.zt[:, cs])
         for b in range(4):
-            new(1, b, 4 + b, ("stay%d" % t, T.stayc[:, rc], T.stayp[:, rc]))
-        for h in (1, 0):
-            for b in range(4):
-                kept(h, b, "v" if b < 2 else "s")
-            if h:
-                for b in range(4):
-                    finish(1, b, 4 + b)
+            new(1, b, 4 + b, ("stay", T.lq[:, 0:160], T.lsc[:, 0:160]))
         if t == 0:
             quant("vq", "vt", T.vq[:], T.vs[:], T.vt[:])
+        for b in range(4):
+            finish(1, b, 4 + b)
         if final:
+            do("v", "ofq lgr", "pk", lambda: V.tensor_copy(T.pk[:].indirect(T.ofq[:]), T.lgr[:]))
+            do("y", "pk", "", lambda: Y.dma_start(T.oq[:], T.pk[0:128:16, :]), "fin", 16)
             quant("lq1", "xl1", T.lq[:, 160:320], T.lsc[:, 160:320], T.xl[:, 640:1280])
-            do("v", "ofq lgr row0", "row", lambda: V.tensor_copy(T.row[:].indirect(T.ofq[:, 0:20]), T.lgr[:]))
             mm("ps4", "lq1 vq", (ps[4][:, 0:160], T.vq[:], T.vs[:], T.lq[:, 160:320], T.lsc[:, 160:320]))
-            do("y", "row", "", lambda: Y.dma_start(T.oq[0:8:2, :], T.row[0:128:32, 0:320]), "fin", 16)
-            do("y", "row", "", lambda: Y.dma_start(T.oq[1:8:2, :], T.row[16:128:32, 16:336]), "fin", 16)
             do("y", "lq1", "", lambda: Y.dma_start(T.oc[:, 640:1280], T.lq[:, 160:320].bitcast(dt.uint8)), "fin", 16)
-            copy("yb1", "ps4", T.yb[:, 160:320], ps[4][:, 0:160])
-            do("y", "yb1", "", lambda: Y.dma_start(T.y[:, 160:320], T.yb[:, 160:320]), "fin", 16)
+            act("yb1 row", "ps4", T.row[:, 160:320], ps[4][:, 0:160])
+            do("y", "yb1", "", lambda: Y.dma_start(T.y[:, 160:320], T.row[:, 160:320]), "fin", 16)
         for b in range(4):
             new(0, b, b, ("land%d" % t, T.landc[:, rc], T.landp[:, rc]))
         for b in range(4):
@@ -538,14 +554,13 @@ def rank_program(g, core, T, topo):
         if not final:
             quant("xq", "xt xqz", T.xq[:, 0:320], T.xs[:, 0:320], T.xt[:])
 
-    quant("lq0", "xl0", T.lq[:, 0:160], T.lsc[:, 0:160], T.xl[:, 0:640])
+    quant("lq0 stay", "xl0", T.lq[:, 0:160], T.lsc[:, 0:160], T.xl[:, 0:640])
     mm("ps5", "lq0 vq", (ps[5][:, 0:160], T.vq[:], T.vs[:], T.lq[:, 0:160], T.lsc[:, 0:160]))
     do("y", "lq0", "", lambda: Y.dma_start(T.oc[:, 0:640], T.lq[:, 0:160].bitcast(dt.uint8)), "fin", 16)
+    act("yb0", "ps5", T.row[:, 0:160], ps[5][:, 0:160])
+    do("s", "yb0", "", lambda: S.dma_start(T.y[:, 0:160], T.row[:, 0:160]), "fin", 16)
     for k in range(4):
-        q = ("s", S) if k % 2 else ("y", Y)
-        do(q[0], "lq0 lq1", "", lambda: q[1].dma_start(T.osc[4 * k:4 * k + 4, :], T.lsc[32 * k:32 * k + 4, :]), "fin", 16)
-    copy("yb0", "ps5", T.yb[:, 0:160], ps[5][:, 0:160])
-    do("y", "yb0", "", lambda: Y.dma_start(T.y[:, 0:160], T.yb[:, 0:160]), "fin", 16)
+        do("y", "lq0 lq1", "", lambda: Y.dma_start(T.osc[4 * k:4 * k + 4, :], T.lsc[32 * k:32 * k + 4, :]), "fin", 16)
     need("y", "fin", count["fin"])
     for k in ("v", "s", "t", "p"):
         need("y", k, count[k])

@@ -10,27 +10,28 @@ def _sb(t, *s):
 
 
 SCRATCH = {
-    "xin": _sb(B, 64, 20), "xt": _sb(B, 5, 64, 4), "xl": _sb(B, 1280), "ut": _sb(B, 512), "vt": _sb(B, 512),
-    "xq": _sb(C8, 384), "xs": _sb(U8, 384), "uq": _sb(C8, 128), "us": _sb(U8, 128), "vq": _sb(C8, 128), "vs": _sb(U8, 128),
-    "wq": _sb(C8, 512), "wsc": _sb(U8, 512), "lq": _sb(C8, 320), "lsc": _sb(U8, 320),
-    "sc": _sb(F, 8, 5, 4), "cm": _sb(B, 4, 8, 5), "a2": _sb(B, 2, 40), "hb": _sb(B, 160), "rk": _sb(B, 40), "pay": _sb(B, 160),
-    "eqr": _sb(B, 5, 40), "prb": _sb(F, 40, 5), "rt": _sb(B, 4, 8, 21), "rq": _sb(C8, 234), "rs": _sb(U8, 234),
+    "xin": _sb(B, 64, 20), "xt": _sb(B, 2, 5, 32, 4), "ut": _sb(B, 512), "vt": _sb(B, 512),
+    "xq": _sb(C8, 320), "xs": _sb(U8, 320), "uq": _sb(C8, 128), "us": _sb(U8, 128), "vq": _sb(C8, 128), "vs": _sb(U8, 128),
+    "uq0": _sb(C8, 128), "us0": _sb(U8, 128), "uo": _sb(U16, 8), "uf": _sb(F, 8),
+    "wq": _sb(C8, 512), "wsc": _sb(U8, 512), "lq": _sb(C8, 160), "lsc": _sb(U8, 160),
+    "sc": _sb(F, 8, 5, 4), "cm": _sb(B, 4, 8, 5), "a2": _sb(B, 2, 40), "hb": _sb(B, 160), "rk": _sb(B, 80), "pay": _sb(B, 320),
+    "eqr": _sb(B, 5, 80), "prb": _sb(F, 80, 5), "rt": _sb(B, 4, 8, 21), "rq": _sb(C8, 168), "rs": _sb(U8, 168),
     "rt2": _sb(B, 6, 88), "rq2": _sb(C8, 150), "rs2": _sb(U8, 150),
-    "tb": _sb(F, 56), "tbb": _sb(F, 50), "val": _sb(F, 2, 50), "sq": _sb(F, 2, 50), "ab": _sb(F, 150), "dt3": _sb(F, 150),
-    "so": _sb(F, 14, 150), "tbp": _sb(F, 20), "sqp": _sb(F, 2, 20), "und": _sb(F, 2, 20), "tt4": _sb(F, 2, 4),
-    "cde": _sb(I, 64), "ca": _sb(I, 64), "c13": _sb(I, 4), "pe": _sb(F, 64), "pt": _sb(B, 512),
+    "tb": _sb(F, 56), "tbb": _sb(F, 50), "val": _sb(F, 2, 50), "sq": _sb(F, 2, 50), "ab": _sb(F, 2, 150), "dt3": _sb(F, 2, 150),
+    "so": _sb(F, 17, 150), "tbp": _sb(F, 20), "sqp": _sb(F, 3, 20), "und": _sb(F, 2, 20), "tt4": _sb(F, 2, 4),
+    "cde": _sb(I, 64), "ca": _sb(I, 64), "pe": _sb(F, 64), "pt": _sb(B, 512),
     "ptq": _sb(C8, 192), "pts": _sb(U8, 192), "ne": _sb(F, 5, 64), "dp": _sb(F, 64), "uop": _sb(F, 2, 5, 64),
-    "inc": _sb(F, 20), "pr": _sb(F, 20), "v2": _sb(I, 2, 20), "dgi": _sb(I, 5, 20), "dg": _sb(B, 2, 32, 4, 4),
+    "inc": _sb(F, 24), "pr": _sb(F, 20), "v2": _sb(I, 2, 20), "dgi": _sb(I, 5, 20), "dg": _sb(B, 2, 32, 4, 4),
     "dgq": _sb(C8, 336), "dgs": _sb(U8, 336), "ofp": _sb(U16, 20), "ofq": _sb(U16, 20), "pk": _sb(F, 320), "row": _sb(F, 320),
     "s5": _sb(F, 5, 64), "xi": _sb(I, 5, 4), "xj": _sb(I, 20), "offa": _sb(U16, 20), "offb": _sb(U16, 20),
     "tp": _sb(B, 1280), "zt": _sb(B, 1280), "at": _sb(B, 1280), "ak": _sb(B, 1280), "tm": _sb(F, 8, 160),
-    "zz": _sb(B, 512), "zf": _sb(F, 4), "wm": _sb(B, 64, 4), "wat": _sb(B, 160, 4), "wbt": _sb(B, 160, 4), "wct": _sb(B, 192, 4),
-    "waq": _sb(C8, 160), "was": _sb(U8, 160), "wbq": _sb(C8, 160), "wbs": _sb(U8, 160), "wcq": _sb(C8, 192), "wcs": _sb(U8, 192),
+    "zz": _sb(B, 512), "zf": _sb(F, 4), "wm": _sb(B, 64, 4), "wat": _sb(B, 160, 4), "wct": _sb(B, 192, 4),
+    "waq": _sb(C8, 160), "was": _sb(U8, 160), "wcq": _sb(C8, 192), "wcs": _sb(U8, 192),
     "et": _sb(B, 516), "ones": _sb(B, 128), "eqc": _sb(C8, 512), "eqs": _sb(U8, 512),
     "w3": _sb(B, 3, 128, 4), "cq3": _sb(C8, 384), "cs3": _sb(U8, 384),
     "nr": _sb(I, 64, 4), "jr": _sb(I, 16, 4), "n60": _sb(I, 60), "nb60": _sb(I, 60), "msk": _sb(F, 4, 60), "ngf": _sb(F, 4),
-    "i20": _sb(I, 20), "ctp": _sb(F, 20), "ngm": _sb(F, 4), "n5": _sb(F, 4),
-    "cti": _sb(I, 50), "ct": _sb(F, 50), "val1": _sb(F, 50), "pi": _sb(I, 4), "pf": _sb(F, 8), "c0": _sb(F, 2, 10), "ci": _sb(F, 40),
+    "i20": _sb(I, 20), "ctp": _sb(F, 20), "ngm": _sb(F, 3, 4),
+    "cti": _sb(I, 50), "ct": _sb(F, 50), "val1": _sb(F, 50), "pi": _sb(I, 8), "pf": _sb(F, 10), "c0": _sb(F, 3, 10),
     "pa2": _sb(B, 160), "pa16": _sb(F, 64), "d16i": _sb(I, 64), "d16": _sb(F, 2, 64),
     "phr": _sb(F, 320), "ph512": _sb(F, 320), "lgr": _sb(F, 320),
 }
@@ -139,39 +140,38 @@ def rank_program(g, core, T, topo):
         post("t", 1, rd, wr)
 
     do("y", "", "xin", lambda: Y.dma_start(T.xin[:], T.x[:]), "dx", 16)
-    for G in range(8):
-        gg = 7 - G
-        q = ("s", S) if G % 2 else ("y", Y)
-        do(q[0], "", "ut", lambda: q[1].dma_start(T.ut[:, 16 * G:16 * G + 16], T.u[:, 64 * gg:64 * gg + 16]), "du", 16, more=True)
-    do("s", "", "ut", lambda: S.dma_start(T.ut[:, 128:512], T.u[:, 128:512]), "du", 16, more=True)
-    do("s", "", "wq", lambda: S.dma_start(T.wq[:].bitcast(dt.uint8), T.wc[:]), "dw", 16, more=True)
-    do("s", "", "wq", lambda: S.dma_start(T.wsc[:], T.ws[:]), "dw", 16, more=True)
-    do("y", "", "vt", lambda: Y.dma_start(T.vt[:], T.v[:]), "dv", 16)
+    do("s", "", "ut", lambda: S.dma_start(T.ut[:], T.u[:]), "du", 16)
 
     lo, up = slice(0, 64), slice(64, 128)
     halves = ((0, lo), (1, up))
     fill("zz", T.zz[:], 0.0)
     fill("ones", T.ones[:], 1.0)
     fill("et0", T.et[:], 0.0)
-    fill("wm0", T.wm[up], 0.0)
-    iota("pi", T.pi[:], [[0, 4]], 0, 1)
+    fill("wc0", T.wct[:], 0.0)
+    iota("pi", T.pi[:], [[0, 8]], 0, 1)
+    iotaf("uf", T.uf[:], [[0, 4], [-64, 2]], 112, 0)
     iota("cti", T.cti[:], [[-8, 10], [0, 5]], 72, 1)
     iotaf("v0i", T.val1[:], [[-1, 50]], 49, 0)
-    iotaf("cii", T.ci[:], [[0, 8], [1, 5]], 0, 0)
+    iotaf("v0j", T.sq[:], [[0, 2], [40, 2], [-1, 25]], 9, 0)
+    iotaf("c0i", T.c0[:, 0, :], [[1, 10]], -7, 0)
+    iotaf("hb0", T.hb[:, 0:160:4], [[0, 8], [1, 5]], 0, 0)
+    iotaf("pay0", T.pay[:, 163:320:4], [[0, 8], [8, 5]], 0, 0)
     select("wm1", "zz", T.wm[lo], T.zz[lo, 0:256], [[-1, 64], [8, 4]], Op.not_equal, 1.0, -56, 1)
     select("wm", "wm1", T.wm[lo], T.wm[lo], [[-1, 64], [8, 4]], Op.not_equal, 1.0, 8, 1)
-    iotaf("c0i", T.c0[:, 0, :], [[1, 10]], -7, 0)
     for h, sl in halves:
         iota("n60", T.n60[sl, :], [[0, 15], [-8, 4]], 120 - 32 * h, 1, more=True)
     iota("i20", T.i20[:], [[64, 5], [0, 4]], 0, 0)
+    iota("d16i", T.d16i[:], [[1, 64]], 128, -1)
+    for h, sl in halves:
+        iotaf("gc%d" % h, T.ngm[sl, 2, :], [[-1, 4]], 71 - 4 * h, 0)
     select("et", "ones et0", T.et[:, 3:515:4], T.ones[:], [[-1, 128]], Op.is_equal, 0.0, 0, 1)
     for h, sl in halves:
         iota("nr", T.nr[sl], [[1, 64], [-8, 4]], 120 - 32 * h, 0, more=True)
     iota("jr", T.jr[:], [[1, 16], [-8, 4]], 8, -1)
-    iota("d16i", T.d16i[:], [[1, 64]], 128, -1)
 
-    quant("xqz", "zz", T.xq[:, 256:384], T.xs[:, 256:384], T.zz[:])
-    quant("rqz", "zz", T.rq[:, 106:234], T.rs[:, 106:234], T.zz[:])
+    ts("pu0", "pi", T.pi[:, 2:3], T.pi[:, 2:3], 3, Op.bitwise_and)
+    ts("pu1", "pi", T.pi[:, 3:4], T.pi[:, 3:4], 12, Op.bitwise_and)
+    ts("pj", "pi", T.pi[:, 0:2], T.pi[:, 0:2], 7, Op.bitwise_and)
     quant("rq2z", "zz", T.rq2[:, 22:150], T.rs2[:, 22:150], T.zz[:])
     for j in range(2):
         act("rt0", "zz", T.rt[:, 2 * j:2 * j + 2, :, :], T.zz[:, 0:336], more=j > 0)
@@ -183,77 +183,104 @@ def rank_program(g, core, T, topo):
         cs = slice(64 * h, 64 * h + 64)
         select("wt0", "ones w3z", T.w3[sl, 0, cs, 0], T.ones[sl, 0:64], [[1, 64]], Op.is_gt, 0.0, 0, -1, more=True)
         select("wt0", "ones w3z", T.w3[sl, 0, cs, 1], T.ones[sl, 0:64], [[-1, 64]], Op.is_ge, 0.0, 0, 1, more=True)
-    iotaf("phr", T.phr[:], [[1, 320]], 0, 0)
-    iotaf("ph512", T.ph512[:], [[512, 320]], 0, 0)
-    iotaf("lgr", T.lgr[:], [[1, 5], [5, 64]], 0, 0)
+    iotaf("phr", T.phr[:], [[32, 5], [160, 2], [1, 32]], 0, 0)
+    iotaf("lgr", T.lgr[:], [[160, 2], [1, 5], [5, 32]], 0, 0)
+    copy("pu2", "pu0", T.pf[:, 6:7], T.pi[:, 2:3])
+    ts("pu3", "pu1", T.pf[:, 7:8], T.pi[:, 3:4], -4.0, Op.mult)
+    ts("g0", "pj", T.pf[:, 0:2], T.pi[:, 0:2], 5.0, Op.mult)
+    ts("g1", "pj", T.pf[:, 2:4], T.pi[:, 0:2], -1.0, Op.mult)
     fill("pa2", T.pa2[:], 2.0)
     fill("zf", T.zf[:], 0.0)
     fill("tb0", T.tb[:, 50:54], 0.0)
-    fill("tb0", T.tb[:, 54:56], 1024 * U, more=True)
-    fill("pa2", T.pa2[:, 0:160:4], 0.0)
-    fill("abk", T.ab[:, 0:150:3], 1 / EPS)
+    ts("uo", "uf pu2 pu3", T.uo[:], T.uf[:], T.pf[:, 6:7], Op.add, T.pf[:, 7:8], Op.add)
     fill("dt0", T.dt3[:], 0.0)
+    fill("pa2", T.pa2[:, 0:160:4], 0.0)
+    ts("cti2", "cti", T.cti[:], T.cti[:], 63, Op.bitwise_and)
+    fill("abk", T.ab[:, :, 0:150:3], 1 / EPS)
+    quant("uq0", "ut", T.uq0[:], T.us0[:], T.ut[:])
     fill("dp0", T.dp[:], 0.0)
     fill("cd0_", T.cde[:], 1)
-    ts("hb0", "cii", T.hb[:, 0:160:4], T.ci[:], -0.4375, Op.add)
-    ts("pj", "pi", T.pi[:, 0:2], T.pi[:, 0:2], 7, Op.bitwise_and)
-    ts("cti2", "cti", T.cti[:], T.cti[:], 63, Op.bitwise_and)
-    ts("g0", "pj", T.pf[:, 0:2], T.pi[:, 0:2], 5.0, Op.mult)
-    ts("g1", "pj", T.pf[:, 2:4], T.pi[:, 0:2], -1.0, Op.mult)
-    ts("ct", "cti2", T.ct[:], T.cti[:], -U / 512, Op.mult, 81.8125 * U, Op.add)
-    ts("v0m", "v0i g0", T.tbb[:], T.val1[:], T.pf[:, 0:1], Op.not_equal)
-    ts("v0n", "v0i v0m", T.val1[:], T.val1[:], 64.4375, Op.add, U, Op.mult)
-    ts("c0a", "c0i g1", T.c0[:, 1, :], T.c0[:, 0, :], T.pf[:, 2:3], Op.is_equal, 128 * U, Op.mult)
-    tt("val1", "v0m v0n", T.val1[:], T.val1[:], T.tbb[:], Op.mult)
+    ts("v0m", "v0i g0", T.tbb[:, 10:50], T.val1[:, 10:50], T.pf[:, 0:1], Op.not_equal)
+    ts("v0m", "v0j g0", T.tbb[:, 0:10], T.sq[:, 0, 0:10], T.pf[:, 0:1], Op.not_equal, more=True)
+    do("v", "uq0 uo", "uq", lambda: V.tensor_copy(T.uq[:].bitcast(dt.uint32), T.uq0[:].bitcast(dt.uint32).indirect(T.uo[:])))
+    do("v", "uq0 uo", "uq", lambda: V.tensor_copy(T.us[:], T.us0[:].indirect(T.uo[:])), more=True)
+    quant("ptqz", "zz", T.ptq[:, 64:192], T.pts[:, 64:192], T.zz[:])
+    for a in (40, 208):
+        quant("dgqz", "zz", T.dgq[:, a:a + 128], T.dgs[:, a:a + 128], T.zz[:], more=True)
 
     for i in range(5):
         if i < 3:
-            copy("xt", "xin", T.xt[:, i, :, :], T.xin[:, :, 4 * i:4 * i + 4], more=True)
+            copy("xt0 xt1", "xin", T.xt[:, :, i, :, :], T.xin[:, :, 4 * i:4 * i + 4], more=True)
         else:
-            act("xt", "xin", T.xt[:, i, :, :], T.xin[:, :, 4 * i:4 * i + 4], more=True)
-    quant("uq", "ut", T.uq[:], T.us[:], T.ut[:])
-    quant("xq", "xt xqz", T.xq[:, 0:320], T.xs[:, 0:320], T.xt[:])
+            act("xt0 xt1", "xin", T.xt[:, :, i, :, :], T.xin[:, :, 4 * i:4 * i + 4], more=True)
+    do("y", "xin", "wq", lambda: Y.dma_start(T.wq[:].bitcast(dt.uint8), T.wc[:]), "dw", 16, more=True)
+    do("y", "", "wq", lambda: Y.dma_start(T.wsc[:], T.ws[:]), "dw", 16, more=True)
+    do("y", "", "vt", lambda: Y.dma_start(T.vt[:], T.v[:]), "dv", 16)
+    ts("ct", "cti2", T.ct[:], T.cti[:], -U / 512, Op.mult, 64.3125 * U, Op.add)
+    ts("v0n", "v0i v0m", T.val1[:], T.val1[:], 64.4375, Op.add, U, Op.mult)
+    ts("c0a", "c0i g1", T.c0[:, 1, :], T.c0[:, 0, :], T.pf[:, 2:3], Op.is_equal)
+    quant("xq0 xq1", "xt0 xt1", T.xq[:], T.xs[:], T.xt[:])
 
     def constants0():
-        ts("c0b", "c0a", T.c0[:, 0, 0:9], T.c0[:, 1, 0:9], 8.0, Op.mult)
+        tt("val1", "v0m v0n", T.val1[:], T.val1[:], T.tbb[:], Op.mult)
+        ts("c0b", "c0a", T.c0[:, 0, 0:9], T.c0[:, 1, 0:9], -1024 * U, Op.mult)
+        tt("c0c", "c0a ct", T.c0[:, 2, 0:8], T.c0[:, 1, 0:8], T.ct[:, 14:50:5], Op.mult)
+        fill("dg1", T.dt3[:, 1, 14:150:15], 1.0)
+        fill("pa16", T.pa16[:], 1.0)
+
+    def constants1():
+        tt("c0", "c0b c0c", T.c0[:, 0, 1:9], T.c0[:, 0, 1:9], T.c0[:, 2, 0:8], Op.add)
         ts("n60b", "n60", T.n60[:], T.n60[:], 63, Op.bitwise_and)
-        tt("c0c", "c0a c0b", T.c0[:, 0, 1:9], T.c0[:, 0, 1:9], T.c0[:, 1, 0:8], Op.subtract)
-        ts("ngm", "n60b", T.ngm[:], T.n60[:, 0:4], -U / 512, Op.mult, 102560.0 / 512 * U, Op.add)
-        tt("i20b", "n60b i20", T.i20[:], T.i20[:], T.n60[:, 0:20], Op.add)
-        ts("n5", "n60b", T.n5[:], T.n60[:, 0:4], 5.0, Op.mult, -1.0, Op.add)
-        ts("c0", "c0c", T.c0[:, 0, 8:9], T.c0[:, 0, 8:9], 128 * U, Op.add)
 
     def constants3():
-        for k, c in (("wat", 5 * U), ("wbt", -U / 64)):
+        for sl, c in ((lo, -U / 64), (up, 5 * U)):
             for a, w in ((0, 64), (64, 64), (128, 32)):
-                act(k, "wm wm0", T[k][:, a:a + w, :], T.wm[:, 0:w, :], c, more=a > 0)
-        act("wct", "zz", T.wct[:, 64:128, :], T.zz[:, 0:256])
+                act("wat", "wm", T.wat[sl, a:a + w, :], T.wm[lo, 0:w, :], c, more=True)
         for a, b, w in ((0, 0, 64), (128, 32, 32), (160, 0, 32)):
-            act("wct", "wm wm0", T.wct[:, a:a + w, :], T.wm[:, b:b + w, :], 5 * U, more=True)
+            act("wct", "wm wc0", T.wct[lo, a:a + w, :], T.wm[lo, b:b + w, :], 5 * U, more=True)
         for j in range(2):
             act("dg0", "zz", T.dg[:, j, :, :, :], T.zz[:], more=j > 0)
 
+    def scores(h, banks):
+        for j, k in enumerate(banks):
+            c = 160 * h + 32 * j
+            mm("ps%d" % k, "xq%d uq" % h, (ps[k][:, 0:128], T.xq[:, c:c + 128], T.xs[:, c:c + 128], T.uq[:], T.us[:]))
+
+    def bring(h, banks):
+        for i in range(5):
+            out = T.sc[32 * h:32 * h + 32, :, i, :]
+            if i < 3:
+                copy("sc%d" % h, "ps%d" % banks[0], out, ps[banks[0]][32 * i:32 * i + 32, 0:32], more=i > 0)
+            else:
+                act("sc%d" % h, "ps%d" % banks[1], out, ps[banks[1]][32 * i - 32:32 * i, 0:32], more=True)
+
     def constants2():
-        for b in range(4):
-            quant("e%d" % b, "et", T.eqc[:, 128 * b:128 * b + 128], T.eqs[:, 128 * b:128 * b + 128], T.et[:, 3 - b:515 - b])
-            yield
-            yield
-        ts("nr2", "nr", T.nr[:], T.nr[:], 63, Op.bitwise_and)
+        ts("ngm", "n60b", T.ngm[:, 0, :], T.n60[:, 0:4], -U / 512, Op.mult, 102560.0 / 512 * U, Op.add)
         yield
+        ts("n5", "n60b", T.inc[:, 0:4], T.n60[:, 0:4], 5.0, Op.mult, -160.0, Op.add)
         yield
+        fill("dg1", T.dt3[:, 1, 29:30], -7.0)
         yield
-        ts("jr2", "jr", T.jr[:], T.jr[:], 15, Op.bitwise_and)
+        fill("dg1", T.dt3[:, 1, 149:150], 64.0, more=True)
+        yield
+        fill("pa16", T.pa16[:, 0:64:16], 0.0)
         yield
         copy("ngf", "n60b", T.ngf[:], T.n60[:, 0:4])
         yield
         ts("nb60", "n60b", T.nb60[:], T.n60[:], 4, Op.logical_shift_right)
         yield
-        fill("pa16", T.pa16[:], 1.0)
-        yield
         ts("d16a", "d16i", T.d16i[:], T.d16i[:], 15, Op.bitwise_and)
         yield
+        for b in range(4):
+            quant("e%d" % b, "et", T.eqc[:, 128 * b:128 * b + 128], T.eqs[:, 128 * b:128 * b + 128], T.et[:, 3 - b:515 - b])
+            yield
+            yield
+        for j in range(2):
+            ts("nr2", "nr", T.nr[:, 32 * j:32 * j + 32, :], T.nr[:, 32 * j:32 * j + 32, :], 63, Op.bitwise_and, more=True)
+            yield
+            yield
+        ts("jr2", "jr", T.jr[:], T.jr[:], 15, Op.bitwise_and)
         yield
-        fill("pa16", T.pa16[:, 0:64:16], 0.0)
         yield
         for h, sl in halves:
             for e in range(4):
@@ -262,15 +289,8 @@ def rank_program(g, core, T, topo):
                 m = 16 * (7 - 4 * h - e)
                 ts("wt2", "jr2 w3z", T.w3[sl, 2, m:m + 16, e], T.jr[sl, :, e], 0, Op.is_equal, more=True)
                 yield
-        quant("ptqz", "zz", T.ptq[:, 64:192], T.pts[:, 64:192], T.zz[:])
-        yield
-        yield
         for j in range(3):
             quant("qwt%d" % j, "wt%d" % j, T.cq3[:, 128 * j:128 * j + 128], T.cs3[:, 128 * j:128 * j + 128], T.w3[:, j, :, :])
-            yield
-            yield
-        for a in (40, 208):
-            quant("dgqz", "zz", T.dgq[:, a:a + 128], T.dgs[:, a:a + 128], T.zz[:], more=True)
             yield
             yield
         for nb in range(4):
@@ -281,10 +301,9 @@ def rank_program(g, core, T, topo):
         ts("d16c", "d16a", T.d16[:, 1, :], T.d16i[:], 1, Op.is_equal, LOW, Op.mult)
         yield
         ts("cb", "d16a", T.pf[:, 4:5], T.d16i[:, 15:16], 0, Op.not_equal, LOW / 512, Op.mult)
-        yield
+
+    def constants4():
         tt("d16", "d16b d16c", T.d16[:, 0, :], T.d16[:, 0, :], T.d16[:, 1, :], Op.subtract)
-        yield
-        yield
         ts("cb2", "cb", T.pf[:, 5:6], T.pf[:, 4:5], -0.499, Op.add)
 
     fill("ne0", T.ne[:, :, 0:64:16], 0.0)
@@ -303,150 +322,166 @@ def rank_program(g, core, T, topo):
 
     for t in range(3):
         final = t == 2
-        for i in range(5):
-            mm("ps%d" % i, "xq uq", (ps[i][:, 0:128], T.xq[:, 64 * i:64 * i + 128], T.xs[:, 64 * i:64 * i + 128], T.uq[:], T.us[:]))
+        if t == 0:
+            scores(1, (4, 5))
+        scores(0, (6, 7))
         if t == 0:
             constants0()
-        for i in range(5):
-            if i % 2:
-                act("sc", "ps%d" % i, T.sc[:, :, i, :], ps[i][:, 0:32], more=i > 0)
-            else:
-                copy("sc", "ps%d" % i, T.sc[:, :, i, :], ps[i][:, 0:32], more=i > 0)
+        bring(1, (4, 5))
+        bring(0, (6, 7))
 
         def unpack():
             for b in range(4):
-                mm("ps%d" % b, "xq e%d" % b, (ps[b][:, 0:320], T.eqc[:, 128 * b:128 * b + 128], T.eqs[:, 128 * b:128 * b + 128], T.xq[:, 0:320], T.xs[:, 0:320]))
+                mm("ps%d" % b, "xq0 xq1 e%d" % b, (ps[b][:, 0:320], T.eqc[:, 128 * b:128 * b + 128], T.eqs[:, 128 * b:128 * b + 128], T.xq[:, 0:320], T.xs[:, 0:320]))
                 act("tp", "ps%d" % b, T.tp[:, 320 * b:320 * b + 320], ps[b][:, 0:320], 0.5, more=b > 0)
 
         if t == 0:
             constants3()
         else:
             unpack()
-        key = lambda a, b: T.sc[:, :, a:b, 3]
+        key = lambda a, b: T.sc[lo, :, a:b, 3]
         for s in range(1, 5):
-            tt("cm", "sc", T.cm[:, s - 1, :, 0:5 - s], key(s, 5), key(0, 5 - s), Op.is_gt, more=True)
-            tt("cm", "sc", T.cm[:, s - 1, :, 5 - s:5], key(0, s), key(5 - s, 5), Op.is_ge, more=True)
-        for b in range(2):
-            ts("hb", "sc hb0", T.hb[:, 1 + b:160:4], T.sc[:, :, :, b], 0.0, Op.is_gt, more=b > 0)
-        tt("a2", "cm", T.a2[:], T.cm[:, 0:2, :, :], T.cm[:, 2:4, :, :], Op.add)
-        ts("hb", "sc hb0", T.hb[:, 3:160:4], T.sc[:, :, :, 2], 0.0, Op.is_gt, more=True)
-        fill("abb", T.ab[:, 2:150:3], EPS)
-        tt("rk", "a2", T.rk[:], T.a2[:, 0, :], T.a2[:, 1, :], Op.add)
-        scan("pay", "pa2 hb", T.pay[:], T.pa2[:], T.hb[:])
-        for r in range(5):
-            ts("eqr%d" % r, "rk", T.eqr[:, r, :], T.rk[:], 4.0 - r, Op.is_equal, 64.0, Op.mult)
-        for r in range(5):
-            scan("prb", "eqr%d pay" % r, T.prb[:, :, r], T.eqr[:, r, :], T.pay[:, 3:160:4], more=True, ops=LATCH)
+            tt("cm", "sc0 sc1", T.cm[lo, s - 1, :, 0:5 - s], key(s, 5), key(0, 5 - s), Op.is_gt, more=True)
+            tt("cm", "sc0 sc1", T.cm[lo, s - 1, :, 5 - s:5], key(0, s), key(5 - s, 5), Op.is_ge, more=True)
+        for b in range(3):
+            ts("hb", "sc0 sc1 hb0", T.hb[lo, 1 + b:160:4], T.sc[lo, :, :, b], 0.0, Op.is_gt, more=b > 0)
+        tt("a2", "cm", T.a2[lo], T.cm[lo, 0:2, :, :], T.cm[lo, 2:4, :, :], Op.add)
+        fill("abb1", T.ab[:, 1, 2:150:3], EPS)
+        if t == 0:
+            constants1()
+        scan("pay", "pa2 hb pay0", T.pay[lo, 0:160], T.pa2[lo], T.hb[lo])
+        for j in range(2):
+            tt("rk", "a2", T.rk[lo, 40 * j:40 * j + 40], T.a2[lo, 0, :], T.a2[lo, 1, :], Op.add, more=j > 0)
 
         def sym(i):
-            ts("rt2", "pay rt20", T.rt2[:, 0:2, 16 * i:16 * i + 20:5], T.pay[:, 3 + 4 * i:160:20], 3.5 - 8 * i, Op.add, more=i > 0)
+            ts("rt2", "pay rt20", T.rt2[lo, 0:2, 16 * i:16 * i + 20:5], T.pay[lo, 3 + 4 * i:160:20], -8.0 * i, Op.add, more=i > 0)
 
         if t == 0:
-            quant("wb", "wbt", T.wbq[:], T.wbs[:], T.wbt[:])
-        sym(0)
-        sym(1)
-        hi, lw = T.rt[:, 0:2, 0:4, 0:20:4], T.rt[:, 2:4, 0:4, 0:20:4]
-        ts("rth", "prb rt0", hi, T.prb[:, 4:40:5, :], M1 * 8, Op.add, M1 * 8, Op.subtract)
+            tt("i20b", "n60b i20", T.i20[:], T.i20[:], T.n60[:, 0:20], Op.add)
+        for i in range(3):
+            sym(i)
+        for r in range(5):
+            ts("eqr%d" % r, "rk", T.eqr[lo, r, :], T.rk[lo], 4.0 - r, Op.is_equal, 64.0, Op.mult)
+        for r in range(5):
+            scan("prb", "eqr%d pay" % r, T.prb[lo, :, r], T.eqr[lo, r, :], T.pay[lo, 3:320:4], more=True, ops=LATCH)
+
         if t == 0:
             quant("wa", "wat", T.waq[:], T.was[:], T.wat[:])
-        sym(2)
         sym(3)
-        tt("rtl", "prb rth", lw, T.prb[:, 4:40:5, :], hi, Op.subtract)
         sym(4)
-        quant("rq", "rqz rth rtl", T.rq[:, 0:168], T.rs[:, 0:168], T.rt[:])
-        mm("ps5", "wa wb rq rqz", *[(ps[5][:, 0:128], wq[:, w:w + 128], wsc[:, w:w + 128], T.rq[:, c:c + 128], T.rs[:, c:c + 128])
-                                    for wq, wsc, w, c in ((T.wbq, T.wbs, 0, 0), (T.wbq, T.wbs, 32, 22), (T.waq, T.was, 0, 84), (T.waq, T.was, 32, 106))])
+        copy("rth", "prb rt0", T.rt[lo, 0:2, 0:4, 0:20:4], T.prb[lo, 44:80:5, :])
+        tt("rtl", "prb rt0", T.rt[up, 0:2, 0:4, 0:20:4], T.prb[lo, 4:40:5, :], T.prb[lo, 44:80:5, :], Op.subtract)
+        fillers(2)
+        quant("rq", "rth rtl", T.rq[:], T.rs[:], T.rt[:])
+        mm("ps5", "wa rq", *[(ps[5][:, 0:128], T.waq[:, w:w + 128], T.was[:, w:w + 128], T.rq[:, c:c + 128], T.rs[:, c:c + 128])
+                             for w, c in ((0, 0), (32, 22))])
         if t == 0:
             quant("wc", "wct", T.wcq[:], T.wcs[:], T.wct[:])
             ts("ctp", "i20b", T.ctp[:], T.i20[:], -U / 512, Op.mult, 64.3125 * U, Op.add)
         quant("rq2", "rq2z rt2", T.rq2[:, 0:132], T.rs2[:, 0:132], T.rt2[:])
         mm("ps6", "wc rq2 rq2z", *[(ps[6][:, 0:128], T.wcq[:, w:w + 128], T.wcs[:, w:w + 128], T.rq2[:, c:c + 128], T.rs2[:, c:c + 128])
                                    for w, c in ((0, 0), (64, 22))])
+        fillers(4)
+        scan("so0", "c0 ps5", T.so[:, 0, 141:150], T.c0[:, 0, 0:9], ps[5][:, 4:45:5], ops=(Op.add, Op.max))
         tt("tb1", "ps5 ct", T.tb[:, 10:50], ps[5][:, 0:40], T.ct[:, 10:50], Op.add)
         tt("tb2", "ps5 ct", T.tb[:, 0:10], ps[5][:, 30:40], T.ct[:, 0:10], Op.add)
-        fillers(1)
-        scan("so0", "c0 tb1 tb0", T.so[:, 0, 141:150], T.c0[:, 0, 0:9], T.tb[:, 14:55:5], ops=LATCH)
-        tt("dtb", "tb1 tb2 tb0 dt0", T.dt3[:, 2:150:3], T.tb[:, 0:50], T.tb[:, 1:51], Op.subtract)
-        tt("tbm", "val1 tb1 tb2", T.tbb[:], T.val1[:], T.tb[:, 0:50], Op.is_ge)
-        tt("tbp", "ps6 ctp", T.tbp[:], ps[6][:, 0:20], T.ctp[:], Op.add)
-
         def cd(n):
-            ts("cd%d" % n, "so%d ngm cd0_" % n, T.cde[:, 14 - n:64:16], T.ngm[:], T.so[:, n, 149:150], Op.subtract, 512 / U, Op.mult)
+            ts("cd%d" % n, "so%d ngm cd0_" % n, T.cde[:, 14 - n:64:16], T.ngm[:, 0, :], T.so[:, n, 149:150], Op.subtract, 512 / U, Op.mult)
+
+        def drew(n):
+            for k, c in (("po0", 4), ("po1", 1)):
+                ts(k, "gc0 gc1 sg%d" % n, T.pt[:, 52 - 4 * n + c:256:64], T.ngm[:, 2, :], T.so[:, 3 + n, 149:150], Op.is_equal, more=n > 11)
 
         def marks(n):
             s, so, a = T.so[:, n, 149:150], "so%d" % n, n % 2
             if 0 < n < 12:
-                j = 10 if n < 3 else 5 if n < 8 else 0
-                act("sq%d" % a, "tb1 tb2 " + so, T.sq[:, a, j:50], T.tb[:, j:50], -1.0, bias=s, func=AF.Square)
+                act("sq%d" % a, "tb1 tb2 " + so, T.sq[:, a, :], T.tb[:, 0:50], -1.0, bias=s, func=AF.Square)
             if n == 0:
                 act("dp", "zf dp0 " + so, T.dp[:, 13:64:16], T.zf[:], bias=s)
             else:
                 act("dp", "tt%d %s" % (1 - a, so), T.dp[:, 13 - n:64:16], T.tt4[:, 1 - a, :], -1.0, bias=s, more=True)
             if n < 13:
-                act("sqp%d" % a, "tbp " + so, T.sqp[:, a, :], T.tbp[:], -1.0, bias=s, func=AF.Square)
+                act("sqp%d" % (n % 3), "tbp " + so, T.sqp[:, n % 3, :], T.tbp[:], -1.0, bias=s, func=AF.Square)
                 act("tt%d" % a, "zf " + so, T.tt4[:, a, :], T.zf[:], bias=s)
-                act("ne", "sqp%d ne0" % a, T.ne[:, :, 14 - n:64:16], T.sqp[:, a, :], func=AF.Sign, more=n > 0)
+                act("ne", "sqp%d ne0" % (n % 3), T.ne[:, :, 14 - n:64:16], T.sqp[:, n % 3, :], func=AF.Sign, more=n > 0)
 
         def undrawn(n):
             a = n % 2
             if n == 0:
                 ts("und0", "sqp0", T.und[:, 0, :], T.sqp[:, 0, :], 1.0, Op.min)
             else:
-                tt("und%d" % a, "und%d sqp%d" % (1 - a, a), T.und[:, a, :], T.und[:, 1 - a, :], T.sqp[:, a, :], Op.min)
+                tt("und%d" % a, "und%d sqp%d" % (1 - a, n % 3), T.und[:, a, :], T.und[:, 1 - a, :], T.sqp[:, n % 3, :], Op.min)
 
         for n in range(1, 14):
             s, so = T.so[:, n - 1, 149:150], "so%d" % (n - 1)
             j = 10 if n < 5 else 5 if n < 10 else 0
             vk, vv = ("val1", T.val1) if n < 3 else ("vl%d" % (n % 2), T.val[:, n % 2, :])
-            marks(n - 1)
-            ts("aba", vk + " abk " + so, T.ab[:, 3 * j + 1:150:3], T.val1[:, j:50] if n < 3 else T.val[:, n % 2, j:50], s, Op.is_lt, EPS, Op.add)
+            if n > 1:
+                marks(n - 1)
+            w = n % 2
+            ts("aba%d" % w, vk + " abk " + so, T.ab[:, w, 3 * j + 1:150:3], T.val1[:, j:50] if n < 3 else T.val[:, n % 2, j:50], s, Op.is_lt, EPS, Op.add)
+            if n == 1:
+                tt("dtb", "tb1 tb2 tb0 dt0", T.dt3[:, 0, 2:150:3], T.tb[:, 0:50], T.tb[:, 1:51], Op.subtract)
+                tt("tbm", "val1 tb1 tb2", T.tbb[:], T.val1[:], T.tb[:, 0:50], Op.is_ge)
+                tt("tbp", "ps6 ctp", T.tbp[:], ps[6][:, 0:20], T.ctp[:], Op.add)
+                marks(0)
+            else:
+                ts("abb%d" % w, "tbb " + so, T.ab[:, w, 3 * j + 2:150:3], T.tbb[:, j:50], s, Op.is_equal, EPS, Op.add)
+            if 2 <= n < 11:
+                fillers(2)
+            if n == 11:
+                cd(10)
+            if n == 12:
+                ts("po0", "ca pt0", T.pt[:, 0:256:4], T.ca[:], 0, Op.is_equal)
+                ts("po1", "ca pt0", T.pt[:, 1:252:4], T.ca[:, 1:64], 0, Op.is_equal)
+            if 2 <= n < 13:
+                old = T.val1[:] if n < 3 else T.val[:, n % 2, :]
+                tt("vl%d" % ((n + 1) % 2), vk + " sq%d" % ((n - 1) % 2), T.val[:, (n + 1) % 2, :], old, T.sq[:, (n - 1) % 2, :], Op.min)
+            if n == 13:
+                drew(12)
+            group = lambda: scan("sg%d" % n, "aba%d abb%d dg1" % (w, w), T.so[:, 3 + n, :], T.ab[:, w, :], T.dt3[:, 1, :])
+            if n == 13:
+                group()
+                scan("pe", "pa16 po0", T.pe[:], T.pa16[:], T.pt[:, 0:256:4])
+            scan("so%d" % n, "aba%d abb%d dtb" % (w, w), T.so[:, n, 3 * j:150], T.ab[:, w, 3 * j:150], T.dt3[:, 0, 3 * j:150])
             if n == 1:
                 tt("tbb", "tbm", T.tbb[:], T.tbb[:], T.tb[:, 0:50], Op.mult)
-            else:
-                ts("abb", "tbb " + so, T.ab[:, 3 * j + 2:150:3], T.tbb[:, j:50], s, Op.is_equal, EPS, Op.add)
-            if 2 <= n < 13:
-                j2 = 10 if n < 4 else 5 if n < 9 else 0
-                old = T.val1[:, j2:50] if n < 3 else T.val[:, n % 2, j2:50]
-                tt("vl%d" % ((n + 1) % 2), vk + " sq%d" % ((n - 1) % 2), T.val[:, (n + 1) % 2, j2:50], old, T.sq[:, (n - 1) % 2, j2:50], Op.min)
-            elif n == 13:
-                cd(12)
-            scan("so%d" % n, "aba abb dtb", T.so[:, n, 3 * j:150], T.ab[:, 3 * j:150], T.dt3[:, 3 * j:150])
-            if n in (3, 8):
-                j2, a = 5 if n == 3 else 0, (n + 1) % 2
-                ts("vl%d" % a, "vl%d" % a, T.val[:, a, j2:j2 + 5], T.val[:, a, 40 + j2:45 + j2], 2.0, Op.mult, more=True)
-            if n < 13:
+            if n == 11:
+                ts("ca", " ".join("cd%d" % m for m in range(11)), T.ca[:], T.cde[:], 63, Op.bitwise_and)
+            if n in (11, 12):
+                group()
+            if n < 11:
                 cd(n - 1)
-            if n >= 2:
-                undrawn(n - 2)
-            fillers(5)
+            if n == 12:
+                drew(11)
+            if 2 <= n < 12 or n == 13:
+                undrawn(n - 2 if n < 12 else 10)
+            if n < 11:
+                fillers(3)
             if t == 0 and n == 5:
                 unpack()
-        fillers(99)
+            if t == 0 and n == 10:
+                fillers(99)
+                act("ph512", "phr", T.ph512[:], T.phr[:], 512.0)
         s = T.so[:, 13, 149:150]
         marks(13)
-        ts("ca", " ".join("cd%d" % n for n in range(13)), T.ca[:], T.cde[:], 63, Op.bitwise_and)
-        ts("c13", "so13 ngm", T.c13[:], T.ngm[:], s, Op.subtract, 512 / U, Op.mult)
+        need("v", "v", reads["po0"]["v"])
+        drew(13)
         ts("ne13", "so13 tbp ne0", T.ne[:, :, 1:64:16], T.tbp[:], s, Op.not_equal)
-        undrawn(12)
-        ts("po0", "ca pt0", T.pt[:, 0:256:4], T.ca[:], 0, Op.is_equal)
-        ts("c13", "c13", T.c13[:], T.c13[:], 63, Op.bitwise_and)
-        ts("po1", "ca pt0", T.pt[:, 1:252:4], T.ca[:, 1:64], 0, Op.is_equal)
-        scan("pe", "pa16 po0", T.pe[:], T.pa16[:], T.pt[:, 0:256:4])
+        for e in range(4):
+            ts("po3", "sg13 pe pt0", T.pt[:, 256 + 65 * e:257 + 65 * e], T.so[:, 16, 149:150], T.ngm[:, 2, e:e + 1], Op.is_equal, T.pe[:, 16 * e + 15:16 * e + 16], Op.add, more=e > 0)
 
         def before(i):
             scan("uopp", "ne ne13 dp", T.uop[:, 0, i, :], T.ne[:, i, :], T.dp[:], more=i > 0)
 
-        before(0)
-        before(1)
-        ts("po0", "c13", T.pt[:, 4:256:64], T.c13[:], 0, Op.is_equal)
-        ts("po1", "c13", T.pt[:, 1:256:64], T.c13[:], 0, Op.is_equal)
-        for e in range(4):
-            ts("po3", "c13 pe pt0", T.pt[:, 256 + 65 * e:257 + 65 * e], T.c13[:, e:e + 1], 0, Op.is_equal, T.pe[:, 16 * e + 15:16 * e + 16], Op.add, more=e > 0)
-        before(2)
-        before(3)
+        undrawn(11)
+        for i in range(3):
+            before(i)
         quant("ptq", "po0 po1 po3 ptqz", T.ptq[:, 0:128], T.pts[:, 0:128], T.pt[:])
         mm("ps4", "ptq ptqz qwt0 qwt1", (ps[4][:, 0:128], *W3(0), T.ptq[:, 0:128], T.pts[:, 0:128]),
            (ps[4][:, 0:128], *W3(1), T.ptq[:, 64:192], T.pts[:, 64:192]))
+        undrawn(12)
+        before(3)
         before(4)
         tt("fl und1", "und0 ne13", T.und[:, 1, :], T.und[:, 0, :], T.ne[:, :, 1:64:16], Op.mult)
 
@@ -455,9 +490,9 @@ def rank_program(g, core, T, topo):
                 j = int(x == "q")
                 ts("di" + x, "v2" + x, T.dgi[:, 3 * j + d, :], T.v2[:, j, :], m, Op.bitwise_and, more=d > 0)
 
-        def spread(x):
+        def spread(x, blocks=range(4)):
             j, nd = (1, 2) if x == "q" else (0, 3)
-            for nb in range(4):
+            for nb in blocks:
                 tt("dg" + x, "di%s msk dg0" % x, T.dg[:, j, 0:5 * nd, nb, :], T.dgi[:, 3 * j:3 * j + nd, :], T.msk[:, nb, 0:20 * nd], Op.mult, more=nb > 0)
 
         def form(x, k):
@@ -468,19 +503,22 @@ def rank_program(g, core, T, topo):
 
         ts("v2p", "uopp", T.v2[:, 0, :], T.uop[:, 0, :, 13:64:16], -512 / U, Op.mult, 102560.0, Op.add)
         for e in range(4):
-            scan("inc", "pa16 fl n5", T.inc[:, e:20:4], T.pa16[:, 1:6], T.und[:, 1, e:20:4], more=e > 0, initial=T.n5[:, e:e + 1])
+            scan("inc", "pa16 fl n5", T.inc[:, 4 + e:24:4], T.pa16[:, 1:6], T.und[:, 1, e:20:4], more=e > 0, initial=T.inc[:, e:e + 1])
         digits("p")
-        tt("pr0", "fl inc", T.pr[:], T.und[:, 1, :], T.inc[:], Op.mult)
+        ts("pr0", "fl", T.pr[:], T.und[:, 1, :], 1024.0, Op.mult, -160.0, Op.add)
         for i in range(5):
             scan("uopq", "ne ne13 ps4", T.uop[:, 1, i, :], T.ne[:, i, :], ps[4][:, 0:64], more=i > 0)
-        ts("pr", "pr0", T.pr[:], T.pr[:], -160.0, Op.add)
-        spread("p")
+        tt("pr", "pr0 inc", T.pr[:], T.pr[:], T.inc[:, 0:20], Op.min)
+        spread("p", (0, 1))
         tt("v2q", "uopq pr", T.v2[:, 1, :], T.uop[:, 1, :, 15:64:16], T.pr[:], Op.add)
-        form("p", 5)
+        spread("p", (2, 3))
         digits("q")
+        form("p", 5)
         spread("q")
         form("q", 6)
         copy("ofp", "ps5", T.ofp[:], ps[5][:, 0:20])
+        if t == 0:
+            constants4()
         tt("pk", "ofp phr ph512", T.pk[:], T.phr[:].indirect(T.ofp[:]), T.ph512[:], Op.add)
         ts("ofq", "ps6", T.ofq[:], ps[6][:, 0:20], 160.0, Op.add)
         do("v", "ofq pk", "row", lambda: V.tensor_copy(T.row[:].indirect(T.ofq[:]), T.pk[:]))
@@ -499,10 +537,12 @@ def rank_program(g, core, T, topo):
             o = slice(10 * h, 10 * h + 10)
             for b in range(4):
                 act("at%d%d" % (h, b), "offa%d tp" % (0 if final else h), T.at[:, 640 * h + b:640 * h + 640:4], T.tp[:, 320 * b:320 * b + 320].indirect(T.offa[:, o]))
-            for b in range(4):
+
+        def blend(h, planes):
+            o = slice(10 * h, 10 * h + 10)
+            for b in planes:
                 cs = slice(640 * h + b, 640 * h + 640, 4)
                 tt("zt%d" % h, "offb tp at%d%d" % (h, b), T.zt[:, cs], T.tp[:, 320 * b:320 * b + 320].indirect(T.offb[:, o]), T.at[:, cs], Op.add, more=b > 0)
-            return slice(640 * h, 640 * h + 640)
 
         def kept(h):
             cs = slice(640 * h, 640 * h + 640)
@@ -513,14 +553,17 @@ def rank_program(g, core, T, topo):
 
         def finish(h, b, k):
             tt("tm%d%d" % (h, b), "ps%d ak%d" % (k, h), T.tm[:, 4 * h + b, :], ps[k][:, 0:160], T.ak[:, 640 * h + b:640 * h + 640:4], Op.add)
-            if final:
-                act("xl%d" % h, "tm%d%d" % (h, b), T.xl[:, 640 * h + b:640 * h + 640:4], T.tm[:, 4 * h + b, :], 2.0 ** -11, more=b > 0)
-            else:
-                act("xt", "tm%d%d" % (h, b), T.xt[:, :, 32 * h:32 * h + 32, b], T.tm[:, 4 * h + b, :], 2.0 ** -11, more=h == 0 or b > 0)
+            act("xt%d" % h, "tm%d%d" % (h, b), T.xt[:, h, :, :, b], T.tm[:, 4 * h + b, :], 2.0 ** -11, more=b > 0)
+
+        def state(h):
+            quant("xq%d" % h, "xt%d" % h, T.xq[:, 160 * h:160 * h + 160], T.xs[:, 160 * h:160 * h + 160], T.xt[:, h, :, :, :])
 
         rc = slice(160 * t, 160 * t + 160)
-        cs = picks(0)
-        quant("send%d" % t, "zt0", T.sendc[:, rc], T.sendp[:, rc], T.zt[:, cs])
+        picks(0)
+        picks(1)
+        blend(0, range(4))
+        blend(1, [0])
+        quant("send%d" % t, "zt0", T.sendc[:, rc], T.sendp[:, rc], T.zt[:, 0:640])
         dst = partner_of(t)
         rid, pid, _ = topo.addr(dst)
         pre("p", "send%d" % t, "")
@@ -528,10 +571,12 @@ def rank_program(g, core, T, topo):
             g.remote_dma(a, b, T.sem["arr%d" % t], T.sem["snd%d" % t], pid, rid, topo.mask(core, dst))
         eng = 2 * len(topo.engines(core, dst))
         last["land%d" % t] = {"arr%d" % t: eng}
-        cs = picks(1)
+        blend(1, [1, 2, 3])
         kept(1)
         kept(0)
-        quant("stay", "zt1", T.lq[:, 0:160], T.lsc[:, 0:160], T.zt[:, cs])
+        if final:
+            act("pk", "lgr offa0", T.pk[:], T.lgr[:].indirect(T.offa[:]))
+        quant("stay", "zt1", T.lq[:, 0:160], T.lsc[:, 0:160], T.zt[:, 640:1280])
         for b in range(4):
             new(1, b, 4 + b, ("stay", T.lq[:, 0:160], T.lsc[:, 0:160]))
         if t == 0:
@@ -539,28 +584,28 @@ def rank_program(g, core, T, topo):
         for b in range(4):
             finish(1, b, 4 + b)
         if final:
-            do("v", "ofq lgr", "pk", lambda: V.tensor_copy(T.pk[:].indirect(T.ofq[:]), T.lgr[:]))
             do("y", "pk", "", lambda: Y.dma_start(T.oq[:], T.pk[0:128:16, :]), "fin", 16)
-            quant("lq1", "xl1", T.lq[:, 160:320], T.lsc[:, 160:320], T.xl[:, 640:1280])
-            mm("ps4", "lq1 vq", (ps[4][:, 0:160], T.vq[:], T.vs[:], T.lq[:, 160:320], T.lsc[:, 160:320]))
-            do("y", "lq1", "", lambda: Y.dma_start(T.oc[:, 640:1280], T.lq[:, 160:320].bitcast(dt.uint8)), "fin", 16)
-            act("yb1 row", "ps4", T.row[:, 160:320], ps[4][:, 0:160])
-            do("y", "yb1", "", lambda: Y.dma_start(T.y[:, 160:320], T.row[:, 160:320]), "fin", 16)
         for b in range(4):
             new(0, b, b, ("land%d" % t, T.landc[:, rc], T.landp[:, rc]))
         for b in range(4):
             finish(0, b, b)
         need("p", "snd%d" % t, eng)
-        if not final:
-            quant("xq", "xt xqz", T.xq[:, 0:320], T.xs[:, 0:320], T.xt[:])
+        state(1)
+        if final:
+            mm("ps4", "xq1 vq", (ps[4][:, 0:160], T.vq[:], T.vs[:], T.xq[:, 160:320], T.xs[:, 160:320]))
+            do("y", "xq1", "", lambda: Y.dma_start(T.oc[:, 640:1280], T.xq[:, 160:320].bitcast(dt.uint8)), "fin", 16)
+            act("yb1 row", "ps4", T.row[:, 160:320], ps[4][:, 0:160])
+            do("y", "yb1", "", lambda: Y.dma_start(T.y[:, 160:320], T.row[:, 160:320]), "fin", 16)
+        else:
+            scores(1, (4, 5))
+        state(0)
 
-    quant("lq0 stay", "xl0", T.lq[:, 0:160], T.lsc[:, 0:160], T.xl[:, 0:640])
-    mm("ps5", "lq0 vq", (ps[5][:, 0:160], T.vq[:], T.vs[:], T.lq[:, 0:160], T.lsc[:, 0:160]))
-    do("y", "lq0", "", lambda: Y.dma_start(T.oc[:, 0:640], T.lq[:, 0:160].bitcast(dt.uint8)), "fin", 16)
+    mm("ps5", "xq0 vq", (ps[5][:, 0:160], T.vq[:], T.vs[:], T.xq[:, 0:160], T.xs[:, 0:160]))
+    do("y", "xq0", "", lambda: Y.dma_start(T.oc[:, 0:640], T.xq[:, 0:160].bitcast(dt.uint8)), "fin", 16)
     act("yb0", "ps5", T.row[:, 0:160], ps[5][:, 0:160])
     do("s", "yb0", "", lambda: S.dma_start(T.y[:, 0:160], T.row[:, 0:160]), "fin", 16)
     for k in range(4):
-        do("y", "lq0 lq1", "", lambda: Y.dma_start(T.osc[4 * k:4 * k + 4, :], T.lsc[32 * k:32 * k + 4, :]), "fin", 16)
+        do("y", "xq0 xq1", "", lambda: Y.dma_start(T.osc[4 * k:4 * k + 4, :], T.xs[32 * k:32 * k + 4, :]), "fin", 16)
     need("y", "fin", count["fin"])
     for k in ("v", "s", "t", "p"):
         need("y", k, count[k])

@@ -16,36 +16,37 @@ SCRATCH = {
     "wq": _sb(C8, 512), "wsc": _sb(U8, 512), "lq": _sb(C8, 160), "lsc": _sb(U8, 160),
     "sc": _sb(F, 8, 5, 4), "cm": _sb(B, 4, 8, 5), "a2": _sb(B, 2, 40), "hb": _sb(B, 160), "rk": _sb(B, 80), "pay": _sb(B, 320),
     "eqr": _sb(B, 5, 80), "prb": _sb(F, 80, 5), "rt": _sb(B, 4, 8, 21), "rq": _sb(C8, 168), "rs": _sb(U8, 168),
-    "rt2": _sb(B, 6, 88), "rq2": _sb(C8, 150), "rs2": _sb(U8, 150),
-    "tb": _sb(F, 56), "tbb": _sb(F, 50), "val": _sb(F, 2, 50), "sq": _sb(F, 2, 50), "ab": _sb(F, 2, 150), "dt3": _sb(F, 2, 150),
+    "rt2": _sb(B, 7, 88), "rq2": _sb(C8, 154), "rs2": _sb(U8, 154),
+    "tb": _sb(F, 56), "tbb": _sb(F, 50), "val": _sb(B, 2, 50), "sq": _sb(B, 2, 50), "ab": _sb(F, 2, 150), "dt3": _sb(F, 2, 150),
     "so": _sb(F, 17, 150), "tbp": _sb(F, 20), "sqp": _sb(F, 3, 20), "und": _sb(F, 2, 20), "tt4": _sb(F, 2, 4),
     "cde": _sb(I, 64), "ca": _sb(I, 64), "pe": _sb(F, 64), "pt": _sb(B, 512),
     "ptq": _sb(C8, 192), "pts": _sb(U8, 192), "ne": _sb(F, 5, 64), "dp": _sb(F, 64), "uop": _sb(F, 2, 5, 64),
-    "inc": _sb(F, 24), "pr": _sb(F, 20), "v2": _sb(I, 2, 20), "dgi": _sb(I, 5, 20), "dg": _sb(B, 2, 32, 4, 4),
-    "dgq": _sb(C8, 336), "dgs": _sb(U8, 336), "ofp": _sb(U16, 20), "ofq": _sb(U16, 20), "pk": _sb(F, 320), "row": _sb(F, 320),
-    "s5": _sb(F, 5, 64), "xi": _sb(I, 5, 4), "xj": _sb(I, 20), "offa": _sb(U16, 20), "offb": _sb(U16, 20),
+    "inc": _sb(F, 24), "pr": _sb(F, 20), "v2": _sb(I, 2, 20), "dgi": _sb(I, 5, 20), "dgp": _sb(B, 17, 5, 2, 4), "dgr": _sb(B, 15, 5, 2, 4),
+    "dgq": _sb(C8, 320), "dgs": _sb(U8, 320), "ofp": _sb(U16, 20), "ofq": _sb(U16, 20), "pk": _sb(F, 320), "row": _sb(F, 320),
+    "s5": _sb(F, 5, 64), "offa": _sb(U16, 20), "tq": _sb(B, 1280), "tw": _sb(B, 640),
     "tp": _sb(B, 1280), "zt": _sb(B, 1280), "at": _sb(B, 1280), "ak": _sb(B, 1280), "tm": _sb(F, 8, 160),
-    "zz": _sb(B, 512), "zf": _sb(F, 4), "wm": _sb(B, 64, 4), "wat": _sb(B, 160, 4), "wct": _sb(B, 192, 4),
-    "waq": _sb(C8, 160), "was": _sb(U8, 160), "wcq": _sb(C8, 192), "wcs": _sb(U8, 192),
+    "zz": _sb(B, 512), "zf": _sb(F, 4), "wm": _sb(B, 64, 4), "wat": _sb(B, 160, 4), "i16": _sb(B, 64),
+    "waq": _sb(C8, 160), "was": _sb(U8, 160),
     "et": _sb(B, 516), "ones": _sb(B, 128), "eqc": _sb(C8, 512), "eqs": _sb(U8, 512),
     "w3": _sb(B, 3, 128, 4), "cq3": _sb(C8, 384), "cs3": _sb(U8, 384),
-    "nr": _sb(I, 64, 4), "jr": _sb(I, 16, 4), "n60": _sb(I, 60), "nb60": _sb(I, 60), "msk": _sb(F, 4, 60), "ngf": _sb(F, 4),
-    "i20": _sb(I, 20), "ctp": _sb(F, 20), "ngm": _sb(F, 3, 4),
-    "cti": _sb(I, 50), "ct": _sb(F, 50), "val1": _sb(F, 50), "pi": _sb(I, 8), "pf": _sb(F, 10), "c0": _sb(F, 3, 10),
+    "n60": _sb(I, 60), "nb60": _sb(I, 60), "msk": _sb(F, 4, 60),
+    "i20": _sb(I, 20), "g20": _sb(I, 20), "ctp": _sb(F, 20), "ngm": _sb(F, 3, 4),
+    "cti": _sb(I, 50), "ct": _sb(F, 50), "val1": _sb(B, 50), "pi": _sb(I, 8), "pf": _sb(F, 10), "c0": _sb(F, 3, 10),
     "pa2": _sb(B, 160), "pa16": _sb(F, 64), "d16i": _sb(I, 64), "d16": _sb(F, 2, 64),
-    "phr": _sb(F, 320), "ph512": _sb(F, 320), "lgr": _sb(F, 320),
+    "phr": _sb(F, 320), "lgr": _sb(F, 320),
 }
 for _k in ("send", "land"):
     SCRATCH[_k + "c"] = _sb(C8, 480)
     SCRATCH[_k + "p"] = _sb(U8, 480)
 for _t in range(8):
     SCRATCH["ps%d" % _t] = ("psum", [128, 512], F)
-SEMAPHORES = ["v", "s", "t", "p", "dx", "du", "dw", "dv", "fin"] + ["%s%d" % (a, i) for a in ("arr", "snd") for i in range(3)]
+SEMAPHORES = ["v", "s", "t", "dx0", "dx1", "du", "dw", "dv", "fin"] + ["p%d" % i for i in range(56)] + ["%s%d" % (a, i) for a in ("arr", "snd") for i in range(3)]
 
 M1 = 12582912.0
 EPS = 2.0 ** -40
 U = 2.0 ** 26
-LOW = 2.0 ** 18
+LOW = 512.0
+CODE = 102608.0
 PARTNER = [1, 2, 3]
 
 
@@ -79,10 +80,16 @@ def rank_program(g, core, T, topo):
             if not more:
                 reads[k] = {}
 
-    def do(e, rd, wr, call, sem=None, n=1, more=False):
+    open_p = {"up": [], "all": [], "lo": []}
+
+    def do(e, rd, wr, call, sem=None, n=1, more=False, part="all"):
         pre(e, rd, "" if more else wr)
         if e == "p":
-            need("p", "p", count.get("p", 0))
+            sem = "p%d" % sum(k[0] == "p" for k in count)
+            for k in open_p[{"up": "all", "all": "up", "lo": "lo"}[part]]:
+                need("p", k, 1)
+            if part != "lo":
+                open_p[part].append(sem)
         if more:
             for k in wr.split():
                 for s, c in reads.get(k, {}).items():
@@ -123,14 +130,14 @@ def rank_program(g, core, T, topo):
         else:
             do("s", rd, wr, lambda: S.activation(out, a, func or AF.Copy, scale=scale), more=more)
 
-    def iota(wr, out, pat, base, cm, more=False):
-        do("p", "", wr, lambda: P.iota(out, pat, base, cm), more=more)
+    def iota(wr, out, pat, base, cm, more=False, part="all"):
+        do("p", "", wr, lambda: P.iota(out, pat, base, cm), more=more, part=part)
 
-    def iotaf(wr, out, pat, base, cm):
-        do("p", "", wr, lambda: P.iota(out, pat, base, cm, allow_small_or_imprecise_dtypes=True))
+    def iotaf(wr, out, pat, base, cm, part="all"):
+        do("p", "", wr, lambda: P.iota(out, pat, base, cm, allow_small_or_imprecise_dtypes=True), part=part)
 
-    def select(wr, rd, out, a, pat, op, c, base, cm, more=False):
-        do("p", rd, wr, lambda: P.affine_select(out, a, pat, op, c, base, cm), more=more)
+    def select(wr, rd, out, a, pat, op, c, base, cm, more=False, part="all"):
+        do("p", rd, wr, lambda: P.affine_select(out, a, pat, op, c, base, cm), more=more, part=part)
 
     def mm(wr, rd, *prods):
         pre("t", rd, wr)
@@ -139,51 +146,59 @@ def rank_program(g, core, T, topo):
         ins.then_inc(T.sem.t, 1)
         post("t", 1, rd, wr)
 
-    do("y", "", "xin", lambda: Y.dma_start(T.xin[:], T.x[:]), "dx", 16)
+    do("y", "", "xin1", lambda: Y.dma_start(T.xin[:, 32:64, :], T.x[:, 640:1280]), "dx1", 16)
     do("s", "", "ut", lambda: S.dma_start(T.ut[:], T.u[:]), "du", 16)
+    do("y", "", "xin0", lambda: Y.dma_start(T.xin[:, 0:32, :], T.x[:, 0:640]), "dx0", 16)
 
     lo, up = slice(0, 64), slice(64, 128)
     halves = ((0, lo), (1, up))
     fill("zz", T.zz[:], 0.0)
     fill("ones", T.ones[:], 1.0)
     fill("et0", T.et[:], 0.0)
-    fill("wc0", T.wct[:], 0.0)
     iota("pi", T.pi[:], [[0, 8]], 0, 1)
     iotaf("uf", T.uf[:], [[0, 4], [-64, 2]], 112, 0)
     iota("cti", T.cti[:], [[-8, 10], [0, 5]], 72, 1)
-    iotaf("v0i", T.val1[:], [[-1, 50]], 49, 0)
-    iotaf("v0j", T.sq[:], [[0, 2], [40, 2], [-1, 25]], 9, 0)
+    iotaf("v0i", T.val1[:], [[-5, 10], [0, 5]], 45, 0)
+    iotaf("tb2", T.tb[:, 0:10], [[-1, 10]], 9, 0)
+    iotaf("tb1", T.tb[:, 10:50], [[-1, 40]], 39, 0)
     iotaf("c0i", T.c0[:, 0, :], [[1, 10]], -7, 0)
     iotaf("hb0", T.hb[:, 0:160:4], [[0, 8], [1, 5]], 0, 0)
     iotaf("pay0", T.pay[:, 163:320:4], [[0, 8], [8, 5]], 0, 0)
-    select("wm1", "zz", T.wm[lo], T.zz[lo, 0:256], [[-1, 64], [8, 4]], Op.not_equal, 1.0, -56, 1)
-    select("wm", "wm1", T.wm[lo], T.wm[lo], [[-1, 64], [8, 4]], Op.not_equal, 1.0, 8, 1)
-    for h, sl in halves:
-        iota("n60", T.n60[sl, :], [[0, 15], [-8, 4]], 120 - 32 * h, 1, more=True)
-    iota("i20", T.i20[:], [[64, 5], [0, 4]], 0, 0)
+    part = ("lo", "up")
+    select("wm1", "zz", T.wm[lo], T.zz[lo, 0:256], [[-1, 64], [8, 4]], Op.not_equal, 1.0, -56, 1, part="lo")
+    iota("i20", T.i20[:], [[32, 5], [0, 4]], 0, 0)
+    select("wm", "wm1", T.wm[lo], T.wm[lo], [[-1, 64], [8, 4]], Op.not_equal, 1.0, 8, 1, part="lo")
     iota("d16i", T.d16i[:], [[1, 64]], 128, -1)
-    for h, sl in halves:
-        iotaf("gc%d" % h, T.ngm[sl, 2, :], [[-1, 4]], 71 - 4 * h, 0)
     select("et", "ones et0", T.et[:, 3:515:4], T.ones[:], [[-1, 128]], Op.is_equal, 0.0, 0, 1)
     for h, sl in halves:
-        iota("nr", T.nr[sl], [[1, 64], [-8, 4]], 120 - 32 * h, 0, more=True)
-    iota("jr", T.jr[:], [[1, 16], [-8, 4]], 8, -1)
+        iota("n60", T.n60[sl, :], [[0, 15], [-8, 4]], 120 - 32 * h, 1, more=True, part=part[h])
+        iotaf("gc%d" % h, T.ngm[sl, 2, :], [[-1, 4]], 71 - 4 * h, 0, part=part[h])
 
     ts("pu0", "pi", T.pi[:, 2:3], T.pi[:, 2:3], 3, Op.bitwise_and)
     ts("pu1", "pi", T.pi[:, 3:4], T.pi[:, 3:4], 12, Op.bitwise_and)
     ts("pj", "pi", T.pi[:, 0:2], T.pi[:, 0:2], 7, Op.bitwise_and)
-    quant("rq2z", "zz", T.rq2[:, 22:150], T.rs2[:, 22:150], T.zz[:])
-    for j in range(2):
-        act("rt0", "zz", T.rt[:, 2 * j:2 * j + 2, :, :], T.zz[:, 0:336], more=j > 0)
-        act("rt20", "zz", T.rt2[:, 3 * j:3 * j + 3, :], T.zz[:, 0:264], more=j > 0)
-    act("pt0", "zz", T.pt[:], T.zz[:])
+    for k, tile in (("rt0", T.rt), ("rt20", T.rt2), ("pt0", T.pt)):
+        fill(k, tile[:], 0.0)
     for j in range(3):
         act("w3z", "zz", T.w3[:, j, :, :], T.zz[:], more=j > 0)
     for h, sl in halves:
         cs = slice(64 * h, 64 * h + 64)
-        select("wt0", "ones w3z", T.w3[sl, 0, cs, 0], T.ones[sl, 0:64], [[1, 64]], Op.is_gt, 0.0, 0, -1, more=True)
-        select("wt0", "ones w3z", T.w3[sl, 0, cs, 1], T.ones[sl, 0:64], [[-1, 64]], Op.is_ge, 0.0, 0, 1, more=True)
-    iotaf("phr", T.phr[:], [[32, 5], [160, 2], [1, 32]], 0, 0)
+        select("wt0", "ones w3z", T.w3[sl, 0, cs, 0], T.ones[sl, 0:64], [[1, 64]], Op.is_gt, 0.0, 0, -1, more=True, part=part[h])
+        select("wt0", "ones w3z", T.w3[sl, 0, cs, 1], T.ones[sl, 0:64], [[-1, 64]], Op.is_ge, 0.0, 0, 1, more=True, part=part[h])
+    for step in range(2):
+        for h, sl in halves:
+            for e in range(4):
+                k0 = 64 - (56 - 32 * h - 8 * e) % 64
+                a, b = T.w3[sl, 1, 64 * h:64 * h + k0, e], T.w3[sl, 1, 64 * h + k0:64 * h + 64, e]
+                name = "wt1%d%d" % (h, e)
+                if step == 0:
+                    select(name + "a", "w3z", a, a, [[-1, k0]], Op.is_ge, -1.0, 0, 1, part=part[h])
+                    if k0 < 64:
+                        select(name + "b", "w3z", b, b, [[-1, 64 - k0]], Op.is_ge, -1.0, -k0, 1, part=part[h])
+                elif k0 < 64:
+                    select(name + "a", name + "a", a, a, [[0, k0]], Op.is_gt, -1.0, k0, -1, part=part[h])
+                    select(name + "b", name + "b", b, b, [[0, 64 - k0]], Op.is_ge, 0.0, -k0, 1, part=part[h])
+    iotaf("phr", T.phr[:], [[1, 320]], 0, 0)
     iotaf("lgr", T.lgr[:], [[160, 2], [1, 5], [5, 32]], 0, 0)
     copy("pu2", "pu0", T.pf[:, 6:7], T.pi[:, 2:3])
     ts("pu3", "pu1", T.pf[:, 7:8], T.pi[:, 3:4], -4.0, Op.mult)
@@ -200,26 +215,31 @@ def rank_program(g, core, T, topo):
     quant("uq0", "ut", T.uq0[:], T.us0[:], T.ut[:])
     fill("dp0", T.dp[:], 0.0)
     fill("cd0_", T.cde[:], 1)
-    ts("v0m", "v0i g0", T.tbb[:, 10:50], T.val1[:, 10:50], T.pf[:, 0:1], Op.not_equal)
-    ts("v0m", "v0j g0", T.tbb[:, 0:10], T.sq[:, 0, 0:10], T.pf[:, 0:1], Op.not_equal, more=True)
+    ts("v0m", "tb1 tb2 g0", T.tbb[:], T.tb[:, 0:50], T.pf[:, 0:1], Op.not_equal)
+    ts("ct0", "cti2", T.ct[:], T.cti[:], -U / 512, Op.mult, 64.40625 * U, Op.add)
+    ts("ct1", "cti2", T.so[:, 0, 0:50], T.cti[:], 32, Op.is_ge, -224 * U / 512, Op.mult)
     do("v", "uq0 uo", "uq", lambda: V.tensor_copy(T.uq[:].bitcast(dt.uint32), T.uq0[:].bitcast(dt.uint32).indirect(T.uo[:])))
-    do("v", "uq0 uo", "uq", lambda: V.tensor_copy(T.us[:], T.us0[:].indirect(T.uo[:])), more=True)
-    quant("ptqz", "zz", T.ptq[:, 64:192], T.pts[:, 64:192], T.zz[:])
-    for a in (40, 208):
-        quant("dgqz", "zz", T.dgq[:, a:a + 128], T.dgs[:, a:a + 128], T.zz[:], more=True)
+    do("s", "uq0 uo", "uq", lambda: S.activation(T.us[:], T.us0[:].indirect(T.uo[:]), AF.Copy), more=True)
 
-    for i in range(5):
-        if i < 3:
-            copy("xt0 xt1", "xin", T.xt[:, :, i, :, :], T.xin[:, :, 4 * i:4 * i + 4], more=True)
-        else:
-            act("xt0 xt1", "xin", T.xt[:, :, i, :, :], T.xin[:, :, 4 * i:4 * i + 4], more=True)
-    do("y", "xin", "wq", lambda: Y.dma_start(T.wq[:].bitcast(dt.uint8), T.wc[:]), "dw", 16, more=True)
+    def state(h):
+        quant("xq%d" % h, "xt%d" % h, T.xq[:, 160 * h:160 * h + 160], T.xs[:, 160 * h:160 * h + 160], T.xt[:, h, :, :, :])
+
+    def places(h):
+        for i in range(5):
+            (copy if i < 4 else act)("xt%d" % h, "xin%d" % h, T.xt[:, h, i, :, :], T.xin[:, 32 * h:32 * h + 32, 4 * i:4 * i + 4], more=True)
+
+    places(1)
+    quant("ptqz", "zz", T.ptq[:, 64:192], T.pts[:, 64:192], T.zz[:])
+    tt("ct", "ct0 ct1", T.ct[:], T.ct[:], T.so[:, 0, 0:50], Op.add)
+    state(1)
+    places(0)
+    do("y", "xin0", "wq", lambda: Y.dma_start(T.wq[:].bitcast(dt.uint8), T.wc[:]), "dw", 16, more=True)
     do("y", "", "wq", lambda: Y.dma_start(T.wsc[:], T.ws[:]), "dw", 16, more=True)
     do("y", "", "vt", lambda: Y.dma_start(T.vt[:], T.v[:]), "dv", 16)
-    ts("ct", "cti2", T.ct[:], T.cti[:], -U / 512, Op.mult, 64.3125 * U, Op.add)
-    ts("v0n", "v0i v0m", T.val1[:], T.val1[:], 64.4375, Op.add, U, Op.mult)
+    ts("v0n", "v0i", T.val1[:], T.val1[:], 66.5, Op.add, U, Op.mult)
     ts("c0a", "c0i g1", T.c0[:, 1, :], T.c0[:, 0, :], T.pf[:, 2:3], Op.is_equal)
-    quant("xq0 xq1", "xt0 xt1", T.xq[:], T.xs[:], T.xt[:])
+    fill("ne0", T.ne[:, :, 0:64:16], 0.0)
+    state(0)
 
     def constants0():
         tt("val1", "v0m v0n", T.val1[:], T.val1[:], T.tbb[:], Op.mult)
@@ -233,13 +253,11 @@ def rank_program(g, core, T, topo):
         ts("n60b", "n60", T.n60[:], T.n60[:], 63, Op.bitwise_and)
 
     def constants3():
-        for sl, c in ((lo, -U / 64), (up, 5 * U)):
+        for sl, c in ((lo, -U / 128), (up, 5 * U)):
             for a, w in ((0, 64), (64, 64), (128, 32)):
                 act("wat", "wm", T.wat[sl, a:a + w, :], T.wm[lo, 0:w, :], c, more=True)
-        for a, b, w in ((0, 0, 64), (128, 32, 32), (160, 0, 32)):
-            act("wct", "wm wc0", T.wct[lo, a:a + w, :], T.wm[lo, b:b + w, :], 5 * U, more=True)
-        for j in range(2):
-            act("dg0", "zz", T.dg[:, j, :, :, :], T.zz[:], more=j > 0)
+        for k, a, b in (("dgp", 0, 9), ("dgp", 9, 17), ("dgr", 0, 8), ("dgr", 8, 15)):
+            act("dg0", "zz", T[k][:, a:b, :, :, :], T.zz[:, 0:40 * (b - a)], more=True)
 
     def scores(h, banks):
         for j, k in enumerate(banks):
@@ -255,7 +273,7 @@ def rank_program(g, core, T, topo):
                 act("sc%d" % h, "ps%d" % banks[1], out, ps[banks[1]][32 * i - 32:32 * i, 0:32], more=True)
 
     def constants2():
-        ts("ngm", "n60b", T.ngm[:, 0, :], T.n60[:, 0:4], -U / 512, Op.mult, 102560.0 / 512 * U, Op.add)
+        ts("ngm", "g20", T.ngm[:, 0, :], T.g20[:, 0:4], -U / 512, Op.mult, CODE / 512 * U, Op.add)
         yield
         ts("n5", "n60b", T.inc[:, 0:4], T.n60[:, 0:4], 5.0, Op.mult, -160.0, Op.add)
         yield
@@ -265,8 +283,6 @@ def rank_program(g, core, T, topo):
         yield
         fill("pa16", T.pa16[:, 0:64:16], 0.0)
         yield
-        copy("ngf", "n60b", T.ngf[:], T.n60[:, 0:4])
-        yield
         ts("nb60", "n60b", T.nb60[:], T.n60[:], 4, Op.logical_shift_right)
         yield
         ts("d16a", "d16i", T.d16i[:], T.d16i[:], 15, Op.bitwise_and)
@@ -275,23 +291,12 @@ def rank_program(g, core, T, topo):
             quant("e%d" % b, "et", T.eqc[:, 128 * b:128 * b + 128], T.eqs[:, 128 * b:128 * b + 128], T.et[:, 3 - b:515 - b])
             yield
             yield
-        for j in range(2):
-            ts("nr2", "nr", T.nr[:, 32 * j:32 * j + 32, :], T.nr[:, 32 * j:32 * j + 32, :], 63, Op.bitwise_and, more=True)
-            yield
-            yield
-        ts("jr2", "jr", T.jr[:], T.jr[:], 15, Op.bitwise_and)
-        yield
+        ts("i16", "d16a", T.i16[:], T.d16i[:], 0, Op.is_equal)
         yield
         for h, sl in halves:
             for e in range(4):
-                ts("wt1", "nr2 ngf w3z", T.w3[sl, 1, 64 * h:64 * h + 64, e], T.nr[sl, :, e], T.ngf[sl, e:e + 1], Op.is_gt, -1.0, Op.mult, more=True)
-                yield
-                m = 16 * (7 - 4 * h - e)
-                ts("wt2", "jr2 w3z", T.w3[sl, 2, m:m + 16, e], T.jr[sl, :, e], 0, Op.is_equal, more=True)
-                yield
-        for j in range(3):
-            quant("qwt%d" % j, "wt%d" % j, T.cq3[:, 128 * j:128 * j + 128], T.cs3[:, 128 * j:128 * j + 128], T.w3[:, j, :, :])
-            yield
+                m, c = 16 * (7 - 4 * h - e), 8 * ((e + 1) % 2)
+                act("wt2", "i16 w3z", T.w3[sl, 2, m:m + 16, e], T.i16[sl, c:c + 16], more=True)
             yield
         for nb in range(4):
             ts("msk", "nb60", T.msk[:, nb, :], T.nb60[:], nb, Op.is_equal, more=True)
@@ -300,13 +305,20 @@ def rank_program(g, core, T, topo):
         yield
         ts("d16c", "d16a", T.d16[:, 1, :], T.d16i[:], 1, Op.is_equal, LOW, Op.mult)
         yield
-        ts("cb", "d16a", T.pf[:, 4:5], T.d16i[:, 15:16], 0, Op.not_equal, LOW / 512, Op.mult)
+        ts("cb", "d16a", T.pf[:, 4:5], T.d16i[:, 15:16], 0, Op.not_equal, LOW, Op.mult)
+        yield
+        yield
+        ts("msk", "msk", T.msk[:, :, 40:60], T.msk[:, :, 40:60], 0.625, Op.mult)
+        yield
+        for j in (0, 2, 1):
+            rd = " ".join(k for k in last if k.startswith("wt%d" % j))
+            quant("qwt%d" % j, rd, T.cq3[:, 128 * j:128 * j + 128], T.cs3[:, 128 * j:128 * j + 128], T.w3[:, j, :, :])
+            yield
+            yield
 
     def constants4():
         tt("d16", "d16b d16c", T.d16[:, 0, :], T.d16[:, 0, :], T.d16[:, 1, :], Op.subtract)
-        ts("cb2", "cb", T.pf[:, 5:6], T.pf[:, 4:5], -0.499, Op.add)
 
-    fill("ne0", T.ne[:, :, 0:64:16], 0.0)
     fill("ne0", T.ne[:, :, 15:64:16], 1.0, more=True)
     rest = constants2()
 
@@ -334,11 +346,16 @@ def rank_program(g, core, T, topo):
             for b in range(4):
                 mm("ps%d" % b, "xq0 xq1 e%d" % b, (ps[b][:, 0:320], T.eqc[:, 128 * b:128 * b + 128], T.eqs[:, 128 * b:128 * b + 128], T.xq[:, 0:320], T.xs[:, 0:320]))
                 act("tp", "ps%d" % b, T.tp[:, 320 * b:320 * b + 320], ps[b][:, 0:320], 0.5, more=b > 0)
+                yield
+                if b < 2:
+                    act("tw", "ps%d" % b, T.tw[:, 320 * b:320 * b + 320], ps[b][:, 0:320], 0.5, more=b > 0)
+                    yield
 
+        planes = unpack()
         if t == 0:
             constants3()
         else:
-            unpack()
+            list(planes)
         key = lambda a, b: T.sc[lo, :, a:b, 3]
         for s in range(1, 5):
             tt("cm", "sc0 sc1", T.cm[lo, s - 1, :, 0:5 - s], key(s, 5), key(0, 5 - s), Op.is_gt, more=True)
@@ -354,12 +371,14 @@ def rank_program(g, core, T, topo):
             tt("rk", "a2", T.rk[lo, 40 * j:40 * j + 40], T.a2[lo, 0, :], T.a2[lo, 1, :], Op.add, more=j > 0)
 
         def sym(i):
-            ts("rt2", "pay rt20", T.rt2[lo, 0:2, 16 * i:16 * i + 20:5], T.pay[lo, 3 + 4 * i:160:20], -8.0 * i, Op.add, more=i > 0)
+            ts("rt2", "pay rt20", T.rt2[up, 0:2, 16 * i:16 * i + 20:5], T.pay[lo, 3 + 4 * i:160:20], -8.0 * i, Op.add, more=i > 0)
 
         if t == 0:
-            tt("i20b", "n60b i20", T.i20[:], T.i20[:], T.n60[:, 0:20], Op.add)
+            ts("g20a", "n60b", T.g20[:], T.n60[:, 0:20], 32, Op.is_ge, 224.0, Op.mult)
         for i in range(3):
             sym(i)
+        if t == 0:
+            tt("g20", "n60b g20a", T.g20[:], T.g20[:], T.n60[:, 0:20], Op.add)
         for r in range(5):
             ts("eqr%d" % r, "rk", T.eqr[lo, r, :], T.rk[lo], 4.0 - r, Op.is_equal, 64.0, Op.mult)
         for r in range(5):
@@ -367,6 +386,7 @@ def rank_program(g, core, T, topo):
 
         if t == 0:
             quant("wa", "wat", T.waq[:], T.was[:], T.wat[:])
+            tt("i20b", "g20 i20", T.i20[:], T.i20[:], T.g20[:], Op.add)
         sym(3)
         sym(4)
         copy("rth", "prb rt0", T.rt[lo, 0:2, 0:4, 0:20:4], T.prb[lo, 44:80:5, :])
@@ -376,11 +396,10 @@ def rank_program(g, core, T, topo):
         mm("ps5", "wa rq", *[(ps[5][:, 0:128], T.waq[:, w:w + 128], T.was[:, w:w + 128], T.rq[:, c:c + 128], T.rs[:, c:c + 128])
                              for w, c in ((0, 0), (32, 22))])
         if t == 0:
-            quant("wc", "wct", T.wcq[:], T.wcs[:], T.wct[:])
-            ts("ctp", "i20b", T.ctp[:], T.i20[:], -U / 512, Op.mult, 64.3125 * U, Op.add)
-        quant("rq2", "rq2z rt2", T.rq2[:, 0:132], T.rs2[:, 0:132], T.rt2[:])
-        mm("ps6", "wc rq2 rq2z", *[(ps[6][:, 0:128], T.wcq[:, w:w + 128], T.wcs[:, w:w + 128], T.rq2[:, c:c + 128], T.rs2[:, c:c + 128])
-                                   for w, c in ((0, 0), (64, 22))])
+            ts("ctp", "i20b", T.ctp[:], T.i20[:], -U / 512, Op.mult, 64.40625 * U, Op.add)
+        quant("rq2", "rt2", T.rq2[:], T.rs2[:], T.rt2[:])
+        for h in range(2):
+            mm("ps%d" % (6 + h), "wa rq2", (ps[6 + h][:, 0:128], T.waq[:, 32 * h:32 * h + 128], T.was[:, 32 * h:32 * h + 128], T.rq2[:, 22 * h:22 * h + 128], T.rs2[:, 22 * h:22 * h + 128]))
         fillers(4)
         scan("so0", "c0 ps5", T.so[:, 0, 141:150], T.c0[:, 0, 0:9], ps[5][:, 4:45:5], ops=(Op.add, Op.max))
         tt("tb1", "ps5 ct", T.tb[:, 10:50], ps[5][:, 0:40], T.ct[:, 10:50], Op.add)
@@ -423,7 +442,8 @@ def rank_program(g, core, T, topo):
             if n == 1:
                 tt("dtb", "tb1 tb2 tb0 dt0", T.dt3[:, 0, 2:150:3], T.tb[:, 0:50], T.tb[:, 1:51], Op.subtract)
                 tt("tbm", "val1 tb1 tb2", T.tbb[:], T.val1[:], T.tb[:, 0:50], Op.is_ge)
-                tt("tbp", "ps6 ctp", T.tbp[:], ps[6][:, 0:20], T.ctp[:], Op.add)
+                for h, sl in halves:
+                    tt("tbp", "ps%d ctp" % (6 + h), T.tbp[sl], ps[6 + h][sl, 0:20], T.ctp[sl], Op.add, more=h > 0)
                 marks(0)
             else:
                 ts("abb%d" % w, "tbb " + so, T.ab[:, w, 3 * j + 2:150:3], T.tbb[:, j:50], s, Op.is_equal, EPS, Op.add)
@@ -447,7 +467,7 @@ def rank_program(g, core, T, topo):
             if n == 1:
                 tt("tbb", "tbm", T.tbb[:], T.tbb[:], T.tb[:, 0:50], Op.mult)
             if n == 11:
-                ts("ca", " ".join("cd%d" % m for m in range(11)), T.ca[:], T.cde[:], 63, Op.bitwise_and)
+                ts("ca", " ".join("cd%d" % m for m in range(11)), T.ca[:], T.cde[:], 256 + 31, Op.bitwise_and)
             if n in (11, 12):
                 group()
             if n < 11:
@@ -457,33 +477,32 @@ def rank_program(g, core, T, topo):
             if 2 <= n < 12 or n == 13:
                 undrawn(n - 2 if n < 12 else 10)
             if n < 11:
-                fillers(3)
-            if t == 0 and n == 5:
-                unpack()
+                fillers(2)
+            if n >= 5:
+                next(planes, None)
             if t == 0 and n == 10:
                 fillers(99)
-                act("ph512", "phr", T.ph512[:], T.phr[:], 512.0)
         s = T.so[:, 13, 149:150]
         marks(13)
         need("v", "v", reads["po0"]["v"])
         drew(13)
         ts("ne13", "so13 tbp ne0", T.ne[:, :, 1:64:16], T.tbp[:], s, Op.not_equal)
+        undrawn(11)
         for e in range(4):
             ts("po3", "sg13 pe pt0", T.pt[:, 256 + 65 * e:257 + 65 * e], T.so[:, 16, 149:150], T.ngm[:, 2, e:e + 1], Op.is_equal, T.pe[:, 16 * e + 15:16 * e + 16], Op.add, more=e > 0)
 
         def before(i):
             scan("uopp", "ne ne13 dp", T.uop[:, 0, i, :], T.ne[:, i, :], T.dp[:], more=i > 0)
 
-        undrawn(11)
+        undrawn(12)
         for i in range(3):
             before(i)
         quant("ptq", "po0 po1 po3 ptqz", T.ptq[:, 0:128], T.pts[:, 0:128], T.pt[:])
         mm("ps4", "ptq ptqz qwt0 qwt1", (ps[4][:, 0:128], *W3(0), T.ptq[:, 0:128], T.pts[:, 0:128]),
            (ps[4][:, 0:128], *W3(1), T.ptq[:, 64:192], T.pts[:, 64:192]))
-        undrawn(12)
+        tt("fl und1", "und0 ne13", T.und[:, 1, :], T.und[:, 0, :], T.ne[:, :, 1:64:16], Op.mult)
         before(3)
         before(4)
-        tt("fl und1", "und0 ne13", T.und[:, 1, :], T.und[:, 0, :], T.ne[:, :, 1:64:16], Op.mult)
 
         def digits(x):
             for d, m in enumerate((15, 240, 256) if x == "p" else (15, -16)):
@@ -493,76 +512,87 @@ def rank_program(g, core, T, topo):
         def spread(x, blocks=range(4)):
             j, nd = (1, 2) if x == "q" else (0, 3)
             for nb in blocks:
-                tt("dg" + x, "di%s msk dg0" % x, T.dg[:, j, 0:5 * nd, nb, :], T.dgi[:, 3 * j:3 * j + nd, :], T.msk[:, nb, 0:20 * nd], Op.mult, more=nb > 0)
+                tt("dg" + x, "di%s msk dg0" % x, T[("dgp", "dgr")[j]][:, nb // 2:2 * nd:2, :, nb % 2, :], T.dgi[:, 3 * j:3 * j + nd, :], T.msk[:, nb, 0:20 * nd], Op.mult, more=nb > 0)
 
         def form(x, k):
             j, nd = (1, 2) if x == "q" else (0, 3)
-            c = 168 * j
-            quant("dq" + x, "dg%s dgqz" % x, T.dgq[:, c:c + 128], T.dgs[:, c:c + 128], T.dg[:, j, :, :, :])
-            mm("ps%d" % k, "dq%s dgqz qwt2" % x, *[(ps[k][:, 0:128], *W3(2), T.dgq[:, c + 20 * d:c + 20 * d + 128], T.dgs[:, c + 20 * d:c + 20 * d + 128]) for d in range(nd)])
+            c, w = 170 * j, 170 - 20 * j
+            quant("dq" + x, "dg" + x, T.dgq[:, c:c + w], T.dgs[:, c:c + w], T[("dgp", "dgr")[j]][:])
+            mm("ps%d" % k, "dq%s qwt2" % x, *[(ps[k][:, 0:128], *W3(2), T.dgq[:, c + 20 * d:c + 20 * d + 128], T.dgs[:, c + 20 * d:c + 20 * d + 128]) for d in range(nd)])
 
-        ts("v2p", "uopp", T.v2[:, 0, :], T.uop[:, 0, :, 13:64:16], -512 / U, Op.mult, 102560.0, Op.add)
+        act("pr0", "fl", T.pr[:], T.und[:, 1, :], 1024.0, bias=-160.0)
         for e in range(4):
             scan("inc", "pa16 fl n5", T.inc[:, 4 + e:24:4], T.pa16[:, 1:6], T.und[:, 1, e:20:4], more=e > 0, initial=T.inc[:, e:e + 1])
-        digits("p")
-        ts("pr0", "fl", T.pr[:], T.und[:, 1, :], 1024.0, Op.mult, -160.0, Op.add)
+        ts("v2p", "uopp", T.v2[:, 0, :], T.uop[:, 0, :, 13:64:16], -512 / U, Op.mult, CODE, Op.add)
         for i in range(5):
             scan("uopq", "ne ne13 ps4", T.uop[:, 1, i, :], T.ne[:, i, :], ps[4][:, 0:64], more=i > 0)
-        tt("pr", "pr0 inc", T.pr[:], T.pr[:], T.inc[:, 0:20], Op.min)
-        spread("p", (0, 1))
+            if i == 2:
+                tt("pr", "pr0 inc", T.pr[:], T.pr[:], T.inc[:, 0:20], Op.min)
+        digits("p")
         tt("v2q", "uopq pr", T.v2[:, 1, :], T.uop[:, 1, :, 15:64:16], T.pr[:], Op.add)
-        spread("p", (2, 3))
+        spread("p", (0, 1))
         digits("q")
-        form("p", 5)
+        spread("p", (2, 3))
         spread("q")
+        form("p", 5)
         form("q", 6)
         copy("ofp", "ps5", T.ofp[:], ps[5][:, 0:20])
         if t == 0:
             constants4()
-        tt("pk", "ofp phr ph512", T.pk[:], T.phr[:].indirect(T.ofp[:]), T.ph512[:], Op.add)
+        for b in (2, 3):
+            act("tq%d" % b, "ofp tp", T.tq[:, 320 * b:320 * b + 320], T.tp[:, 320 * b:320 * b + 320].indirect(T.ofp[:]))
+
+        def early(b, h):
+            cs = slice(320 * b + 160 * h, 320 * b + 160 * h + 160)
+            tt("tq%d" % b, "ofp tp tw", T.tq[:, cs], T.tp[:, 320 * b:320 * b + 320].indirect(T.ofp[:, 10 * h:10 * h + 10]), T.tw[:, cs], Op.add, more=h > 0)
+
         ts("ofq", "ps6", T.ofq[:], ps[6][:, 0:20], 160.0, Op.add)
-        do("v", "ofq pk", "row", lambda: V.tensor_copy(T.row[:].indirect(T.ofq[:]), T.pk[:]))
+        early(0, 0)
+        do("v", "ofq phr", "row", lambda: V.tensor_copy(T.row[:].indirect(T.ofq[:]), T.phr[:]))
+        early(0, 1)
         for i in range(5):
             scan("s5", "d16 row", T.s5[:, i, :], T.d16[:, 0, :], T.row[:, 64 * i:64 * i + 64] if final else T.row[:, i:320:5], more=i > 0, ops=LATCH)
+        early(1, 0)
         parts = [(slice(0, 20), slice(0, 4))] if final else [(slice(10 * h, 10 * h + 10), slice(2 * h, 2 * h + 2)) for h in range(2)]
         for h, (o, v) in enumerate(parts):
-            ts("offa%d" % h, "s5 cb2", T.offa[:, o], T.s5[:, :, 15 + 16 * v.start:16 * v.stop:16], 1 / 512, Op.mult, T.pf[:, 5:6], Op.add)
-            if h == 0:
-                copy("xi", "s5", T.xi[:], T.s5[:, :, 15:64:16])
-        for h, (o, v) in enumerate(parts):
-            ts("xj", "xi", T.xj[:, o], T.xi[:, :, v], 511, Op.bitwise_and, more=h > 0)
-        copy("offb", "xj", T.offb[:], T.xj[:])
+            ts("offa%d" % h, "s5 cb", T.offa[:, o], T.s5[:, :, 15 + 16 * v.start:16 * v.stop:16], T.pf[:, 4:5], Op.add)
+
+        early(1, 1)
 
         def picks(h):
-            o = slice(10 * h, 10 * h + 10)
-            for b in range(4):
-                act("at%d%d" % (h, b), "offa%d tp" % (0 if final else h), T.at[:, 640 * h + b:640 * h + 640:4], T.tp[:, 320 * b:320 * b + 320].indirect(T.offa[:, o]))
+            for b in (2, 3):
+                act("at%d%d" % (h, b), "offa%d tp" % (0 if final else h), T.at[:, 640 * h + b:640 * h + 640:4], T.tp[:, 320 * b:320 * b + 320].indirect(T.offa[:, 10 * h:10 * h + 10]))
 
         def blend(h, planes):
-            o = slice(10 * h, 10 * h + 10)
             for b in planes:
-                cs = slice(640 * h + b, 640 * h + 640, 4)
-                tt("zt%d" % h, "offb tp at%d%d" % (h, b), T.zt[:, cs], T.tp[:, 320 * b:320 * b + 320].indirect(T.offb[:, o]), T.at[:, cs], Op.add, more=b > 0)
+                cs, win = slice(640 * h + b, 640 * h + 640, 4), T.tq[:, 320 * b:320 * b + 320].indirect(T.offa[:, 10 * h:10 * h + 10])
+                rd = "offa%d tq%d" % (0 if final else h, b)
+                if (h, b) == (0, 1):
+                    act("zt0", rd, T.zt[:, cs], win, more=True)
+                elif b < 2:
+                    copy("zt%d" % h, rd, T.zt[:, cs], win, more=b > 0)
+                else:
+                    tt("zt%d" % h, rd + " at%d%d" % (h, b), T.zt[:, cs], win, T.at[:, cs], Op.add, more=True)
 
         def kept(h):
-            cs = slice(640 * h, 640 * h + 640)
-            act("ak%d" % h, " ".join("at%d%d" % (h, b) for b in range(4)), T.ak[:, cs], T.at[:, cs], 2048.0)
+            for b in range(4):
+                cs = slice(640 * h + b, 640 * h + 640, 4)
+                if b < 2:
+                    act("ak%d%d" % (h, b), "offa%d tp" % (0 if final else h), T.ak[:, cs], T.tp[:, 320 * b:320 * b + 320].indirect(T.offa[:, 10 * h:10 * h + 10]), 2048.0)
+                else:
+                    act("ak%d%d" % (h, b), "at%d%d" % (h, b), T.ak[:, cs], T.at[:, cs], 2048.0)
 
         def new(h, b, k, cod):
             mm("ps%d" % k, "wq " + cod[0], (ps[k][:, 0:160], T.wq[:, 128 * b:128 * b + 128], T.wsc[:, 128 * b:128 * b + 128], cod[1], cod[2]))
 
         def finish(h, b, k):
-            tt("tm%d%d" % (h, b), "ps%d ak%d" % (k, h), T.tm[:, 4 * h + b, :], ps[k][:, 0:160], T.ak[:, 640 * h + b:640 * h + 640:4], Op.add)
+            tt("tm%d%d" % (h, b), "ps%d ak%d%d" % (k, h, b), T.tm[:, 4 * h + b, :], ps[k][:, 0:160], T.ak[:, 640 * h + b:640 * h + 640:4], Op.add)
             act("xt%d" % h, "tm%d%d" % (h, b), T.xt[:, h, :, :, b], T.tm[:, 4 * h + b, :], 2.0 ** -11, more=b > 0)
-
-        def state(h):
-            quant("xq%d" % h, "xt%d" % h, T.xq[:, 160 * h:160 * h + 160], T.xs[:, 160 * h:160 * h + 160], T.xt[:, h, :, :, :])
 
         rc = slice(160 * t, 160 * t + 160)
         picks(0)
-        picks(1)
         blend(0, range(4))
-        blend(1, [0])
+        picks(1)
         quant("send%d" % t, "zt0", T.sendc[:, rc], T.sendp[:, rc], T.zt[:, 0:640])
         dst = partner_of(t)
         rid, pid, _ = topo.addr(dst)
@@ -571,7 +601,7 @@ def rank_program(g, core, T, topo):
             g.remote_dma(a, b, T.sem["arr%d" % t], T.sem["snd%d" % t], pid, rid, topo.mask(core, dst))
         eng = 2 * len(topo.engines(core, dst))
         last["land%d" % t] = {"arr%d" % t: eng}
-        blend(1, [1, 2, 3])
+        blend(1, range(4))
         kept(1)
         kept(0)
         if final:
@@ -607,7 +637,5 @@ def rank_program(g, core, T, topo):
     for k in range(4):
         do("y", "xq0 xq1", "", lambda: Y.dma_start(T.osc[4 * k:4 * k + 4, :], T.xs[32 * k:32 * k + 4, :]), "fin", 16)
     need("y", "fin", count["fin"])
-    for k in ("v", "s", "t", "p"):
-        need("y", k, count[k])
-    for k in ("dx", "du", "dw", "dv"):
-        need("y", k, count[k])
+    for k in count:
+        need("y" if k in ("fin", "v", "s", "t") else "p", k, count[k])

@@ -14,25 +14,24 @@ SCRATCH = {
     "xq": _sb(C8, 320), "xs": _sb(U8, 320), "uq": _sb(C8, 128), "us": _sb(U8, 128), "vq": _sb(C8, 128), "vs": _sb(U8, 128),
     "uq0": _sb(C8, 128), "us0": _sb(U8, 128), "uo": _sb(U16, 8), "uf": _sb(F, 8),
     "wq": _sb(C8, 512), "wsc": _sb(U8, 512), "lq": _sb(C8, 160), "lsc": _sb(U8, 160),
-    "sc": _sb(F, 8, 5, 4), "cm": _sb(B, 4, 8, 5), "a2": _sb(B, 2, 40), "hb": _sb(B, 160), "rk": _sb(B, 80), "pay": _sb(B, 320),
-    "eqr": _sb(B, 5, 80), "prb": _sb(F, 80, 5), "rt": _sb(B, 4, 8, 21), "rq": _sb(C8, 168), "rs": _sb(U8, 168),
+    "sc": _sb(F, 8, 5, 4), "cm": _sb(B, 4, 8, 5), "a2": _sb(B, 2, 40), "hb": _sb(B, 160), "rk": _sb(B, 40), "pay": _sb(B, 160),
+    "pd": _sb(B, 80), "eqr": _sb(B, 5, 80), "prb": _sb(B, 80, 5), "rt": _sb(B, 4, 8, 21), "rq": _sb(C8, 168), "rs": _sb(U8, 168),
     "rt2": _sb(B, 7, 88), "rq2": _sb(C8, 154), "rs2": _sb(U8, 154),
-    "tb": _sb(F, 56), "tbb": _sb(F, 50), "val": _sb(B, 2, 50), "sq": _sb(B, 2, 50), "ab": _sb(F, 2, 150), "dt3": _sb(F, 2, 150),
-    "so": _sb(F, 17, 150), "tbp": _sb(F, 20), "sqp": _sb(F, 3, 20), "und": _sb(F, 2, 20), "tt4": _sb(F, 2, 4),
+    "tbb": _sb(B, 50), "val": _sb(B, 2, 50), "sq": _sb(B, 2, 50), "ab": _sb(B, 2, 150), "dt3": _sb(B, 3, 150),
+    "so": _sb(B, 31, 150), "tbp": _sb(F, 2, 20), "sqp": _sb(F, 3, 20), "und": _sb(F, 2, 20), "tt4": _sb(F, 2, 4),
     "cde": _sb(I, 64), "ca": _sb(I, 64), "pe": _sb(F, 64), "pt": _sb(B, 512),
     "ptq": _sb(C8, 192), "pts": _sb(U8, 192), "ne": _sb(F, 5, 64), "dp": _sb(F, 64), "uop": _sb(F, 2, 5, 64),
-    "inc": _sb(F, 24), "pr": _sb(F, 20), "v2": _sb(I, 2, 20), "dgi": _sb(I, 5, 20), "dgp": _sb(B, 17, 5, 2, 4), "dgr": _sb(B, 15, 5, 2, 4),
-    "dgq": _sb(C8, 320), "dgs": _sb(U8, 320), "ofp": _sb(U16, 20), "ofq": _sb(U16, 20), "pk": _sb(F, 320), "row": _sb(F, 320),
+    "inc": _sb(F, 24), "pr": _sb(F, 20), "v2": _sb(I, 2, 20), "dgi": _sb(I, 6, 20), "dgp": _sb(B, 19, 5, 2, 4), "dgr": _sb(B, 15, 5, 2, 4),
+    "dgq": _sb(C8, 340), "dgs": _sb(U8, 340), "ofp": _sb(U16, 20), "ofq": _sb(U16, 20), "pk": _sb(F, 320), "row": _sb(F, 320),
     "s5": _sb(F, 5, 64), "offa": _sb(U16, 20), "tq": _sb(B, 1280), "tw": _sb(B, 640),
     "tp": _sb(B, 1280), "zt": _sb(B, 1280), "at": _sb(B, 1280), "ak": _sb(B, 1280), "tm": _sb(F, 8, 160),
     "zz": _sb(B, 512), "zf": _sb(F, 4), "wm": _sb(B, 64, 4), "wat": _sb(B, 160, 4), "i16": _sb(B, 64),
     "waq": _sb(C8, 160), "was": _sb(U8, 160),
     "et": _sb(B, 516), "ones": _sb(B, 128), "eqc": _sb(C8, 512), "eqs": _sb(U8, 512),
     "w3": _sb(B, 3, 128, 4), "cq3": _sb(C8, 384), "cs3": _sb(U8, 384),
-    "n60": _sb(I, 60), "nb60": _sb(I, 60), "msk": _sb(F, 4, 60),
-    "i20": _sb(I, 20), "g20": _sb(I, 20), "ctp": _sb(F, 20), "ngm": _sb(F, 3, 4),
-    "cti": _sb(I, 50), "ct": _sb(F, 50), "val1": _sb(B, 50), "pi": _sb(I, 8), "pf": _sb(F, 10), "c0": _sb(F, 3, 10),
-    "pa2": _sb(B, 160), "pa16": _sb(F, 64), "d16i": _sb(I, 64), "d16": _sb(F, 2, 64),
+    "n80": _sb(I, 80), "nb80": _sb(I, 80), "msk": _sb(F, 4, 80), "cg": _sb(F, 20), "grp": _sb(F, 2, 4),
+    "ct": _sb(F, 4, 50), "val1": _sb(B, 50), "pi": _sb(I, 8), "pf": _sb(F, 10), "c0": _sb(F, 5, 10),
+    "pa": _sb(B, 160), "pa16": _sb(F, 64), "d16i": _sb(I, 64), "d16": _sb(F, 2, 64),
     "phr": _sb(F, 320), "lgr": _sb(F, 320),
 }
 for _k in ("send", "land"):
@@ -40,13 +39,11 @@ for _k in ("send", "land"):
     SCRATCH[_k + "p"] = _sb(U8, 480)
 for _t in range(8):
     SCRATCH["ps%d" % _t] = ("psum", [128, 512], F)
-SEMAPHORES = ["v", "s", "t", "dx0", "dx1", "du", "dw", "dv", "fin"] + ["p%d" % i for i in range(56)] + ["%s%d" % (a, i) for a in ("arr", "snd") for i in range(3)]
+SEMAPHORES = ["v", "s", "t", "dx0", "dx1", "du", "dw", "dv", "fin"] + ["p%d" % i for i in range(60)] + ["%s%d" % (a, i) for a in ("arr", "snd") for i in range(3)]
 
-M1 = 12582912.0
 EPS = 2.0 ** -40
-U = 2.0 ** 26
+U = 2.0 ** 18
 LOW = 512.0
-CODE = 102608.0
 PARTNER = [1, 2, 3]
 
 
@@ -113,8 +110,6 @@ def rank_program(g, core, T, topo):
     def scan(wr, rd, out, a, b, more=False, ops=(Op.mult, Op.add), initial=0.0):
         do("v", rd, wr, lambda: V.tensor_tensor_scan(out, a, b, initial, ops[0], ops[1]), more=more)
 
-    LATCH = (Op.add, Op.min)
-
     def copy(wr, rd, out, a, more=False):
         do("v", rd, wr, lambda: V.tensor_copy(out, a), more=more)
 
@@ -130,11 +125,14 @@ def rank_program(g, core, T, topo):
         else:
             do("s", rd, wr, lambda: S.activation(out, a, func or AF.Copy, scale=scale), more=more)
 
+    def const(wr, out, n, c, more=False):
+        act(wr, "zz", out, T.zz[:, 0:n], bias=c, more=more)
+
     def iota(wr, out, pat, base, cm, more=False, part="all"):
         do("p", "", wr, lambda: P.iota(out, pat, base, cm), more=more, part=part)
 
-    def iotaf(wr, out, pat, base, cm, part="all"):
-        do("p", "", wr, lambda: P.iota(out, pat, base, cm, allow_small_or_imprecise_dtypes=True), part=part)
+    def iotaf(wr, out, pat, base, cm=0, more=False, part="all"):
+        do("p", "", wr, lambda: P.iota(out, pat, base, cm, allow_small_or_imprecise_dtypes=True), more=more, part=part)
 
     def select(wr, rd, out, a, pat, op, c, base, cm, more=False, part="all"):
         do("p", rd, wr, lambda: P.affine_select(out, a, pat, op, c, base, cm), more=more, part=part)
@@ -151,36 +149,53 @@ def rank_program(g, core, T, topo):
     do("y", "", "xin0", lambda: Y.dma_start(T.xin[:, 0:32, :], T.x[:, 0:640]), "dx0", 16)
 
     lo, up = slice(0, 64), slice(64, 128)
-    halves = ((0, lo), (1, up))
+    halves, part = ((0, lo), (1, up)), ("lo", "up")
     fill("zz", T.zz[:], 0.0)
     fill("ones", T.ones[:], 1.0)
     fill("et0", T.et[:], 0.0)
     iota("pi", T.pi[:], [[0, 8]], 0, 1)
-    iotaf("uf", T.uf[:], [[0, 4], [-64, 2]], 112, 0)
-    iota("cti", T.cti[:], [[-8, 10], [0, 5]], 72, 1)
-    iotaf("v0i", T.val1[:], [[-5, 10], [0, 5]], 45, 0)
-    iotaf("tb2", T.tb[:, 0:10], [[-1, 10]], 9, 0)
-    iotaf("tb1", T.tb[:, 10:50], [[-1, 40]], 39, 0)
-    iotaf("c0i", T.c0[:, 0, :], [[1, 10]], -7, 0)
-    iotaf("hb0", T.hb[:, 0:160:4], [[0, 8], [1, 5]], 0, 0)
-    iotaf("pay0", T.pay[:, 163:320:4], [[0, 8], [8, 5]], 0, 0)
-    part = ("lo", "up")
+    iotaf("uf", T.uf[:], [[0, 4], [-64, 2]], 112)
+    iotaf("ct0", T.ct[:, 0, 0:10], [[1, 10]], 158)
+    iotaf("ct0", T.ct[:, 0, 10:50], [[1, 40]], 128, more=True)
+    iotaf("ct3", T.ct[:, 3, 0:10], [[-1, 2], [0, 5]], 129)
+    iotaf("ct3", T.ct[:, 3, 10:50], [[-1, 8], [0, 5]], 135, more=True)
+    iotaf("c0i", T.c0[:, 0, :], [[1, 10]], -7)
     select("wm1", "zz", T.wm[lo], T.zz[lo, 0:256], [[-1, 64], [8, 4]], Op.not_equal, 1.0, -56, 1, part="lo")
-    iota("i20", T.i20[:], [[32, 5], [0, 4]], 0, 0)
-    select("wm", "wm1", T.wm[lo], T.wm[lo], [[-1, 64], [8, 4]], Op.not_equal, 1.0, 8, 1, part="lo")
     iota("d16i", T.d16i[:], [[1, 64]], 128, -1)
+    select("wm", "wm1", T.wm[lo], T.wm[lo], [[-1, 64], [8, 4]], Op.not_equal, 1.0, 8, 1, part="lo")
     select("et", "ones et0", T.et[:, 3:515:4], T.ones[:], [[-1, 128]], Op.is_equal, 0.0, 0, 1)
+    for j in range(2):
+        iotaf("pd0", T.pd[up, j:80:2], [[0, 8], [2 * j - 1, 5]], 0, more=True, part="up")
     for h, sl in halves:
-        iota("n60", T.n60[sl, :], [[0, 15], [-8, 4]], 120 - 32 * h, 1, more=True, part=part[h])
-        iotaf("gc%d" % h, T.ngm[sl, 2, :], [[-1, 4]], 71 - 4 * h, 0, part=part[h])
+        iotaf("cg", T.cg[sl], [[0, 5], [5, 4]], 132 + 20 * h, more=True, part=part[h])
+        iotaf("gc", T.grp[sl, 0, :], [[-1, 4]], 135 - 4 * h, more=True, part=part[h])
+        iota("n80", T.n80[sl, :], [[0, 20], [-8, 4]], 120 - 32 * h, 1, more=True, part=part[h])
 
     ts("pu0", "pi", T.pi[:, 2:3], T.pi[:, 2:3], 3, Op.bitwise_and)
     ts("pu1", "pi", T.pi[:, 3:4], T.pi[:, 3:4], 12, Op.bitwise_and)
     ts("pj", "pi", T.pi[:, 0:2], T.pi[:, 0:2], 7, Op.bitwise_and)
-    for k, tile in (("rt0", T.rt), ("rt20", T.rt2), ("pt0", T.pt)):
+    ts("pk0", "pi", T.pi[:, 4:5], T.pi[:, 4:5], 63, Op.bitwise_and)
+    for k, tile in (("rt0", T.rt), ("rt20", T.rt2), ("w3z", T.w3)):
         fill(k, tile[:], 0.0)
-    for j in range(3):
-        act("w3z", "zz", T.w3[:, j, :, :], T.zz[:], more=j > 0)
+    const("zf", T.zf[:], 4, 0.0)
+    const("pa", T.pa[:], 160, 0.0)
+    const("hb0", T.hb[:, 0:160:4], 40, 0.0)
+    const("eq0", T.eqr[:, :, 0:80:2], 200, 1.0)
+    const("dt0", T.dt3[:, :, 1:150:3], 150, 0.0)
+    const("abk", T.ab[:, :, 0:150:3], 100, 1 / EPS)
+    const("pa", T.pa[:, 0:160:4], 40, 128.0)
+    for j in range(10):
+        const("v0n", T.val1[:, 5 * j:5 * j + 5], 5, 200 * U * 2.0 ** (9 - j), more=True)
+    act("ct1", "ct0", T.ct[:, 1, :], T.ct[:, 0, :], U)
+    act("ct2", "ct0", T.ct[:, 2, :], T.ct[:, 0, :], -U / EPS)
+    act("dg1", "ct3", T.dt3[:, 2, 2:150:3], T.ct[:, 3, :])
+    act("dg1", "ct3", T.dt3[:, 2, 0:150:3], T.ct[:, 3, :], -1 / EPS, more=True)
+    const("dp0", T.dp[:], 64, 0.0)
+    const("pa16", T.pa16[:], 64, 1.0)
+    const("ne0", T.ne[:, :, 0:64:16], 20, 0.0)
+    const("ne0", T.ne[:, :, 15:64:16], 20, 1.0, more=True)
+    const("pt0", T.pt[:], 512, 0.0)
+    const("pa16", T.pa16[:, 0:64:16], 4, 0.0)
     for h, sl in halves:
         cs = slice(64 * h, 64 * h + 64)
         select("wt0", "ones w3z", T.w3[sl, 0, cs, 0], T.ones[sl, 0:64], [[1, 64]], Op.is_gt, 0.0, 0, -1, more=True, part=part[h])
@@ -198,26 +213,22 @@ def rank_program(g, core, T, topo):
                 elif k0 < 64:
                     select(name + "a", name + "a", a, a, [[0, k0]], Op.is_gt, -1.0, k0, -1, part=part[h])
                     select(name + "b", name + "b", b, b, [[0, 64 - k0]], Op.is_ge, 0.0, -k0, 1, part=part[h])
-    iotaf("phr", T.phr[:], [[1, 320]], 0, 0)
-    iotaf("lgr", T.lgr[:], [[160, 2], [1, 5], [5, 32]], 0, 0)
+    iotaf("phr", T.phr[:], [[1, 320]], 0)
+    iotaf("lgr", T.lgr[:], [[160, 2], [1, 5], [5, 32]], 0)
     copy("pu2", "pu0", T.pf[:, 6:7], T.pi[:, 2:3])
     ts("pu3", "pu1", T.pf[:, 7:8], T.pi[:, 3:4], -4.0, Op.mult)
-    ts("g0", "pj", T.pf[:, 0:2], T.pi[:, 0:2], 5.0, Op.mult)
+    ts("g0", "pj", T.pf[:, 0:2], T.pi[:, 0:2], -5.0, Op.mult, 167.0, Op.add)
     ts("g1", "pj", T.pf[:, 2:4], T.pi[:, 0:2], -1.0, Op.mult)
-    fill("pa2", T.pa2[:], 2.0)
-    fill("zf", T.zf[:], 0.0)
-    fill("tb0", T.tb[:, 50:54], 0.0)
-    ts("uo", "uf pu2 pu3", T.uo[:], T.uf[:], T.pf[:, 6:7], Op.add, T.pf[:, 7:8], Op.add)
-    fill("dt0", T.dt3[:], 0.0)
-    fill("pa2", T.pa2[:, 0:160:4], 0.0)
-    ts("cti2", "cti", T.cti[:], T.cti[:], 63, Op.bitwise_and)
-    fill("abk", T.ab[:, :, 0:150:3], 1 / EPS)
-    quant("uq0", "ut", T.uq0[:], T.us0[:], T.ut[:])
-    fill("dp0", T.dp[:], 0.0)
+    ts("kf", "pk0", T.pf[:, 8:9], T.pi[:, 4:5], -1024.0, Op.add)
     fill("cd0_", T.cde[:], 1)
-    ts("v0m", "tb1 tb2 g0", T.tbb[:], T.tb[:, 0:50], T.pf[:, 0:1], Op.not_equal)
-    ts("ct0", "cti2", T.ct[:], T.cti[:], -U / 512, Op.mult, 64.40625 * U, Op.add)
-    ts("ct1", "cti2", T.so[:, 0, 0:50], T.cti[:], 32, Op.is_ge, -224 * U / 512, Op.mult)
+    quant("ptqz", "zz", T.ptq[:, 64:192], T.pts[:, 64:192], T.zz[:])
+    ts("uo", "uf pu2 pu3", T.uo[:], T.uf[:], T.pf[:, 6:7], Op.add, T.pf[:, 7:8], Op.add)
+    ts("v0m", "ct0 g0", T.tbb[:], T.ct[:, 0, :], T.pf[:, 0:1], Op.not_equal)
+    ts("c0a", "c0i g1", T.c0[:, 1, :], T.c0[:, 0, :], T.pf[:, 2:3], Op.is_equal)
+    quant("uq0", "ut", T.uq0[:], T.us0[:], T.ut[:])
+    ts("c0n", "c0i g1", T.c0[:, 2, :], T.c0[:, 0, :], T.pf[:, 2:3], Op.not_equal)
+    tt("val1", "v0m v0n", T.val1[:], T.val1[:], T.tbb[:], Op.mult)
+    tt("c0c c0i", "c0a ct1", T.c0[:, 0, 0:8], T.c0[:, 1, 0:8], T.ct[:, 1, 14:50:5], Op.mult)
     do("v", "uq0 uo", "uq", lambda: V.tensor_copy(T.uq[:].bitcast(dt.uint32), T.uq0[:].bitcast(dt.uint32).indirect(T.uo[:])))
     do("s", "uq0 uo", "uq", lambda: S.activation(T.us[:], T.us0[:].indirect(T.uo[:]), AF.Copy), more=True)
 
@@ -226,38 +237,79 @@ def rank_program(g, core, T, topo):
 
     def places(h):
         for i in range(5):
-            (copy if i < 4 else act)("xt%d" % h, "xin%d" % h, T.xt[:, h, i, :, :], T.xin[:, 32 * h:32 * h + 32, 4 * i:4 * i + 4], more=True)
+            (copy if i < 3 + h else act)("xt%d" % h, "xin%d" % h, T.xt[:, h, i, :, :], T.xin[:, 32 * h:32 * h + 32, 4 * i:4 * i + 4], more=True)
+
+    def turner(sl, c):
+        for a, w in ((0, 64), (64, 64), (128, 32)):
+            act("wat", "wm", T.wat[sl, a:a + w, :], T.wm[lo, 0:w, :], c, more=True)
 
     places(1)
-    quant("ptqz", "zz", T.ptq[:, 64:192], T.pts[:, 64:192], T.zz[:])
-    tt("ct", "ct0 ct1", T.ct[:], T.ct[:], T.so[:, 0, 0:50], Op.add)
+    act("c0b", "c0a", T.c0[:, 3, 0:9], T.c0[:, 1, 0:9], -1024.0)
+    tt("c0d", "c0a ct3", T.c0[:, 4, 0:8], T.c0[:, 1, 0:8], T.ct[:, 3, 14:50:5], Op.mult)
+    tt("c0", "c0n c0c", T.c0[:, 2, 1:9], T.c0[:, 2, 1:9], T.c0[:, 0, 0:8], Op.max)
     state(1)
     places(0)
     do("y", "xin0", "wq", lambda: Y.dma_start(T.wq[:].bitcast(dt.uint8), T.wc[:]), "dw", 16, more=True)
     do("y", "", "wq", lambda: Y.dma_start(T.wsc[:], T.ws[:]), "dw", 16, more=True)
     do("y", "", "vt", lambda: Y.dma_start(T.vt[:], T.v[:]), "dv", 16)
-    ts("v0n", "v0i", T.val1[:], T.val1[:], 66.5, Op.add, U, Op.mult)
-    ts("c0a", "c0i g1", T.c0[:, 1, :], T.c0[:, 0, :], T.pf[:, 2:3], Op.is_equal)
-    fill("ne0", T.ne[:, :, 0:64:16], 0.0)
+    tt("c1", "c0b c0d", T.c0[:, 3, 1:9], T.c0[:, 3, 1:9], T.c0[:, 4, 0:8], Op.add)
     state(0)
+    turner(lo, 1.0)
 
-    def constants0():
-        tt("val1", "v0m v0n", T.val1[:], T.val1[:], T.tbb[:], Op.mult)
-        ts("c0b", "c0a", T.c0[:, 0, 0:9], T.c0[:, 1, 0:9], -1024 * U, Op.mult)
-        tt("c0c", "c0a ct", T.c0[:, 2, 0:8], T.c0[:, 1, 0:8], T.ct[:, 14:50:5], Op.mult)
-        fill("dg1", T.dt3[:, 1, 14:150:15], 1.0)
-        fill("pa16", T.pa16[:], 1.0)
-
-    def constants1():
-        tt("c0", "c0b c0c", T.c0[:, 0, 1:9], T.c0[:, 0, 1:9], T.c0[:, 2, 0:8], Op.add)
-        ts("n60b", "n60", T.n60[:], T.n60[:], 63, Op.bitwise_and)
-
-    def constants3():
-        for sl, c in ((lo, -U / 128), (up, 5 * U)):
-            for a, w in ((0, 64), (64, 64), (128, 32)):
-                act("wat", "wm", T.wat[sl, a:a + w, :], T.wm[lo, 0:w, :], c, more=True)
-        for k, a, b in (("dgp", 0, 9), ("dgp", 9, 17), ("dgr", 0, 8), ("dgr", 8, 15)):
+    def zeros():
+        for k, a, b in (("dgp", 0, 10), ("dgp", 10, 19), ("dgr", 0, 8), ("dgr", 8, 15)):
             act("dg0", "zz", T[k][:, a:b, :, :, :], T.zz[:, 0:40 * (b - a)], more=True)
+            yield
+
+    def numbers():
+        ts("d16a", "d16i", T.d16i[:], T.d16i[:], 15, Op.bitwise_and)
+        yield
+        ts("n80b", "n80", T.n80[:], T.n80[:], 63, Op.bitwise_and)
+        yield
+        ts("nb80", "n80b", T.nb80[:], T.n80[:], 4, Op.logical_shift_right)
+        yield
+        ts("n5", "n80b", T.inc[:, 0:4], T.n80[:, 0:4], 5.0, Op.mult, -160.0, Op.add)
+        yield
+        ts("i16", "d16a", T.i16[:], T.d16i[:], 0, Op.is_equal)
+        yield
+        ts("d16b", "d16a", T.d16[:, 0, :], T.d16i[:], 0, Op.is_equal, 4 * LOW, Op.mult)
+        yield
+        ts("d16c", "d16a", T.d16[:, 1, :], T.d16i[:], 1, Op.is_equal, LOW, Op.mult)
+        yield
+        ts("cb", "d16a", T.pf[:, 4:5], T.d16i[:, 15:16], 0, Op.not_equal, LOW, Op.mult)
+        yield
+        for nb in range(4):
+            ts("msk0", "nb80", T.msk[:, nb, :], T.nb80[:], nb, Op.is_equal, more=True)
+            yield
+        for h, sl in halves:
+            for e in range(4):
+                m, c = 16 * (7 - 4 * h - e), 8 * ((e + 1) % 2)
+                act("wt2", "i16 w3z", T.w3[sl, 2, m:m + 16, e], T.i16[sl, c:c + 16], more=True)
+        yield
+        act("msk", "msk0", T.msk[:, :, 40:60], T.msk[:, :, 40:60], 5.0)
+        act("msk", "msk0", T.msk[:, :, 60:80], T.msk[:, :, 60:80], 0.25, more=True)
+
+    def tiles():
+        for b in range(4):
+            quant("e%d" % b, "et", T.eqc[:, 128 * b:128 * b + 128], T.eqs[:, 128 * b:128 * b + 128], T.et[:, 3 - b:515 - b])
+            yield
+        fillers(99)
+        for j in (0, 1, 2):
+            rd = " ".join(k for k in last if k.startswith("wt%d" % j))
+            quant("qwt%d" % j, rd, T.cq3[:, 128 * j:128 * j + 128], T.cs3[:, 128 * j:128 * j + 128], T.w3[:, j, :, :])
+            yield
+
+    blank, rest, big = zeros(), numbers(), tiles()
+
+    def fillers(n):
+        for _ in range(n):
+            next(rest, None)
+
+    def W3(j):
+        return T.cq3[:, 128 * j:128 * j + 128], T.cs3[:, 128 * j:128 * j + 128]
+
+    ps = [T["ps%d" % i] for i in range(8)]
+    partner_of = lambda t: T.cores[rank ^ PARTNER[t]]
 
     def scores(h, banks):
         for j, k in enumerate(banks):
@@ -272,157 +324,103 @@ def rank_program(g, core, T, topo):
             else:
                 act("sc%d" % h, "ps%d" % banks[1], out, ps[banks[1]][32 * i - 32:32 * i, 0:32], more=True)
 
-    def constants2():
-        ts("ngm", "g20", T.ngm[:, 0, :], T.g20[:, 0:4], -U / 512, Op.mult, CODE / 512 * U, Op.add)
-        yield
-        ts("n5", "n60b", T.inc[:, 0:4], T.n60[:, 0:4], 5.0, Op.mult, -160.0, Op.add)
-        yield
-        fill("dg1", T.dt3[:, 1, 29:30], -7.0)
-        yield
-        fill("dg1", T.dt3[:, 1, 149:150], 64.0, more=True)
-        yield
-        fill("pa16", T.pa16[:, 0:64:16], 0.0)
-        yield
-        ts("nb60", "n60b", T.nb60[:], T.n60[:], 4, Op.logical_shift_right)
-        yield
-        ts("d16a", "d16i", T.d16i[:], T.d16i[:], 15, Op.bitwise_and)
+    def unpack():
+        for b in range(4):
+            mm("ps%d" % b, "xq0 xq1 e%d" % b, (ps[b][:, 0:320], T.eqc[:, 128 * b:128 * b + 128], T.eqs[:, 128 * b:128 * b + 128], T.xq[:, 0:320], T.xs[:, 0:320]))
         yield
         for b in range(4):
-            quant("e%d" % b, "et", T.eqc[:, 128 * b:128 * b + 128], T.eqs[:, 128 * b:128 * b + 128], T.et[:, 3 - b:515 - b])
+            act("tp", "ps%d" % b, T.tp[:, 320 * b:320 * b + 320], ps[b][:, 0:320], 0.5, more=b > 0)
             yield
-            yield
-        ts("i16", "d16a", T.i16[:], T.d16i[:], 0, Op.is_equal)
-        yield
-        for h, sl in halves:
-            for e in range(4):
-                m, c = 16 * (7 - 4 * h - e), 8 * ((e + 1) % 2)
-                act("wt2", "i16 w3z", T.w3[sl, 2, m:m + 16, e], T.i16[sl, c:c + 16], more=True)
-            yield
-        for nb in range(4):
-            ts("msk", "nb60", T.msk[:, nb, :], T.nb60[:], nb, Op.is_equal, more=True)
-            yield
-        ts("d16b", "d16a", T.d16[:, 0, :], T.d16i[:], 0, Op.is_equal, 4 * LOW, Op.mult)
-        yield
-        ts("d16c", "d16a", T.d16[:, 1, :], T.d16i[:], 1, Op.is_equal, LOW, Op.mult)
-        yield
-        ts("cb", "d16a", T.pf[:, 4:5], T.d16i[:, 15:16], 0, Op.not_equal, LOW, Op.mult)
-        yield
-        yield
-        ts("msk", "msk", T.msk[:, :, 40:60], T.msk[:, :, 40:60], 0.625, Op.mult)
-        yield
-        for j in (0, 2, 1):
-            rd = " ".join(k for k in last if k.startswith("wt%d" % j))
-            quant("qwt%d" % j, rd, T.cq3[:, 128 * j:128 * j + 128], T.cs3[:, 128 * j:128 * j + 128], T.w3[:, j, :, :])
-            yield
-            yield
-
-    def constants4():
-        tt("d16", "d16b d16c", T.d16[:, 0, :], T.d16[:, 0, :], T.d16[:, 1, :], Op.subtract)
-
-    fill("ne0", T.ne[:, :, 15:64:16], 1.0, more=True)
-    rest = constants2()
-
-    def fillers(n):
-        for _ in range(n):
-            next(rest, None)
-
-    def W3(j):
-        return T.cq3[:, 128 * j:128 * j + 128], T.cs3[:, 128 * j:128 * j + 128]
-
-    ps = [T["ps%d" % i] for i in range(8)]
-    partner_of = lambda t: T.cores[rank ^ PARTNER[t]]
+            if b < 2:
+                act("tw", "ps%d" % b, T.tw[:, 320 * b:320 * b + 320], ps[b][:, 0:320], 0.5, more=b > 0)
+                yield
 
     for t in range(3):
         final = t == 2
         if t == 0:
             scores(1, (4, 5))
         scores(0, (6, 7))
-        if t == 0:
-            constants0()
         bring(1, (4, 5))
         bring(0, (6, 7))
-
-        def unpack():
-            for b in range(4):
-                mm("ps%d" % b, "xq0 xq1 e%d" % b, (ps[b][:, 0:320], T.eqc[:, 128 * b:128 * b + 128], T.eqs[:, 128 * b:128 * b + 128], T.xq[:, 0:320], T.xs[:, 0:320]))
-                act("tp", "ps%d" % b, T.tp[:, 320 * b:320 * b + 320], ps[b][:, 0:320], 0.5, more=b > 0)
-                yield
-                if b < 2:
-                    act("tw", "ps%d" % b, T.tw[:, 320 * b:320 * b + 320], ps[b][:, 0:320], 0.5, more=b > 0)
-                    yield
-
         planes = unpack()
         if t == 0:
-            constants3()
+            turner(up, 16.0)
         else:
-            list(planes)
+            for j in range(4):
+                next(planes)
         key = lambda a, b: T.sc[lo, :, a:b, 3]
         for s in range(1, 5):
-            tt("cm", "sc0 sc1", T.cm[lo, s - 1, :, 0:5 - s], key(s, 5), key(0, 5 - s), Op.is_gt, more=True)
-            tt("cm", "sc0 sc1", T.cm[lo, s - 1, :, 5 - s:5], key(0, s), key(5 - s, 5), Op.is_ge, more=True)
+            tt("cm%d" % s, "sc0 sc1", T.cm[lo, s - 1, :, 0:5 - s], key(s, 5), key(0, 5 - s), Op.is_gt)
+            tt("cm%d" % s, "sc0 sc1", T.cm[lo, s - 1, :, 5 - s:5], key(0, s), key(5 - s, 5), Op.is_ge, more=True)
+        tt("a20", "cm1 cm2", T.a2[lo, 0, :], T.cm[lo, 0, :, :], T.cm[lo, 1, :, :], Op.add)
         for b in range(3):
-            ts("hb", "sc0 sc1 hb0", T.hb[lo, 1 + b:160:4], T.sc[lo, :, :, b], 0.0, Op.is_gt, more=b > 0)
-        tt("a2", "cm", T.a2[lo], T.cm[lo, 0:2, :, :], T.cm[lo, 2:4, :, :], Op.add)
-        fill("abb1", T.ab[:, 1, 2:150:3], EPS)
-        if t == 0:
-            constants1()
-        scan("pay", "pa2 hb pay0", T.pay[lo, 0:160], T.pa2[lo], T.hb[lo])
-        for j in range(2):
-            tt("rk", "a2", T.rk[lo, 40 * j:40 * j + 40], T.a2[lo, 0, :], T.a2[lo, 1, :], Op.add, more=j > 0)
-
-        def sym(i):
-            ts("rt2", "pay rt20", T.rt2[up, 0:2, 16 * i:16 * i + 20:5], T.pay[lo, 3 + 4 * i:160:20], -8.0 * i, Op.add, more=i > 0)
-
-        if t == 0:
-            ts("g20a", "n60b", T.g20[:], T.n60[:, 0:20], 32, Op.is_ge, 224.0, Op.mult)
-        for i in range(3):
-            sym(i)
-        if t == 0:
-            tt("g20", "n60b g20a", T.g20[:], T.g20[:], T.n60[:, 0:20], Op.add)
-        for r in range(5):
-            ts("eqr%d" % r, "rk", T.eqr[lo, r, :], T.rk[lo], 4.0 - r, Op.is_equal, 64.0, Op.mult)
-        for r in range(5):
-            scan("prb", "eqr%d pay" % r, T.prb[lo, :, r], T.eqr[lo, r, :], T.pay[lo, 3:320:4], more=True, ops=LATCH)
-
+            ts("hb", "sc0 sc1 hb0", T.hb[lo, 1 + b:160:4], T.sc[lo, :, :, b], 0.0, Op.is_gt, (0.0625, 0.25, 0.5)[b], Op.max, more=b > 0)
+        tt("a21", "cm3 cm4", T.a2[lo, 1, :], T.cm[lo, 2, :, :], T.cm[lo, 3, :, :], Op.add)
+        fillers(2)
+        scan("pay", "pa hb", T.pay[lo], T.hb[lo], T.pa[lo])
+        for h, sl in halves:
+            tt("rk", "a20 a21", T.rk[sl], T.a2[lo, 0, :], T.a2[lo, 1, :], Op.add, more=h > 0)
         if t == 0:
             quant("wa", "wat", T.waq[:], T.was[:], T.wat[:])
-            tt("i20b", "g20 i20", T.i20[:], T.i20[:], T.g20[:], Op.add)
-        sym(3)
-        sym(4)
-        copy("rth", "prb rt0", T.rt[lo, 0:2, 0:4, 0:20:4], T.prb[lo, 44:80:5, :])
-        tt("rtl", "prb rt0", T.rt[up, 0:2, 0:4, 0:20:4], T.prb[lo, 4:40:5, :], T.prb[lo, 44:80:5, :], Op.subtract)
-        fillers(2)
-        quant("rq", "rth rtl", T.rq[:], T.rs[:], T.rt[:])
-        mm("ps5", "wa rq", *[(ps[5][:, 0:128], T.waq[:, w:w + 128], T.was[:, w:w + 128], T.rq[:, c:c + 128], T.rs[:, c:c + 128])
-                             for w, c in ((0, 0), (32, 22))])
-        if t == 0:
-            ts("ctp", "i20b", T.ctp[:], T.i20[:], -U / 512, Op.mult, 64.40625 * U, Op.add)
+        for j in range(2):
+            act("pd", "pay pd0", T.pd[lo, j:80:2], T.pay[lo, 3:160:4], 2.0 * j - 1, more=j > 0)
+        for i in range(5):
+            act("rt2", "pay rt20", T.rt2[lo, 0:2, 16 * i:16 * i + 20:5], T.pay[lo, 3 + 4 * i:160:20], U, more=i > 0)
+            act("rt2", "rk rt20", T.rt2[up, 2:4, 16 * i:16 * i + 20:5], T.rk[up, i:40:5], -0.0625, more=True)
+        const("abb1", T.ab[:, 1, 2:150:3], 50, EPS)
+        for r in range(5):
+            ts("eqr%d" % r, "rk eq0", T.eqr[:, r, 1:80:2], T.rk[:], 4.0 - r, Op.not_equal)
+        for r in range(5):
+            scan("prb", "eqr%d pd" % r, T.prb[:, :, r], T.eqr[:, r, :], T.pd[:], more=True)
+
         quant("rq2", "rt2", T.rq2[:], T.rs2[:], T.rt2[:])
+        act("rth", "prb rt0", T.rt[up, 2:4, 0:4, 0:20:4], T.prb[up, 9:80:10, :])
+        copy("rtl", "prb rt0", T.rt[lo, 0:2, 0:4, 0:20:4], T.prb[lo, 9:80:10, :])
+        list(planes if t else [])
+        fillers(3)
+        quant("rq", "rth rtl", T.rq[:], T.rs[:], T.rt[:])
+        mm("ps5", "wa rq", *[(ps[5][:, 0:130], T.waq[:, w:w + 128], T.was[:, w:w + 128], T.rq[:, c:c + 130], T.rs[:, c:c + 130])
+                             for w, c in ((0, 0), (32, 22))])
         for h in range(2):
             mm("ps%d" % (6 + h), "wa rq2", (ps[6 + h][:, 0:128], T.waq[:, 32 * h:32 * h + 128], T.was[:, 32 * h:32 * h + 128], T.rq2[:, 22 * h:22 * h + 128], T.rs2[:, 22 * h:22 * h + 128]))
-        fillers(4)
-        scan("so0", "c0 ps5", T.so[:, 0, 141:150], T.c0[:, 0, 0:9], ps[5][:, 4:45:5], ops=(Op.add, Op.max))
-        tt("tb1", "ps5 ct", T.tb[:, 10:50], ps[5][:, 0:40], T.ct[:, 10:50], Op.add)
-        tt("tb2", "ps5 ct", T.tb[:, 0:10], ps[5][:, 30:40], T.ct[:, 0:10], Op.add)
+        fillers(7)
+        word = lambda a, b: T.dt3[:, 0, 3 * a + 2:3 * b:3]
+        scan("so0", "c0 ps5", T.so[:, 0, 141:150], T.c0[:, 2, 0:9], ps[5][:, 4:45:5], ops=(Op.mult, Op.max))
+        tt("tb1", "ps5 ct1 dt0", word(10, 50), ps[5][:, 0:40], T.ct[:, 1, 10:50], Op.mult)
+        tt("tk1", "ps5 ct2", T.dt3[:, 0, 30:150:3], ps[5][:, 0:40], T.ct[:, 2, 10:50], Op.mult)
+        tt("tc1", "ps5 ct3", T.dt3[:, 1, 32:150:3], ps[5][:, 84:124], T.ct[:, 3, 10:50], Op.add)
+        scan("sw0", "c1 ps5", T.so[:, 14, 141:150], T.c0[:, 3, 0:9], ps[5][:, 88:129:5], ops=(Op.add, Op.max))
+        act("tc3", "tc1", T.dt3[:, 1, 30:150:3], T.dt3[:, 1, 32:150:3], -1 / EPS)
+        act("tb2", "tb1", word(0, 10), word(40, 50))
+        for k, j, c in (("tk1", 0, 0), ("tc1", 1, 2), ("tc3", 1, 0)):
+            act(k + "b", k, T.dt3[:, j, c:30:3], T.dt3[:, j, 120 + c:150:3])
+
         def cd(n):
-            ts("cd%d" % n, "so%d ngm cd0_" % n, T.cde[:, 14 - n:64:16], T.ngm[:, 0, :], T.so[:, n, 149:150], Op.subtract, 512 / U, Op.mult)
+            ts("cd%d" % n, "sw%d gc cd0_" % n, T.cde[:, 14 - n:64:16], T.grp[:, 0, :], T.so[:, 14 + n, 149:150], Op.subtract)
 
         def drew(n):
+            if n == 11:
+                act("gq", "gc sg11", T.grp[:, 1, :], T.grp[:, 0, :], -1.0, bias=T.so[:, 28, 149:150], func=AF.Square)
             for k, c in (("po0", 4), ("po1", 1)):
-                ts(k, "gc0 gc1 sg%d" % n, T.pt[:, 52 - 4 * n + c:256:64], T.ngm[:, 2, :], T.so[:, 3 + n, 149:150], Op.is_equal, more=n > 11)
+                if n == 11:
+                    act(k, "gq", T.pt[:, 8 + c:256:64], T.grp[:, 1, :], -1.0, bias=1.0, func=AF.Relu)
+                else:
+                    ts(k, "gc sg%d" % n, T.pt[:, 52 - 4 * n + c:256:64], T.grp[:, 0, :], T.so[:, 17 + n, 149:150], Op.is_equal, more=True)
 
-        def marks(n):
-            s, so, a = T.so[:, n, 149:150], "so%d" % n, n % 2
-            if 0 < n < 12:
-                act("sq%d" % a, "tb1 tb2 " + so, T.sq[:, a, :], T.tb[:, 0:50], -1.0, bias=s, func=AF.Square)
+        def far(n):
+            act("sqp%d" % (n % 3), "tbp so%d" % n, T.sqp[:, n % 3, :], T.tbp[:, 0, :], -1.0, bias=T.so[:, n, 149:150], func=AF.Square)
+
+        def other(n):
+            act("ne", "sqp%d ne0" % (n % 3), T.ne[:, :, 14 - n:64:16], T.sqp[:, n % 3, :], func=AF.Sign, more=n > 0)
+
+        def steps(n):
+            s, so, a = T.so[:, 14 + n, 149:150], "sw%d" % n, n % 2
             if n == 0:
                 act("dp", "zf dp0 " + so, T.dp[:, 13:64:16], T.zf[:], bias=s)
             else:
                 act("dp", "tt%d %s" % (1 - a, so), T.dp[:, 13 - n:64:16], T.tt4[:, 1 - a, :], -1.0, bias=s, more=True)
             if n < 13:
-                act("sqp%d" % (n % 3), "tbp " + so, T.sqp[:, n % 3, :], T.tbp[:], -1.0, bias=s, func=AF.Square)
                 act("tt%d" % a, "zf " + so, T.tt4[:, a, :], T.zf[:], bias=s)
-                act("ne", "sqp%d ne0" % (n % 3), T.ne[:, :, 14 - n:64:16], T.sqp[:, n % 3, :], func=AF.Sign, more=n > 0)
 
         def undrawn(n):
             a = n % 2
@@ -433,112 +431,126 @@ def rank_program(g, core, T, topo):
 
         for n in range(1, 14):
             s, so = T.so[:, n - 1, 149:150], "so%d" % (n - 1)
-            j = 10 if n < 5 else 5 if n < 10 else 0
-            vk, vv = ("val1", T.val1) if n < 3 else ("vl%d" % (n % 2), T.val[:, n % 2, :])
-            if n > 1:
-                marks(n - 1)
-            w = n % 2
-            ts("aba%d" % w, vk + " abk " + so, T.ab[:, w, 3 * j + 1:150:3], T.val1[:, j:50] if n < 3 else T.val[:, n % 2, j:50], s, Op.is_lt, EPS, Op.add)
+            j, w = 10 if n < 5 else 5 if n < 10 else 0, n % 2
+            vk = "val1" if n < 3 else "vl%d" % w
+            if 1 < n < 13:
+                act("sq%d" % (1 - w), "tb1 tb2 " + so, T.sq[:, 1 - w, :], word(0, 50), -1.0, bias=s, func=AF.Square)
+            late = range(3) if n == 3 else [n - 1] if n > 3 else []
+            for m in late:
+                far(m)
+            steps(n - 1)
+            if n > 2:
+                next(planes if n > 6 else blank, None)
+            for m in late:
+                other(m)
+            ts("aba%d" % w, vk + " abk " + so, T.ab[:, w, 3 * j + 1:150:3], T.val1[:, j:50] if n < 3 else T.val[:, w, j:50], s, Op.is_lt, EPS, Op.add)
             if n == 1:
-                tt("dtb", "tb1 tb2 tb0 dt0", T.dt3[:, 0, 2:150:3], T.tb[:, 0:50], T.tb[:, 1:51], Op.subtract)
-                tt("tbm", "val1 tb1 tb2", T.tbb[:], T.val1[:], T.tb[:, 0:50], Op.is_ge)
+                tt("tbm", "val1 tb1", T.tbb[:, 10:50], T.val1[:, 10:50], word(10, 50), Op.is_ge)
                 for h, sl in halves:
-                    tt("tbp", "ps%d ctp" % (6 + h), T.tbp[sl], ps[6 + h][sl, 0:20], T.ctp[sl], Op.add, more=h > 0)
-                marks(0)
+                    tt("tbq", "ps%d cg" % (6 + h), T.tbp[sl, 1, :], ps[6 + h][sl, 44:64], T.cg[sl], Op.add, more=h > 0)
             else:
-                ts("abb%d" % w, "tbb " + so, T.ab[:, w, 3 * j + 2:150:3], T.tbb[:, j:50], s, Op.is_equal, EPS, Op.add)
-            if 2 <= n < 11:
-                fillers(2)
+                ts("abb%d" % w, ("tbb " if n < 5 else "tbd ") + so, T.ab[:, w, 3 * j + 2:150:3], T.tbb[:, j:50], s, Op.is_equal, EPS, Op.add)
+            if n == 2:
+                for h, sl in halves:
+                    tt("tbp", "ps%d tbq" % (6 + h), T.tbp[sl, 0, :], ps[6 + h][sl, 0:20], T.tbp[sl, 1, :], Op.mult, more=h > 0)
+            elif n > 2:
+                next(big, None)
+            if n == 4:
+                undrawn(1)
             if n == 11:
                 cd(10)
             if n == 12:
                 ts("po0", "ca pt0", T.pt[:, 0:256:4], T.ca[:], 0, Op.is_equal)
                 ts("po1", "ca pt0", T.pt[:, 1:252:4], T.ca[:, 1:64], 0, Op.is_equal)
+                bulk = count["v"]
             if 2 <= n < 13:
-                old = T.val1[:] if n < 3 else T.val[:, n % 2, :]
-                tt("vl%d" % ((n + 1) % 2), vk + " sq%d" % ((n - 1) % 2), T.val[:, (n + 1) % 2, :], old, T.sq[:, (n - 1) % 2, :], Op.min)
+                tt("vl%d" % (1 - w), vk + " sq%d" % (1 - w), T.val[:, 1 - w, :], T.val1[:] if n < 3 else T.val[:, w, :], T.sq[:, 1 - w, :], Op.min)
             if n == 13:
+                need("v", "v", bulk)
                 drew(12)
-            group = lambda: scan("sg%d" % n, "aba%d abb%d dg1" % (w, w), T.so[:, 3 + n, :], T.ab[:, w, :], T.dt3[:, 1, :])
+
+            def search(name, rd, row, d):
+                scan(name, "aba%d abb%d %s" % (w, w, rd), T.so[:, row, 3 * j:150], T.ab[:, w, 3 * j:150], T.dt3[:, d, 3 * j:150])
+
             if n == 13:
-                group()
+                search("sg13", "dg1", 30, 2)
                 scan("pe", "pa16 po0", T.pe[:], T.pa16[:], T.pt[:, 0:256:4])
-            scan("so%d" % n, "aba%d abb%d dtb" % (w, w), T.so[:, n, 3 * j:150], T.ab[:, w, 3 * j:150], T.dt3[:, 0, 3 * j:150])
+            search("so%d" % n, "tb1 tk1" if n < 5 else "tb2 tk1b", n, 0)
             if n == 1:
-                tt("tbb", "tbm", T.tbb[:], T.tbb[:], T.tb[:, 0:50], Op.mult)
+                tt("tbb", "tbm", T.tbb[:, 10:50], T.tbb[:, 10:50], word(10, 50), Op.mult)
+                act("tbd", "tb2", T.tbb[:, 0:10], word(0, 10))
             if n == 11:
-                ts("ca", " ".join("cd%d" % m for m in range(11)), T.ca[:], T.cde[:], 256 + 31, Op.bitwise_and)
+                ts("ca", " ".join("cd%d" % m for m in range(11)), T.ca[:], T.cde[:], 15, Op.bitwise_and)
             if n in (11, 12):
-                group()
+                search("sg%d" % n, "dg1", 17 + n, 2)
+            search("sw%d" % n, "tc1 tc3" if n < 5 else "tc1b tc3b", 14 + n, 1)
             if n < 11:
                 cd(n - 1)
             if n == 12:
                 drew(11)
-            if 2 <= n < 12 or n == 13:
-                undrawn(n - 2 if n < 12 else 10)
-            if n < 11:
-                fillers(2)
-            if n >= 5:
-                next(planes, None)
-            if t == 0 and n == 10:
-                fillers(99)
+            if n >= 3:
+                undrawn(0 if n == 3 else n - 2)
         s = T.so[:, 13, 149:150]
-        marks(13)
+        steps(13)
         need("v", "v", reads["po0"]["v"])
         drew(13)
-        ts("ne13", "so13 tbp ne0", T.ne[:, :, 1:64:16], T.tbp[:], s, Op.not_equal)
-        undrawn(11)
         for e in range(4):
-            ts("po3", "sg13 pe pt0", T.pt[:, 256 + 65 * e:257 + 65 * e], T.so[:, 16, 149:150], T.ngm[:, 2, e:e + 1], Op.is_equal, T.pe[:, 16 * e + 15:16 * e + 16], Op.add, more=e > 0)
+            ts("po3", "sg13 pe pt0", T.pt[:, 256 + 65 * e:257 + 65 * e], T.so[:, 30, 149:150], T.grp[:, 0, e:e + 1], Op.is_equal, T.pe[:, 16 * e + 15:16 * e + 16], Op.add, more=e > 0)
+            if e == 1:
+                ts("ne13", "so13 tbp ne0", T.ne[:, :, 1:64:16], T.tbp[:, 0, :], s, Op.not_equal)
 
         def before(i):
             scan("uopp", "ne ne13 dp", T.uop[:, 0, i, :], T.ne[:, i, :], T.dp[:], more=i > 0)
 
         undrawn(12)
-        for i in range(3):
-            before(i)
+        before(0)
+        before(1)
         quant("ptq", "po0 po1 po3 ptqz", T.ptq[:, 0:128], T.pts[:, 0:128], T.pt[:])
         mm("ps4", "ptq ptqz qwt0 qwt1", (ps[4][:, 0:128], *W3(0), T.ptq[:, 0:128], T.pts[:, 0:128]),
            (ps[4][:, 0:128], *W3(1), T.ptq[:, 64:192], T.pts[:, 64:192]))
         tt("fl und1", "und0 ne13", T.und[:, 1, :], T.und[:, 0, :], T.ne[:, :, 1:64:16], Op.mult)
-        before(3)
-        before(4)
+        for i in range(2, 5):
+            before(i)
+        form_of = {"p": (0, 0, (15, 16, 32, 896), T.dgp, 0, 190), "q": (1, 4, (15, -16), T.dgr, 190, 150)}
 
         def digits(x):
-            for d, m in enumerate((15, 240, 256) if x == "p" else (15, -16)):
-                j = int(x == "q")
-                ts("di" + x, "v2" + x, T.dgi[:, 3 * j + d, :], T.v2[:, j, :], m, Op.bitwise_and, more=d > 0)
+            j, d0, masks = form_of[x][:3]
+            for d, m in enumerate(masks):
+                ts("di" + x, "v2" + x, T.dgi[:, d0 + d, :], T.v2[:, j, :], m, Op.bitwise_and, more=d > 0)
 
         def spread(x, blocks=range(4)):
-            j, nd = (1, 2) if x == "q" else (0, 3)
+            j, d0, masks, tile = form_of[x][:4]
+            nd = len(masks)
             for nb in blocks:
-                tt("dg" + x, "di%s msk dg0" % x, T[("dgp", "dgr")[j]][:, nb // 2:2 * nd:2, :, nb % 2, :], T.dgi[:, 3 * j:3 * j + nd, :], T.msk[:, nb, 0:20 * nd], Op.mult, more=nb > 0)
+                tt("dg" + x, "di%s msk msk0 dg0" % x, tile[:, nb // 2:2 * nd:2, :, nb % 2, :], T.dgi[:, d0:d0 + nd, :], T.msk[:, nb, 0:20 * nd], Op.mult, more=nb > 0)
 
         def form(x, k):
-            j, nd = (1, 2) if x == "q" else (0, 3)
-            c, w = 170 * j, 170 - 20 * j
-            quant("dq" + x, "dg" + x, T.dgq[:, c:c + w], T.dgs[:, c:c + w], T[("dgp", "dgr")[j]][:])
-            mm("ps%d" % k, "dq%s qwt2" % x, *[(ps[k][:, 0:128], *W3(2), T.dgq[:, c + 20 * d:c + 20 * d + 128], T.dgs[:, c + 20 * d:c + 20 * d + 128]) for d in range(nd)])
+            masks, tile, c, w = form_of[x][2:]
+            quant("dq" + x, "dg" + x, T.dgq[:, c:c + w], T.dgs[:, c:c + w], tile[:])
+            mm("ps%d" % k, "dq%s qwt2" % x, *[(ps[k][:, 0:128], *W3(2), T.dgq[:, c + 20 * d:c + 20 * d + 128], T.dgs[:, c + 20 * d:c + 20 * d + 128]) for d in range(len(masks))])
 
         act("pr0", "fl", T.pr[:], T.und[:, 1, :], 1024.0, bias=-160.0)
         for e in range(4):
             scan("inc", "pa16 fl n5", T.inc[:, 4 + e:24:4], T.pa16[:, 1:6], T.und[:, 1, e:20:4], more=e > 0, initial=T.inc[:, e:e + 1])
-        ts("v2p", "uopp", T.v2[:, 0, :], T.uop[:, 0, :, 13:64:16], -512 / U, Op.mult, CODE, Op.add)
+        ts("v2p", "uopp kf", T.v2[:, 0, :], T.uop[:, 0, :, 13:64:16], 8.0, Op.mult, T.pf[:, 8:9], Op.add)
         for i in range(5):
             scan("uopq", "ne ne13 ps4", T.uop[:, 1, i, :], T.ne[:, i, :], ps[4][:, 0:64], more=i > 0)
             if i == 2:
                 tt("pr", "pr0 inc", T.pr[:], T.pr[:], T.inc[:, 0:20], Op.min)
-        digits("p")
         tt("v2q", "uopq pr", T.v2[:, 1, :], T.uop[:, 1, :, 15:64:16], T.pr[:], Op.add)
-        spread("p", (0, 1))
+        digits("p")
         digits("q")
-        spread("p", (2, 3))
+        spread("p", (0,))
         spread("q")
-        form("p", 5)
+        spread("p", (1,))
         form("q", 6)
-        copy("ofp", "ps5", T.ofp[:], ps[5][:, 0:20])
+        spread("p", (2, 3))
         if t == 0:
-            constants4()
+            tt("d16", "d16b d16c", T.d16[:, 0, :], T.d16[:, 0, :], T.d16[:, 1, :], Op.subtract)
+        ts("ofq", "ps6", T.ofq[:], ps[6][:, 0:20], 160.0, Op.add)
+        form("p", 5)
+        do("v", "ofq phr", "row", lambda: V.tensor_copy(T.row[:].indirect(T.ofq[:]), T.phr[:]))
+        copy("ofp", "ps5", T.ofp[:], ps[5][:, 0:20])
         for b in (2, 3):
             act("tq%d" % b, "ofp tp", T.tq[:, 320 * b:320 * b + 320], T.tp[:, 320 * b:320 * b + 320].indirect(T.ofp[:]))
 
@@ -546,25 +558,22 @@ def rank_program(g, core, T, topo):
             cs = slice(320 * b + 160 * h, 320 * b + 160 * h + 160)
             tt("tq%d" % b, "ofp tp tw", T.tq[:, cs], T.tp[:, 320 * b:320 * b + 320].indirect(T.ofp[:, 10 * h:10 * h + 10]), T.tw[:, cs], Op.add, more=h > 0)
 
-        ts("ofq", "ps6", T.ofq[:], ps[6][:, 0:20], 160.0, Op.add)
-        early(0, 0)
-        do("v", "ofq phr", "row", lambda: V.tensor_copy(T.row[:].indirect(T.ofq[:]), T.phr[:]))
-        early(0, 1)
         for i in range(5):
-            scan("s5", "d16 row", T.s5[:, i, :], T.d16[:, 0, :], T.row[:, 64 * i:64 * i + 64] if final else T.row[:, i:320:5], more=i > 0, ops=LATCH)
-        early(1, 0)
+            scan("s5", "d16 row", T.s5[:, i, :], T.d16[:, 0, :], T.row[:, 64 * i:64 * i + 64] if final else T.row[:, i:320:5], more=i > 0, ops=(Op.add, Op.min))
+        early(0, 0)
         parts = [(slice(0, 20), slice(0, 4))] if final else [(slice(10 * h, 10 * h + 10), slice(2 * h, 2 * h + 2)) for h in range(2)]
         for h, (o, v) in enumerate(parts):
             ts("offa%d" % h, "s5 cb", T.offa[:, o], T.s5[:, :, 15 + 16 * v.start:16 * v.stop:16], T.pf[:, 4:5], Op.add)
-
+        early(0, 1)
+        early(1, 0)
         early(1, 1)
 
         def picks(h):
             for b in (2, 3):
                 act("at%d%d" % (h, b), "offa%d tp" % (0 if final else h), T.at[:, 640 * h + b:640 * h + 640:4], T.tp[:, 320 * b:320 * b + 320].indirect(T.offa[:, 10 * h:10 * h + 10]))
 
-        def blend(h, planes):
-            for b in planes:
+        def blend(h):
+            for b in range(4):
                 cs, win = slice(640 * h + b, 640 * h + 640, 4), T.tq[:, 320 * b:320 * b + 320].indirect(T.offa[:, 10 * h:10 * h + 10])
                 rd = "offa%d tq%d" % (0 if final else h, b)
                 if (h, b) == (0, 1):
@@ -587,11 +596,12 @@ def rank_program(g, core, T, topo):
 
         def finish(h, b, k):
             tt("tm%d%d" % (h, b), "ps%d ak%d%d" % (k, h, b), T.tm[:, 4 * h + b, :], ps[k][:, 0:160], T.ak[:, 640 * h + b:640 * h + 640:4], Op.add)
-            act("xt%d" % h, "tm%d%d" % (h, b), T.xt[:, h, :, :, b], T.tm[:, 4 * h + b, :], 2.0 ** -11, more=b > 0)
+            if (h, b) != (0, 3):
+                act("xt%d" % h, "tm%d%d" % (h, b), T.xt[:, h, :, :, b], T.tm[:, 4 * h + b, :], 2.0 ** -11, more=b > 0)
 
         rc = slice(160 * t, 160 * t + 160)
         picks(0)
-        blend(0, range(4))
+        blend(0)
         picks(1)
         quant("send%d" % t, "zt0", T.sendc[:, rc], T.sendp[:, rc], T.zt[:, 0:640])
         dst = partner_of(t)
@@ -601,7 +611,7 @@ def rank_program(g, core, T, topo):
             g.remote_dma(a, b, T.sem["arr%d" % t], T.sem["snd%d" % t], pid, rid, topo.mask(core, dst))
         eng = 2 * len(topo.engines(core, dst))
         last["land%d" % t] = {"arr%d" % t: eng}
-        blend(1, range(4))
+        blend(1)
         kept(1)
         kept(0)
         if final:
@@ -621,6 +631,7 @@ def rank_program(g, core, T, topo):
             finish(0, b, b)
         need("p", "snd%d" % t, eng)
         state(1)
+        ts("xt0", "tm03", T.xt[:, 0, :, :, 3], T.tm[:, 3, :], 2.0 ** -11, Op.mult, more=True)
         if final:
             mm("ps4", "xq1 vq", (ps[4][:, 0:160], T.vq[:], T.vs[:], T.xq[:, 160:320], T.xs[:, 160:320]))
             do("y", "xq1", "", lambda: Y.dma_start(T.oc[:, 640:1280], T.xq[:, 160:320].bitcast(dt.uint8)), "fin", 16)
@@ -636,6 +647,5 @@ def rank_program(g, core, T, topo):
     do("s", "yb0", "", lambda: S.dma_start(T.y[:, 0:160], T.row[:, 0:160]), "fin", 16)
     for k in range(4):
         do("y", "xq0 xq1", "", lambda: Y.dma_start(T.osc[4 * k:4 * k + 4, :], T.xs[32 * k:32 * k + 4, :]), "fin", 16)
-    need("y", "fin", count["fin"])
     for k in count:
         need("y" if k in ("fin", "v", "s", "t") else "p", k, count[k])

@@ -1,8 +1,9 @@
 import numpy as np
-from concourse.mybir import dt, AluOpType as Op, ActivationFunctionType as AF
+from concourse.mybir import dt, AluOpType as Op, ActivationFunctionType as AF, AxisListType as AX
 
 F, B, I, U16 = "float32", "bfloat16", "int32", "uint16"
 C8, U8 = "float8_e4m3fn_x4", "uint8"
+PL = 416
 
 
 def _sb(t, *s):
@@ -14,25 +15,24 @@ SCRATCH = {
     "xq": _sb(C8, 320), "xs": _sb(U8, 320), "uq": _sb(C8, 128), "us": _sb(U8, 128), "vq": _sb(C8, 128), "vs": _sb(U8, 128),
     "uq0": _sb(C8, 128), "us0": _sb(U8, 128), "uo": _sb(U16, 8), "uf": _sb(F, 8),
     "wq": _sb(C8, 512), "wsc": _sb(U8, 512), "lq": _sb(C8, 160), "lsc": _sb(U8, 160),
-    "sc": _sb(F, 8, 5, 4), "cm": _sb(B, 4, 8, 5), "a2": _sb(B, 2, 40), "hb": _sb(B, 160), "rk": _sb(B, 40), "pay": _sb(B, 160),
-    "pd": _sb(B, 80), "eqr": _sb(B, 5, 80), "prb": _sb(B, 80, 5), "rt": _sb(B, 4, 8, 21), "rq": _sb(C8, 168), "rs": _sb(U8, 168),
-    "rt2": _sb(B, 7, 88), "rq2": _sb(C8, 154), "rs2": _sb(U8, 154),
-    "tbb": _sb(B, 50), "val": _sb(B, 2, 50), "sq": _sb(B, 2, 50), "ab": _sb(B, 2, 150), "dt3": _sb(B, 3, 150),
-    "so": _sb(B, 31, 150), "tbp": _sb(F, 2, 20), "sqp": _sb(F, 3, 20), "und": _sb(F, 2, 20), "tt4": _sb(F, 2, 4),
-    "cde": _sb(I, 64), "ca": _sb(I, 64), "pe": _sb(F, 64), "pt": _sb(B, 512),
-    "ptq": _sb(C8, 192), "pts": _sb(U8, 192), "ne": _sb(F, 5, 64), "dp": _sb(F, 64), "uop": _sb(F, 2, 5, 64),
-    "inc": _sb(F, 24), "pr": _sb(F, 20), "v2": _sb(I, 2, 20), "dgi": _sb(I, 6, 20), "dgp": _sb(B, 19, 5, 2, 4), "dgr": _sb(B, 15, 5, 2, 4),
-    "dgq": _sb(C8, 340), "dgs": _sb(U8, 340), "ofp": _sb(U16, 20), "ofq": _sb(U16, 20), "pk": _sb(F, 320), "row": _sb(F, 320),
-    "s5": _sb(F, 5, 64), "offa": _sb(U16, 20), "tq": _sb(B, 1280), "tw": _sb(B, 640),
-    "tp": _sb(B, 1280), "zt": _sb(B, 1280), "at": _sb(B, 1280), "ak": _sb(B, 1280), "tm": _sb(F, 8, 160),
+    "sc": _sb(F, 8, 5, 4), "cm": _sb(B, 4, 8, 5), "a2": _sb(B, 7, 40), "hb": _sb(B, 3, 120), "pd": _sb(B, 80),
+    "eqr": _sb(B, 5, 80), "prb": _sb(B, 5, 80), "rt": _sb(B, 2, 376), "rq": _sb(C8, 198), "rs": _sb(U8, 198),
+    "tbb": _sb(B, 120), "val": _sb(B, 2, 60), "ab": _sb(B, 2, 360), "dt2": _sb(B, 2, 180),
+    "so": _sb(B, 28, 180), "tbp": _sb(F, 20), "sqp": _sb(F, 3, 20), "tt4": _sb(F, 2, 4),
+    "pe": _sb(F, 64), "pt": _sb(B, 512), "ptq": _sb(C8, 192), "pts": _sb(U8, 192), "pc": _sb(B, 512), "pcq": _sb(C8, 128), "pcs": _sb(U8, 128),
+    "ne": _sb(B, 320), "un": _sb(B, 320), "dp": _sb(F, 64), "uop": _sb(F, 2, 5, 64),
+    "inc": _sb(F, 24), "pr": _sb(F, 20), "v2": _sb(I, 2, 20), "dgi": _sb(I, 4, 20), "dgp": _sb(B, 15, 5, 2, 4), "dgr": _sb(B, 15, 5, 2, 4),
+    "dgq": _sb(C8, 300), "dgs": _sb(U8, 300), "ofp": _sb(U16, 20), "ofq": _sb(U16, 20), "pk": _sb(F, 320), "row": _sb(F, 320),
+    "s5": _sb(F, 5, 64), "offa": _sb(U16, 20),
+    "tp": _sb(B, 4 * PL), "tq": _sb(B, 1280), "tz": _sb(B, 4 * PL), "zt": _sb(B, 1280), "ak": _sb(B, 1280), "tm": _sb(F, 8, 160),
     "zz": _sb(B, 512), "zf": _sb(F, 4), "wm": _sb(B, 64, 4), "wat": _sb(B, 160, 4), "i16": _sb(B, 64),
-    "waq": _sb(C8, 160), "was": _sb(U8, 160),
-    "et": _sb(B, 516), "ones": _sb(B, 128), "eqc": _sb(C8, 512), "eqs": _sb(U8, 512),
+    "waq": _sb(C8, 160), "was": _sb(U8, 160), "et": _sb(B, 516), "eqc": _sb(C8, 512), "eqs": _sb(U8, 512),
     "w3": _sb(B, 3, 128, 4), "cq3": _sb(C8, 384), "cs3": _sb(U8, 384),
-    "n80": _sb(I, 80), "nb80": _sb(I, 80), "msk": _sb(F, 4, 80), "cg": _sb(F, 20), "grp": _sb(F, 2, 4),
-    "ct": _sb(F, 4, 50), "val1": _sb(B, 50), "pi": _sb(I, 8), "pf": _sb(F, 10), "c0": _sb(F, 5, 10),
-    "pa": _sb(B, 160), "pa16": _sb(F, 64), "d16i": _sb(I, 64), "d16": _sb(F, 2, 64),
-    "phr": _sb(F, 320), "lgr": _sb(F, 320),
+    "n40": _sb(I, 40), "nb40": _sb(I, 40), "msk": _sb(F, 4, 40), "cg": _sb(F, 20), "grp": _sb(F, 4), "gi": _sb(I, 2, 4),
+    "tv": _sb(F, 60), "val1": _sb(B, 2, 60), "pi": _sb(I, 8), "pf": _sb(F, 12), "c0": _sb(F, 2, 10),
+    "av": _sb(I, 2, 10), "stv": _sb(F, 3, 12), "stt": _sb(F, 48), "uc": _sb(B, 320),
+    "pa": _sb(B, 120), "pa16": _sb(F, 64), "d16i": _sb(I, 64), "d16": _sb(F, 2, 64),
+    "phr": _sb(F, 320), "lgr": _sb(F, PL),
 }
 for _k in ("send", "land"):
     SCRATCH[_k + "c"] = _sb(C8, 480)
@@ -41,8 +41,9 @@ for _t in range(8):
     SCRATCH["ps%d" % _t] = ("psum", [128, 512], F)
 SEMAPHORES = ["v", "s", "t", "dx0", "dx1", "du", "dw", "dv", "fin"] + ["p%d" % i for i in range(60)] + ["%s%d" % (a, i) for a in ("arr", "snd") for i in range(3)]
 
-EPS = 2.0 ** -40
-U = 2.0 ** 18
+EPS = 2.0 ** -24
+U = 2.0 ** -10
+MID = 248
 LOW = 512.0
 PARTNER = [1, 2, 3]
 
@@ -125,8 +126,8 @@ def rank_program(g, core, T, topo):
         else:
             do("s", rd, wr, lambda: S.activation(out, a, func or AF.Copy, scale=scale), more=more)
 
-    def const(wr, out, n, c, more=False):
-        act(wr, "zz", out, T.zz[:, 0:n], bias=c, more=more)
+    def const(wr, out, n, c, more=False, rd=""):
+        act(wr, "zz " + rd, out, T.zz[:, 0:n], bias=c, more=more)
 
     def iota(wr, out, pat, base, cm, more=False, part="all"):
         do("p", "", wr, lambda: P.iota(out, pat, base, cm), more=more, part=part)
@@ -137,10 +138,10 @@ def rank_program(g, core, T, topo):
     def select(wr, rd, out, a, pat, op, c, base, cm, more=False, part="all"):
         do("p", rd, wr, lambda: P.affine_select(out, a, pat, op, c, base, cm), more=more, part=part)
 
-    def mm(wr, rd, *prods):
-        pre("t", rd, wr)
+    def mm(wr, rd, *prods, first=True, done=True):
+        pre("t", rd, wr if first else "")
         for i, p in enumerate(prods):
-            ins = g.tensor.matmul_mx(*p, i == 0, i == len(prods) - 1)
+            ins = g.tensor.matmul_mx(*p, first and i == 0, done and i == len(prods) - 1)
         ins.then_inc(T.sem.t, 1)
         post("t", 1, rd, wr)
 
@@ -151,159 +152,202 @@ def rank_program(g, core, T, topo):
     lo, up = slice(0, 64), slice(64, 128)
     halves, part = ((0, lo), (1, up)), ("lo", "up")
     fill("zz", T.zz[:], 0.0)
-    fill("ones", T.ones[:], 1.0)
     fill("et0", T.et[:], 0.0)
     iota("pi", T.pi[:], [[0, 8]], 0, 1)
     iotaf("uf", T.uf[:], [[0, 4], [-64, 2]], 112)
-    iotaf("ct0", T.ct[:, 0, 0:10], [[1, 10]], 158)
-    iotaf("ct0", T.ct[:, 0, 10:50], [[1, 40]], 128, more=True)
-    iotaf("ct3", T.ct[:, 3, 0:10], [[-1, 2], [0, 5]], 129)
-    iotaf("ct3", T.ct[:, 3, 10:50], [[-1, 8], [0, 5]], 135, more=True)
-    iotaf("c0i", T.c0[:, 0, :], [[1, 10]], -7)
+    iota("av", T.av[:, 0, :], [[-8, 10]], 72, 1)
     select("wm1", "zz", T.wm[lo], T.zz[lo, 0:256], [[-1, 64], [8, 4]], Op.not_equal, 1.0, -56, 1, part="lo")
-    iota("d16i", T.d16i[:], [[1, 64]], 128, -1)
+    iotaf("c0i", T.c0[:, 0, 0:2], [[-1, 2]], 1)
+    iotaf("c0i", T.c0[:, 0, 2:10], [[-1, 8]], 7, more=True)
     select("wm", "wm1", T.wm[lo], T.wm[lo], [[-1, 64], [8, 4]], Op.not_equal, 1.0, 8, 1, part="lo")
-    select("et", "ones et0", T.et[:, 3:515:4], T.ones[:], [[-1, 128]], Op.is_equal, 0.0, 0, 1)
+    iotaf("tv0", T.tv[:, 12:60], [[-64, 8], [0, 6]], 258)
+    select("et", "zz et0", T.et[:, 3:515:4], T.zz[:, 0:128], [[-1, 128]], Op.not_equal, 0.5, 0, 1)
+    iota("d16i", T.d16i[:], [[1, 64]], 128, -1)
     for j in range(2):
         iotaf("pd0", T.pd[up, j:80:2], [[0, 8], [2 * j - 1, 5]], 0, more=True, part="up")
     for h, sl in halves:
-        iotaf("cg", T.cg[sl], [[0, 5], [5, 4]], 132 + 20 * h, more=True, part=part[h])
-        iotaf("gc", T.grp[sl, 0, :], [[-1, 4]], 135 - 4 * h, more=True, part=part[h])
-        iota("n80", T.n80[sl, :], [[0, 20], [-8, 4]], 120 - 32 * h, 1, more=True, part=part[h])
+        iotaf("gc", T.grp[sl, :], [[-1, 4]], 8 - 4 * h, more=True, part=part[h])
+        iota("n40", T.n40[sl, :], [[0, 10], [-8, 4]], 120 - 32 * h, 1, more=True, part=part[h])
+        iota("gi", T.gi[sl, 0, :], [[1, 4]], 4 * h, 0, more=True, part=part[h])
 
-    ts("pu0", "pi", T.pi[:, 2:3], T.pi[:, 2:3], 3, Op.bitwise_and)
-    ts("pu1", "pi", T.pi[:, 3:4], T.pi[:, 3:4], 12, Op.bitwise_and)
-    ts("pj", "pi", T.pi[:, 0:2], T.pi[:, 0:2], 7, Op.bitwise_and)
-    ts("pk0", "pi", T.pi[:, 4:5], T.pi[:, 4:5], 63, Op.bitwise_and)
-    for k, tile in (("rt0", T.rt), ("rt20", T.rt2), ("w3z", T.w3)):
-        fill(k, tile[:], 0.0)
-    const("zf", T.zf[:], 4, 0.0)
-    const("pa", T.pa[:], 160, 0.0)
-    const("hb0", T.hb[:, 0:160:4], 40, 0.0)
-    const("eq0", T.eqr[:, :, 0:80:2], 200, 1.0)
-    const("dt0", T.dt3[:, :, 1:150:3], 150, 0.0)
-    const("abk", T.ab[:, :, 0:150:3], 100, 1 / EPS)
-    const("pa", T.pa[:, 0:160:4], 40, 128.0)
-    for j in range(10):
-        const("v0n", T.val1[:, 5 * j:5 * j + 5], 5, 200 * U * 2.0 ** (9 - j), more=True)
-    act("ct1", "ct0", T.ct[:, 1, :], T.ct[:, 0, :], U)
-    act("ct2", "ct0", T.ct[:, 2, :], T.ct[:, 0, :], -U / EPS)
-    act("dg1", "ct3", T.dt3[:, 2, 2:150:3], T.ct[:, 3, :])
-    act("dg1", "ct3", T.dt3[:, 2, 0:150:3], T.ct[:, 3, :], -1 / EPS, more=True)
-    const("dp0", T.dp[:], 64, 0.0)
-    const("pa16", T.pa16[:], 64, 1.0)
-    const("ne0", T.ne[:, :, 0:64:16], 20, 0.0)
-    const("ne0", T.ne[:, :, 15:64:16], 20, 1.0, more=True)
-    const("pt0", T.pt[:], 512, 0.0)
-    const("pa16", T.pa16[:, 0:64:16], 4, 0.0)
-    for h, sl in halves:
-        cs = slice(64 * h, 64 * h + 64)
-        select("wt0", "ones w3z", T.w3[sl, 0, cs, 0], T.ones[sl, 0:64], [[1, 64]], Op.is_gt, 0.0, 0, -1, more=True, part=part[h])
-        select("wt0", "ones w3z", T.w3[sl, 0, cs, 1], T.ones[sl, 0:64], [[-1, 64]], Op.is_ge, 0.0, 0, 1, more=True, part=part[h])
-    for step in range(2):
-        for h, sl in halves:
-            for e in range(4):
-                k0 = 64 - (56 - 32 * h - 8 * e) % 64
-                a, b = T.w3[sl, 1, 64 * h:64 * h + k0, e], T.w3[sl, 1, 64 * h + k0:64 * h + 64, e]
-                name = "wt1%d%d" % (h, e)
-                if step == 0:
-                    select(name + "a", "w3z", a, a, [[-1, k0]], Op.is_ge, -1.0, 0, 1, part=part[h])
-                    if k0 < 64:
-                        select(name + "b", "w3z", b, b, [[-1, 64 - k0]], Op.is_ge, -1.0, -k0, 1, part=part[h])
-                elif k0 < 64:
-                    select(name + "a", name + "a", a, a, [[0, k0]], Op.is_gt, -1.0, k0, -1, part=part[h])
-                    select(name + "b", name + "b", b, b, [[0, 64 - k0]], Op.is_ge, 0.0, -k0, 1, part=part[h])
-    iotaf("phr", T.phr[:], [[1, 320]], 0)
-    iotaf("lgr", T.lgr[:], [[160, 2], [1, 5], [5, 32]], 0)
-    copy("pu2", "pu0", T.pf[:, 6:7], T.pi[:, 2:3])
-    ts("pu3", "pu1", T.pf[:, 7:8], T.pi[:, 3:4], -4.0, Op.mult)
-    ts("g0", "pj", T.pf[:, 0:2], T.pi[:, 0:2], -5.0, Op.mult, 167.0, Op.add)
-    ts("g1", "pj", T.pf[:, 2:4], T.pi[:, 0:2], -1.0, Op.mult)
-    ts("kf", "pk0", T.pf[:, 8:9], T.pi[:, 4:5], -1024.0, Op.add)
-    fill("cd0_", T.cde[:], 1)
-    quant("ptqz", "zz", T.ptq[:, 64:192], T.pts[:, 64:192], T.zz[:])
-    ts("uo", "uf pu2 pu3", T.uo[:], T.uf[:], T.pf[:, 6:7], Op.add, T.pf[:, 7:8], Op.add)
-    ts("v0m", "ct0 g0", T.tbb[:], T.ct[:, 0, :], T.pf[:, 0:1], Op.not_equal)
-    ts("c0a", "c0i g1", T.c0[:, 1, :], T.c0[:, 0, :], T.pf[:, 2:3], Op.is_equal)
-    quant("uq0", "ut", T.uq0[:], T.us0[:], T.ut[:])
-    ts("c0n", "c0i g1", T.c0[:, 2, :], T.c0[:, 0, :], T.pf[:, 2:3], Op.not_equal)
-    tt("val1", "v0m v0n", T.val1[:], T.val1[:], T.tbb[:], Op.mult)
-    tt("c0c c0i", "c0a ct1", T.c0[:, 0, 0:8], T.c0[:, 1, 0:8], T.ct[:, 1, 14:50:5], Op.mult)
-    do("v", "uq0 uo", "uq", lambda: V.tensor_copy(T.uq[:].bitcast(dt.uint32), T.uq0[:].bitcast(dt.uint32).indirect(T.uo[:])))
-    do("s", "uq0 uo", "uq", lambda: S.activation(T.us[:], T.us0[:].indirect(T.uo[:]), AF.Copy), more=True)
+    def orders(j):
+        if j == 0:
+            for h, sl in halves:
+                cs = slice(64 * h, 64 * h + 64)
+                select("wt0", "w30", T.w3[sl, 0, cs, 0], T.w3[sl, 0, cs, 0], [[-1, 64]], Op.is_ge, 1.0, 0, 1, more=True, part=part[h])
+                select("wt0", "w30", T.w3[sl, 0, cs, 1], T.w3[sl, 0, cs, 1], [[1, 64]], Op.is_gt, 1.0, 0, -1, more=True, part=part[h])
+            return
+        for step in range(2):
+            for h, sl in halves:
+                for e in range(4):
+                    k0 = 64 - (56 - 32 * h - 8 * e) % 64
+                    a, b = T.w3[sl, 1, 64 * h:64 * h + k0, e], T.w3[sl, 1, 64 * h + k0:64 * h + 64, e]
+                    name = "wt1%d%d" % (h, e)
+                    if step == 0:
+                        select(name + "a", "w31", a, a, [[-1, k0]], Op.is_ge, -1.0, 0, 1, part=part[h])
+                        if k0 < 64:
+                            select(name + "b", "w31", b, b, [[-1, 64 - k0]], Op.is_ge, -1.0, -k0, 1, part=part[h])
+                    elif k0 < 64:
+                        select(name + "a", name + "a", a, a, [[0, k0]], Op.is_gt, -1.0, k0, -1, part=part[h])
+                        select(name + "b", name + "b", b, b, [[0, 64 - k0]], Op.is_ge, 0.0, -k0, 1, part=part[h])
+        iotaf("phr", T.phr[:], [[256, 2], [1, 160]], 0)
+        for h in range(2):
+            iotaf("lgr", T.lgr[:, 256 * h:256 * h + 160], [[1, 5], [5, 32]], 160 * h, more=True)
 
     def state(h):
         quant("xq%d" % h, "xt%d" % h, T.xq[:, 160 * h:160 * h + 160], T.xs[:, 160 * h:160 * h + 160], T.xt[:, h, :, :, :])
 
     def places(h):
         for i in range(5):
-            (copy if i < 3 + h else act)("xt%d" % h, "xin%d" % h, T.xt[:, h, i, :, :], T.xin[:, 32 * h:32 * h + 32, 4 * i:4 * i + 4], more=True)
+            (copy if i < 4 else act)("xt%d" % h, "xin%d" % h, T.xt[:, h, i, :, :], T.xin[:, 32 * h:32 * h + 32, 4 * i:4 * i + 4], more=True)
 
-    def turner(sl, c):
-        for a, w in ((0, 64), (64, 64), (128, 32)):
+    def turner(sl, c, pieces):
+        for a, w in pieces:
             act("wat", "wm", T.wat[sl, a:a + w, :], T.wm[lo, 0:w, :], c, more=True)
 
+    ts("pu0", "pi", T.pi[:, 2:3], T.pi[:, 2:3], 3, Op.bitwise_and)
+    ts("pu1", "pi", T.pi[:, 3:4], T.pi[:, 3:4], 12, Op.bitwise_and)
+    ts("pj", "pi", T.pi[:, 0:1], T.pi[:, 0:1], 7, Op.bitwise_and)
+    ts("pk0", "pi", T.pi[:, 4:5], T.pi[:, 4:5], 63, Op.bitwise_and, 3, Op.logical_shift_right)
+    ts("av1", "av", T.av[:, 0, :], T.av[:, 0, :], 63, Op.bitwise_and, 3, Op.logical_shift_right)
+    copy("pu2", "pu0", T.pf[:, 6:7], T.pi[:, 2:3])
+    ts("pu3", "pu1", T.pf[:, 7:8], T.pi[:, 3:4], -4.0, Op.mult)
+    copy("r7", "pj", T.pf[:, 0:1], T.pi[:, 0:1])
+    quant("rqz", "zz", T.rq[:, 70:198], T.rs[:, 70:198], T.zz[:])
+    ts("av2", "av1", T.av[:, 1, :], T.av[:, 0, :], 4.0, Op.is_ge, 28.0, Op.mult)
+    ts("uo", "uf pu2 pu3", T.uo[:], T.uf[:], T.pf[:, 6:7], Op.add, T.pf[:, 7:8], Op.add)
+    fill("w30", T.w3[:, 0, :, :], 0.0)
+    tt("stv", "av1 av2", T.stv[:, 0, 0:10], T.av[:, 0, :], T.av[:, 1, :], Op.add)
+    quant("uq0", "ut", T.uq0[:], T.us0[:], T.ut[:])
+    const("pa", T.pa[:], 120, 2.0)
+    const("eq0", T.eqr[:, :, 0:80:2], 200, 1.0)
+    const("dt0", T.dt2[:], 360, 0.0)
+    const("pa", T.pa[:, 0:120:3], 40, 0.0)
+    const("tv1", T.tv[:, 0:12], 12, 258.0)
+    const("zf", T.zf[:], 4, 0.0)
+    const("stz", T.stv[:, 0, 10:11], 1, 0.0)
+    const("abk", T.ab[:, :, 0:180:3], 120, 1 / EPS)
+    const("dg1", T.dt2[:, 1, 16:180:18], 10, 1 / EPS, rd="dt0")
     places(1)
-    act("c0b", "c0a", T.c0[:, 3, 0:9], T.c0[:, 1, 0:9], -1024.0)
-    tt("c0d", "c0a ct3", T.c0[:, 4, 0:8], T.c0[:, 1, 0:8], T.ct[:, 3, 14:50:5], Op.mult)
-    tt("c0", "c0n c0c", T.c0[:, 2, 1:9], T.c0[:, 2, 1:9], T.c0[:, 0, 0:8], Op.max)
-    state(1)
+    ts("c0a", "c0i r7", T.c0[:, 1, :], T.c0[:, 0, :], T.pf[:, 0:1], Op.is_equal)
     places(0)
+    do("v", "uq0 uo", "uq", lambda: V.tensor_copy(T.uq[:].bitcast(dt.uint32), T.uq0[:].bitcast(dt.uint32).indirect(T.uo[:])))
+    do("s", "uq0 uo", "uq", lambda: S.activation(T.us[:], T.us0[:].indirect(T.uo[:]), AF.Copy), more=True)
+    state(1)
+    state(0)
     do("y", "xin0", "wq", lambda: Y.dma_start(T.wq[:].bitcast(dt.uint8), T.wc[:]), "dw", 16, more=True)
     do("y", "", "wq", lambda: Y.dma_start(T.wsc[:], T.ws[:]), "dw", 16, more=True)
     do("y", "", "vt", lambda: Y.dma_start(T.vt[:], T.v[:]), "dv", 16)
-    tt("c1", "c0b c0d", T.c0[:, 3, 1:9], T.c0[:, 3, 1:9], T.c0[:, 4, 0:8], Op.add)
-    state(0)
-    turner(lo, 1.0)
+    const("dg1", T.dt2[:, 1, 34:35], 1, -7 / EPS)
+    const("tv", T.tv[:, 5:60:6], 10, -1 / U, rd="tv0 tv1")
+    turner(lo, 64 * U, ((0, 64), (64, 64), (128, 32)))
+    fill("rt0", T.rt[:], 0.0)
+    tt("sg0", "stv stz", T.stv[:, 1, 0:10], T.stv[:, 0, 0:10], T.stv[:, 0, 1:11], Op.subtract)
+    tt("st1", "stv c0a", T.stv[:, 2, 0:8], T.stv[:, 0, 2:10], T.c0[:, 1, 2:10], Op.mult)
+    orders(0)
+
+    def tables():
+        fill("w31", T.w3[:, 1, :, :], 0.0)
+        orders(1)
+        yield
+        turner(up, 4 * U, ((0, 64),))
+        yield
+        turner(up, 4 * U, ((64, 64),))
+        yield
+        do("v", "st1", "st2", lambda: V.tensor_reduce(T.pf[:, 1:2], T.stv[:, 2, 0:8], AX.X, Op.add))
+        next(big)
+        yield
+        turner(up, 4 * U, ((128, 32),))
+        act("v0", "tv", T.val1[:, 0, :], T.tv[:], U)
+        act("v0a", "tv", T.val1[:, 1, :], T.tv[:], U, bias=222 * U)
+        yield
+        quant("wa", "wat", T.waq[:], T.was[:], T.wat[:])
+        ts("st0", "st2", T.pf[:, 2:3], T.pf[:, 1:2], U, Op.mult, -MID * U, Op.add)
+        for r in range(6):
+            act("stt", "stv", T.stt[:, r:48:6], T.stv[:, 0, 2:10], U, bias=-MID * U if r < 5 else 1.0, more=True)
+        act("sig", "sg0 dt0", T.dt2[:, 0, 16:180:18], T.stv[:, 1, 0:10], U / EPS)
+        yield
+        for j in range(2):
+            tt("val1", "v0 v0a c0a", T.val1[:, j, 4:60:6], T.val1[:, j, 4:60:6], T.c0[:, 1, :], Op.subtract, more=j > 0)
+        for h, sl in halves:
+            for i in range(5):
+                act("cg", "stv", T.cg[sl, 4 * i:4 * i + 4], T.stv[sl, 0, 2 + 4 * h:6 + 4 * h], U, bias=(4 * i - MID) * U, more=True)
+        const("ne0", T.ne[:, 0:320:16], 20, 0.0)
+        const("ne0", T.ne[:, 15:320:16], 20, 1 / 1024, more=True)
+        const("dp0", T.dp[:], 64, 0.0)
+        fill("pt0", T.pt[:], 0.0)
+        const("w32", T.w3[:, 2, :, :], 512, 0.0)
+        yield
 
     def zeros():
-        for k, a, b in (("dgp", 0, 10), ("dgp", 10, 19), ("dgr", 0, 8), ("dgr", 8, 15)):
+        for k, a, b in (("dgp", 0, 8), ("dgp", 8, 15), ("dgr", 0, 8), ("dgr", 8, 15)):
             act("dg0", "zz", T[k][:, a:b, :, :, :], T.zz[:, 0:40 * (b - a)], more=True)
             yield
+        const("pc0", T.pc[:], 512, 0.0)
+        yield
+        const("uc", T.uc[:], 320, 0.0)
+        const("pa16", T.pa16[:], 64, 1.0)
+        yield
+        for b in range(4):
+            for k in ("tp", "tz"):
+                const("gap", T[k][:, PL * b + 160:PL * b + 256], 96, 0.0, more=True)
+            if b == 1:
+                const("pa16", T.pa16[:, 3:64:16], 4, 0.0)
+            if b % 2:
+                yield
+        const("uc", T.uc[:, 0:320:16], 20, 1024.0)
+        const("uc", T.uc[:, 13:320:16], 20, T.pf[:, 8:9], more=True, rd="kh")
+        const("uc", T.uc[:, 14:320:16], 20, T.pf[:, 9:10], more=True, rd="kh")
+        const("uc", T.uc[:, 15:320:16], 20, 152 / 1024, more=True)
+        const("lgr", T.lgr[:, 160:256], 96, 0.0, more=True)
+        yield
 
     def numbers():
         ts("d16a", "d16i", T.d16i[:], T.d16i[:], 15, Op.bitwise_and)
-        yield
-        ts("n80b", "n80", T.n80[:], T.n80[:], 63, Op.bitwise_and)
-        yield
-        ts("nb80", "n80b", T.nb80[:], T.n80[:], 4, Op.logical_shift_right)
-        yield
-        ts("n5", "n80b", T.inc[:, 0:4], T.n80[:, 0:4], 5.0, Op.mult, -160.0, Op.add)
+        ts("n40b", "n40", T.n40[:], T.n40[:], 63, Op.bitwise_and)
+        ts("kh", "pk0", T.pf[:, 8:9], T.pi[:, 4:5], -1.0, Op.mult, 8.0, Op.add)
+        ts("kh", "pk0", T.pf[:, 9:10], T.pi[:, 4:5], -160.0, Op.add, more=True)
         yield
         ts("i16", "d16a", T.i16[:], T.d16i[:], 0, Op.is_equal)
+        yield
+        ts("nb40", "n40b", T.nb40[:], T.n40[:], 4, Op.logical_shift_right)
+        for h, sl in halves:
+            for e in range(4):
+                m, c = 16 * (7 - 4 * h - e), 8 * ((e + 1) % 2)
+                act("wt2", "i16 w32", T.w3[sl, 2, m:m + 16, e], T.i16[sl, c:c + 16], more=True)
+        yield
+        tt("gi1", "gi n40b", T.gi[:, 0, :], T.gi[:, 0, :], T.n40[:, 0:4], Op.add)
+        yield
+        ts("n5a", "n40b", T.pr[:, 0:4], T.n40[:, 0:4], 5.0, Op.mult, -152.0, Op.add)
+        yield
+        ts("gi2", "gi1", T.gi[:, 1, :], T.gi[:, 0, :], 3, Op.logical_shift_right)
         yield
         ts("d16b", "d16a", T.d16[:, 0, :], T.d16i[:], 0, Op.is_equal, 4 * LOW, Op.mult)
         yield
         ts("d16c", "d16a", T.d16[:, 1, :], T.d16i[:], 1, Op.is_equal, LOW, Op.mult)
         yield
+        tt("n5 pr", "n5a gi2", T.inc[:, 0:4], T.pr[:, 0:4], T.gi[:, 1, :], Op.subtract)
+        yield
         ts("cb", "d16a", T.pf[:, 4:5], T.d16i[:, 15:16], 0, Op.not_equal, LOW, Op.mult)
         yield
         for nb in range(4):
-            ts("msk0", "nb80", T.msk[:, nb, :], T.nb80[:], nb, Op.is_equal, more=True)
+            ts("msk", "nb40", T.msk[:, nb, :], T.nb40[:], nb, Op.is_equal, more=True)
             yield
-        for h, sl in halves:
-            for e in range(4):
-                m, c = 16 * (7 - 4 * h - e), 8 * ((e + 1) % 2)
-                act("wt2", "i16 w3z", T.w3[sl, 2, m:m + 16, e], T.i16[sl, c:c + 16], more=True)
+        tt("d16", "d16b d16c", T.d16[:, 0, :], T.d16[:, 0, :], T.d16[:, 1, :], Op.subtract)
         yield
-        act("msk", "msk0", T.msk[:, :, 40:60], T.msk[:, :, 40:60], 5.0)
-        act("msk", "msk0", T.msk[:, :, 60:80], T.msk[:, :, 60:80], 0.25, more=True)
 
     def tiles():
         for b in range(4):
             quant("e%d" % b, "et", T.eqc[:, 128 * b:128 * b + 128], T.eqs[:, 128 * b:128 * b + 128], T.et[:, 3 - b:515 - b])
             yield
-        fillers(99)
-        for j in (0, 1, 2):
+        quant("ptqz", "zz", T.ptq[:, 64:192], T.pts[:, 64:192], T.zz[:])
+        yield
+        for j in (0, 2, 1):
             rd = " ".join(k for k in last if k.startswith("wt%d" % j))
             quant("qwt%d" % j, rd, T.cq3[:, 128 * j:128 * j + 128], T.cs3[:, 128 * j:128 * j + 128], T.w3[:, j, :, :])
             yield
 
-    blank, rest, big = zeros(), numbers(), tiles()
-
-    def fillers(n):
-        for _ in range(n):
-            next(rest, None)
+    tab, blank, rest, big = tables(), zeros(), numbers(), tiles()
 
     def W3(j):
         return T.cq3[:, 128 * j:128 * j + 128], T.cs3[:, 128 * j:128 * j + 128]
@@ -329,11 +373,13 @@ def rank_program(g, core, T, topo):
             mm("ps%d" % b, "xq0 xq1 e%d" % b, (ps[b][:, 0:320], T.eqc[:, 128 * b:128 * b + 128], T.eqs[:, 128 * b:128 * b + 128], T.xq[:, 0:320], T.xs[:, 0:320]))
         yield
         for b in range(4):
-            act("tp", "ps%d" % b, T.tp[:, 320 * b:320 * b + 320], ps[b][:, 0:320], 0.5, more=b > 0)
-            yield
-            if b < 2:
-                act("tw", "ps%d" % b, T.tw[:, 320 * b:320 * b + 320], ps[b][:, 0:320], 0.5, more=b > 0)
+            for h in range(2):
+                act("tp%d" % b, "ps%d" % b, T.tp[:, PL * b + 256 * h:PL * b + 256 * h + 160], ps[b][:, 160 * h:160 * h + 160], more=h > 0)
                 yield
+        act("tq3", "ps3", T.tq[:, 960:1280], ps[3][:, 0:320])
+        yield
+
+    plane = lambda buf, b: buf[:, PL * b:PL * b + PL]
 
     for t in range(3):
         final = t == 2
@@ -342,79 +388,72 @@ def rank_program(g, core, T, topo):
         scores(0, (6, 7))
         bring(1, (4, 5))
         bring(0, (6, 7))
+        next(tab, None)
         planes = unpack()
-        if t == 0:
-            turner(up, 16.0)
-        else:
-            for j in range(4):
-                next(planes)
+        if t > 0:
+            next(planes)
         key = lambda a, b: T.sc[lo, :, a:b, 3]
         for s in range(1, 5):
             tt("cm%d" % s, "sc0 sc1", T.cm[lo, s - 1, :, 0:5 - s], key(s, 5), key(0, 5 - s), Op.is_gt)
             tt("cm%d" % s, "sc0 sc1", T.cm[lo, s - 1, :, 5 - s:5], key(0, s), key(5 - s, 5), Op.is_ge, more=True)
-        tt("a20", "cm1 cm2", T.a2[lo, 0, :], T.cm[lo, 0, :, :], T.cm[lo, 1, :, :], Op.add)
-        for b in range(3):
-            ts("hb", "sc0 sc1 hb0", T.hb[lo, 1 + b:160:4], T.sc[lo, :, :, b], 0.0, Op.is_gt, (0.0625, 0.25, 0.5)[b], Op.max, more=b > 0)
-        tt("a21", "cm3 cm4", T.a2[lo, 1, :], T.cm[lo, 2, :, :], T.cm[lo, 3, :, :], Op.add)
-        fillers(2)
-        scan("pay", "pa hb", T.pay[lo], T.hb[lo], T.pa[lo])
-        for h, sl in halves:
-            tt("rk", "a20 a21", T.rk[sl], T.a2[lo, 0, :], T.a2[lo, 1, :], Op.add, more=h > 0)
-        if t == 0:
-            quant("wa", "wat", T.waq[:], T.was[:], T.wat[:])
         for j in range(2):
-            act("pd", "pay pd0", T.pd[lo, j:80:2], T.pay[lo, 3:160:4], 2.0 * j - 1, more=j > 0)
+            for h, sl in halves:
+                tt("a2%d" % j, "cm%d cm%d" % (2 * j + 1, 2 * j + 2), T.a2[sl, 5 + j, :], T.cm[lo, 2 * j, :, :], T.cm[lo, 2 * j + 1, :, :], Op.add, more=h > 0)
+        act("hb0", "sc0 sc1", T.hb[lo, 0, :], T.sc[lo, :, :, 0:3], func=AF.Sign)
+        next(tab, None)
+        act("hb1", "hb0", T.hb[lo, 1, :], T.hb[lo, 0, :], func=AF.Relu)
+        next(tab, None)
+        order = (4, 0, 1, 2, 3)
+        for r in order:
+            act("ar%d" % r, "a20", T.a2[:, r, :], T.a2[:, 5, :], -1.0, bias=4.0 - r)
+        scan("sym", "pa hb1", T.hb[lo, 2, :], T.pa[lo], T.hb[lo, 1, :])
+        next(tab, None)
+        for j in range(2):
+            act("pd", "sym pd0", T.pd[lo, j:80:2], T.hb[lo, 2, 2:120:3], 2.0 * j - 1, more=j > 0)
+        for r in order:
+            tt("eqr%d" % r, "ar%d a21 eq0" % r, T.eqr[:, r, 1:80:2], T.a2[:, r, :], T.a2[:, 6, :], Op.not_equal)
         for i in range(5):
-            act("rt2", "pay rt20", T.rt2[lo, 0:2, 16 * i:16 * i + 20:5], T.pay[lo, 3 + 4 * i:160:20], U, more=i > 0)
-            act("rt2", "rk rt20", T.rt2[up, 2:4, 16 * i:16 * i + 20:5], T.rk[up, i:40:5], -0.0625, more=True)
-        const("abb1", T.ab[:, 1, 2:150:3], 50, EPS)
-        for r in range(5):
-            ts("eqr%d" % r, "rk eq0", T.eqr[:, r, 1:80:2], T.rk[:], 4.0 - r, Op.not_equal)
-        for r in range(5):
-            scan("prb", "eqr%d pd" % r, T.prb[:, :, r], T.eqr[:, r, :], T.pd[:], more=True)
+            act("rtu", "sym rt0", T.rt[lo, :, 196 + 16 * i:212 + 16 * i:5], T.hb[lo, 2, 2 + 3 * i:120:15], more=i > 0)
+        next(tab, None)
+        for r in order:
+            scan("prb%d" % r, "eqr%d pd" % r, T.prb[:, r, :], T.eqr[:, r, :], T.pd[:])
+            act("rts", "prb%d rt0" % r, T.rt[:, :, 4 * r:4 * r + 76:25], T.prb[:, r, 9:80:10], more=r != 4)
+        for a, c in ((0, 192), (1, 96)):
+            tt("rt1", "prb4 c0a rt0", T.rt[:, a, c:c + 4], T.prb[:, 4, 9 + 40 * a:40 + 40 * a:10], T.c0[:, 1, 2 + 4 * a:6 + 4 * a], Op.mult, more=a > 0)
+        next(tab, None)
+        const("abb1", T.ab[:, 1, 2:180:3], 60, EPS)
 
-        quant("rq2", "rt2", T.rq2[:], T.rs2[:], T.rt2[:])
-        act("rth", "prb rt0", T.rt[up, 2:4, 0:4, 0:20:4], T.prb[up, 9:80:10, :])
-        copy("rtl", "prb rt0", T.rt[lo, 0:2, 0:4, 0:20:4], T.prb[lo, 9:80:10, :])
-        list(planes if t else [])
-        fillers(3)
-        quant("rq", "rth rtl", T.rq[:], T.rs[:], T.rt[:])
-        mm("ps5", "wa rq", *[(ps[5][:, 0:130], T.waq[:, w:w + 128], T.was[:, w:w + 128], T.rq[:, c:c + 130], T.rs[:, c:c + 130])
-                             for w, c in ((0, 0), (32, 22))])
-        for h in range(2):
-            mm("ps%d" % (6 + h), "wa rq2", (ps[6 + h][:, 0:128], T.waq[:, 32 * h:32 * h + 128], T.was[:, 32 * h:32 * h + 128], T.rq2[:, 22 * h:22 * h + 128], T.rs2[:, 22 * h:22 * h + 128]))
-        fillers(7)
-        word = lambda a, b: T.dt3[:, 0, 3 * a + 2:3 * b:3]
-        scan("so0", "c0 ps5", T.so[:, 0, 141:150], T.c0[:, 2, 0:9], ps[5][:, 4:45:5], ops=(Op.mult, Op.max))
-        tt("tb1", "ps5 ct1 dt0", word(10, 50), ps[5][:, 0:40], T.ct[:, 1, 10:50], Op.mult)
-        tt("tk1", "ps5 ct2", T.dt3[:, 0, 30:150:3], ps[5][:, 0:40], T.ct[:, 2, 10:50], Op.mult)
-        tt("tc1", "ps5 ct3", T.dt3[:, 1, 32:150:3], ps[5][:, 84:124], T.ct[:, 3, 10:50], Op.add)
-        scan("sw0", "c1 ps5", T.so[:, 14, 141:150], T.c0[:, 3, 0:9], ps[5][:, 88:129:5], ops=(Op.add, Op.max))
-        act("tc3", "tc1", T.dt3[:, 1, 30:150:3], T.dt3[:, 1, 32:150:3], -1 / EPS)
-        act("tb2", "tb1", word(0, 10), word(40, 50))
-        for k, j, c in (("tk1", 0, 0), ("tc1", 1, 2), ("tc3", 1, 0)):
-            act(k + "b", k, T.dt3[:, j, c:30:3], T.dt3[:, j, 120 + c:150:3])
-
-        def cd(n):
-            ts("cd%d" % n, "sw%d gc cd0_" % n, T.cde[:, 14 - n:64:16], T.grp[:, 0, :], T.so[:, 14 + n, 149:150], Op.subtract)
+        quant("rq", "rts rtu rt1 rqz", T.rq[:, 0:188], T.rs[:, 0:188], T.rt[:])
+        mm("ps5", "wa rq", *[(ps[5][:, 0:128], T.waq[:, w:w + 128], T.was[:, w:w + 128], T.rq[:, c:c + 128], T.rs[:, c:c + 128])
+                             for w, c in ((0, 0), (32, 70))])
+        list(tab)
+        next(rest, None)
+        next(rest, None)
+        tt("tbw", "ps5 stt", T.tbb[:, 72:120], ps[5][:, 0:48], T.stt[:], Op.add)
+        ts("tb1", "ps5 dt0", T.dt2[:, 0, 38:180:3], ps[5][:, 0:48], -MID * U, Op.add)
+        ts("tk1", "ps5 dt0", T.dt2[:, 0, 36:180:3], ps[5][:, 0:48], -MID * U, Op.add, -1 / EPS, Op.mult)
+        act("tbw2", "tbw", T.tbb[:, 60:72], T.tbb[:, 108:120])
+        act("tbd", "tbw", T.tbb[:, 0:12], T.tbb[:, 108:120])
+        for k, c in (("tb1", 2), ("tk1", 0)):
+            act(k + "b", k, T.dt2[:, 0, c:36:3], T.dt2[:, 0, 144 + c:180:3])
 
         def drew(n):
-            if n == 11:
-                act("gq", "gc sg11", T.grp[:, 1, :], T.grp[:, 0, :], -1.0, bias=T.so[:, 28, 149:150], func=AF.Square)
-            for k, c in (("po0", 4), ("po1", 1)):
-                if n == 11:
-                    act(k, "gq", T.pt[:, 8 + c:256:64], T.grp[:, 1, :], -1.0, bias=1.0, func=AF.Relu)
-                else:
-                    ts(k, "gc sg%d" % n, T.pt[:, 52 - 4 * n + c:256:64], T.grp[:, 0, :], T.so[:, 17 + n, 149:150], Op.is_equal, more=True)
+            s, c = T.so[:, 14 + n, 179:180], 56 - 4 * n
+            ts("po%d" % n, "gc pt0 %ssg%d" % ("pe " if n > 11 else "", n), T.pt[:, c:256:64], T.grp[:], s, Op.is_equal)
+            if n < 13:
+                act("pp%d" % n, "po%d" % n, T.pt[:, c - 3:256:64], T.pt[:, c:256:64])
+            else:
+                ts("pp13", "gc sg13", T.pt[:, c - 3:256:64], T.grp[:], s, Op.is_equal)
+                ts("pq13", "gc sg13", T.pt[:, 256:512:65], T.grp[:], s, Op.is_equal)
 
         def far(n):
-            act("sqp%d" % (n % 3), "tbp so%d" % n, T.sqp[:, n % 3, :], T.tbp[:, 0, :], -1.0, bias=T.so[:, n, 149:150], func=AF.Square)
+            act("sqp%d" % (n % 3), "tbp so%d" % n, T.sqp[:, n % 3, :], T.tbp[:], -1.0, bias=T.so[:, n, 179:180], func=AF.Square)
 
         def other(n):
-            act("ne", "sqp%d ne0" % (n % 3), T.ne[:, :, 14 - n:64:16], T.sqp[:, n % 3, :], func=AF.Sign, more=n > 0)
+            act("ne", "sqp%d ne0" % (n % 3), T.ne[:, 14 - n:320:16], T.sqp[:, n % 3, :], func=AF.Sign, more=n > 0)
 
         def steps(n):
-            s, so, a = T.so[:, 14 + n, 149:150], "sw%d" % n, n % 2
+            s, so, a = T.so[:, n, 179:180], "so%d" % n, n % 2
             if n == 0:
                 act("dp", "zf dp0 " + so, T.dp[:, 13:64:16], T.zf[:], bias=s)
             else:
@@ -422,174 +461,140 @@ def rank_program(g, core, T, topo):
             if n < 13:
                 act("tt%d" % a, "zf " + so, T.tt4[:, a, :], T.zf[:], bias=s)
 
-        def undrawn(n):
-            a = n % 2
-            if n == 0:
-                ts("und0", "sqp0", T.und[:, 0, :], T.sqp[:, 0, :], 1.0, Op.min)
-            else:
-                tt("und%d" % a, "und%d sqp%d" % (1 - a, n % 3), T.und[:, a, :], T.und[:, 1 - a, :], T.sqp[:, n % 3, :], Op.min)
-
         for n in range(1, 14):
-            s, so = T.so[:, n - 1, 149:150], "so%d" % (n - 1)
-            j, w = 10 if n < 5 else 5 if n < 10 else 0, n % 2
+            s, so = T.so[:, n - 1, 179:180], "so%d" % (n - 1)
+            j, w = 2 if n < 5 else 1 if n < 10 else 0, n % 2
             vk = "val1" if n < 3 else "vl%d" % w
-            if 1 < n < 13:
-                act("sq%d" % (1 - w), "tb1 tb2 " + so, T.sq[:, 1 - w, :], word(0, 50), -1.0, bias=s, func=AF.Square)
-            late = range(3) if n == 3 else [n - 1] if n > 3 else []
+            old = lambda a, b: T.val1[:, 0, a:b] if n < 3 else T.val[:, w, a:b]
+
+            def marks(a):
+                tt("vl%d" % (1 - w), vk + " abb%d" % w, T.val[:, 1 - w, 30 * a:30 * a + 30], old(30 * a, 30 * a + 30), T.ab[:, w, 182 + 90 * a:270 + 90 * a:3], Op.subtract, more=a > 0)
+
+            def search(name, rd, row, d):
+                scan(name, "aba%d abb%d %s" % (w, w, rd), T.so[:, row, 18 * j:180], T.ab[:, w, 18 * j:180], T.dt2[:, d, 18 * j:180])
+
+            if n == 1:
+                ts("aba1", "val1 abk ps5", T.ab[:, 1, 37:180:3], T.val1[:, 1, 12:60], ps[5][:, 48:49], Op.is_lt, EPS, Op.add)
+                ts("so0", "ps5 st0", s, ps[5][:, 48:49], T.pf[:, 2:3], Op.add)
+                tt("tbb", "val1 tbw", T.tbb[:, 12:60], T.val1[:, 0, 12:60], T.tbb[:, 72:120], Op.min)
+            else:
+                ts("abb%d" % w, ("tbb tbw2 " if n < 5 else "tbd ") + so, T.ab[:, w, 18 * j + 2:360:3], T.tbb[:, 6 * j:120], s, Op.is_equal, EPS, Op.add)
+                ts("aba%d" % w, vk + " abk " + so, T.ab[:, w, 18 * j + 1:180:3], old(6 * j, 60), s, Op.is_lt, EPS, Op.add)
+                drew(n - 1)
+                next(rest, None)
+            late = range(2) if n == 2 else [n - 1] if n > 2 else []
             for m in late:
                 far(m)
             steps(n - 1)
-            if n > 2:
-                next(planes if n > 6 else blank, None)
+            if t == 0:
+                if n == 6:
+                    next(planes)
+                next(planes if 6 < n < 12 else blank, None)
+                if n in (2, 7, 8, 9, 10):
+                    next(planes if n > 6 else blank, None)
+            elif n > 1:
+                next(planes, None)
             for m in late:
                 other(m)
-            ts("aba%d" % w, vk + " abk " + so, T.ab[:, w, 3 * j + 1:150:3], T.val1[:, j:50] if n < 3 else T.val[:, w, j:50], s, Op.is_lt, EPS, Op.add)
-            if n == 1:
-                tt("tbm", "val1 tb1", T.tbb[:, 10:50], T.val1[:, 10:50], word(10, 50), Op.is_ge)
-                for h, sl in halves:
-                    tt("tbq", "ps%d cg" % (6 + h), T.tbp[sl, 1, :], ps[6 + h][sl, 44:64], T.cg[sl], Op.add, more=h > 0)
-            else:
-                ts("abb%d" % w, ("tbb " if n < 5 else "tbd ") + so, T.ab[:, w, 3 * j + 2:150:3], T.tbb[:, j:50], s, Op.is_equal, EPS, Op.add)
-            if n == 2:
-                for h, sl in halves:
-                    tt("tbp", "ps%d tbq" % (6 + h), T.tbp[sl, 0, :], ps[6 + h][sl, 0:20], T.tbp[sl, 1, :], Op.mult, more=h > 0)
-            elif n > 2:
-                next(big, None)
-            if n == 4:
-                undrawn(1)
-            if n == 11:
-                cd(10)
-            if n == 12:
-                ts("po0", "ca pt0", T.pt[:, 0:256:4], T.ca[:], 0, Op.is_equal)
-                ts("po1", "ca pt0", T.pt[:, 1:252:4], T.ca[:, 1:64], 0, Op.is_equal)
-                bulk = count["v"]
             if 2 <= n < 13:
-                tt("vl%d" % (1 - w), vk + " sq%d" % (1 - w), T.val[:, 1 - w, :], T.val1[:] if n < 3 else T.val[:, w, :], T.sq[:, 1 - w, :], Op.min)
+                marks(0)
             if n == 13:
-                need("v", "v", bulk)
-                drew(12)
-
-            def search(name, rd, row, d):
-                scan(name, "aba%d abb%d %s" % (w, w, rd), T.so[:, row, 3 * j:150], T.ab[:, w, 3 * j:150], T.dt3[:, d, 3 * j:150])
-
-            if n == 13:
-                search("sg13", "dg1", 30, 2)
-                scan("pe", "pa16 po0", T.pe[:], T.pa16[:], T.pt[:, 0:256:4])
-            search("so%d" % n, "tb1 tk1" if n < 5 else "tb2 tk1b", n, 0)
+                search("sg13", "dg1", 27, 1)
+            search("so%d" % n, "tb1 tk1 sig" if n < 5 else "tb1b tk1b", n, 0)
+            if 2 <= n < 13:
+                marks(1)
+            if n < 13:
+                search("sg%d" % n, "dg1", 14 + n, 1)
             if n == 1:
-                tt("tbb", "tbm", T.tbb[:, 10:50], T.tbb[:, 10:50], word(10, 50), Op.mult)
-                act("tbd", "tb2", T.tbb[:, 0:10], word(0, 10))
-            if n == 11:
-                ts("ca", " ".join("cd%d" % m for m in range(11)), T.ca[:], T.cde[:], 15, Op.bitwise_and)
-            if n in (11, 12):
-                search("sg%d" % n, "dg1", 17 + n, 2)
-            search("sw%d" % n, "tc1 tc3" if n < 5 else "tc1b tc3b", 14 + n, 1)
-            if n < 11:
-                cd(n - 1)
+                for h, sl in halves:
+                    tt("tbp", "ps5 cg", T.tbp[sl], ps[5][sl, 49 + 24 * h:69 + 24 * h], T.cg[sl], Op.add, more=h > 0)
+            elif n < 12:
+                next(rest if n in (5, 7, 10) else big, None)
             if n == 12:
-                drew(11)
-            if n >= 3:
-                undrawn(0 if n == 3 else n - 2)
-        s = T.so[:, 13, 149:150]
+                scan("pe", "pa16 " + " ".join("po%d" % m for m in range(1, 12)), T.pe[:], T.pa16[:], T.pt[:, 0:256:4])
+        s = T.so[:, 13, 179:180]
+        tt("pc", "pe po12 pc0", T.pc[:, 0:256:65], T.pe[:, 15:64:16], T.pt[:, 8:256:64], Op.add)
+        list(blank)
         steps(13)
-        need("v", "v", reads["po0"]["v"])
         drew(13)
-        for e in range(4):
-            ts("po3", "sg13 pe pt0", T.pt[:, 256 + 65 * e:257 + 65 * e], T.so[:, 30, 149:150], T.grp[:, 0, e:e + 1], Op.is_equal, T.pe[:, 16 * e + 15:16 * e + 16], Op.add, more=e > 0)
-            if e == 1:
-                ts("ne13", "so13 tbp ne0", T.ne[:, :, 1:64:16], T.tbp[:, 0, :], s, Op.not_equal)
-
-        def before(i):
-            scan("uopp", "ne ne13 dp", T.uop[:, 0, i, :], T.ne[:, i, :], T.dp[:], more=i > 0)
-
-        undrawn(12)
-        before(0)
-        before(1)
-        quant("ptq", "po0 po1 po3 ptqz", T.ptq[:, 0:128], T.pts[:, 0:128], T.pt[:])
+        ts("ne13", "so13 tbp ne0", T.ne[:, 1:320:16], T.tbp[:], s, Op.not_equal)
+        quant("pcq", "pc", T.pcq[:], T.pcs[:], T.pc[:])
+        mm("ps4", "pcq qwt1", (ps[4][:, 0:128], *W3(1), T.pcq[:], T.pcs[:]), done=False)
+        quant("ptq", "ptqz pq13 " + " ".join("po%d pp%d" % (m, m) for m in range(1, 14)), T.ptq[:, 0:128], T.pts[:, 0:128], T.pt[:])
         mm("ps4", "ptq ptqz qwt0 qwt1", (ps[4][:, 0:128], *W3(0), T.ptq[:, 0:128], T.pts[:, 0:128]),
-           (ps[4][:, 0:128], *W3(1), T.ptq[:, 64:192], T.pts[:, 64:192]))
-        tt("fl und1", "und0 ne13", T.und[:, 1, :], T.und[:, 0, :], T.ne[:, :, 1:64:16], Op.mult)
-        for i in range(2, 5):
-            before(i)
-        form_of = {"p": (0, 0, (15, 16, 32, 896), T.dgp, 0, 190), "q": (1, 4, (15, -16), T.dgr, 190, 150)}
+           (ps[4][:, 0:128], *W3(1), T.ptq[:, 64:192], T.pts[:, 64:192]), first=False)
+        scan("un", "ne ne13 uc", T.un[:], T.ne[:], T.uc[:])
+        for i in range(5):
+            scan("uopp", "ne ne13 dp", T.uop[:, 0, i, :], T.ne[:, 64 * i:64 * i + 64], T.dp[:], more=i > 0)
+        form_of = {"p": (0, (3, 60), T.dgp), "q": (1, (15, -16), T.dgr)}
 
         def digits(x):
-            j, d0, masks = form_of[x][:3]
+            j, masks = form_of[x][:2]
             for d, m in enumerate(masks):
-                ts("di" + x, "v2" + x, T.dgi[:, d0 + d, :], T.v2[:, j, :], m, Op.bitwise_and, more=d > 0)
+                ts("di" + x, "v2" + x, T.dgi[:, 2 * j + d, :], T.v2[:, j, :], m, Op.bitwise_and, more=d > 0)
 
         def spread(x, blocks=range(4)):
-            j, d0, masks, tile = form_of[x][:4]
-            nd = len(masks)
+            j, masks, tile = form_of[x]
             for nb in blocks:
-                tt("dg" + x, "di%s msk msk0 dg0" % x, tile[:, nb // 2:2 * nd:2, :, nb % 2, :], T.dgi[:, d0:d0 + nd, :], T.msk[:, nb, 0:20 * nd], Op.mult, more=nb > 0)
+                tt("dg" + x, "di%s msk dg0" % x, tile[:, nb // 2:4:2, :, nb % 2, :], T.dgi[:, 2 * j:2 * j + 2, :], T.msk[:, nb, :], Op.mult, more=nb > 0)
 
         def form(x, k):
-            masks, tile, c, w = form_of[x][2:]
-            quant("dq" + x, "dg" + x, T.dgq[:, c:c + w], T.dgs[:, c:c + w], tile[:])
-            mm("ps%d" % k, "dq%s qwt2" % x, *[(ps[k][:, 0:128], *W3(2), T.dgq[:, c + 20 * d:c + 20 * d + 128], T.dgs[:, c + 20 * d:c + 20 * d + 128]) for d in range(len(masks))])
+            j, masks, tile = form_of[x]
+            c = 150 * j
+            quant("dq" + x, "dg" + x, T.dgq[:, c:c + 150], T.dgs[:, c:c + 150], tile[:])
+            mm("ps%d" % k, "dq%s qwt2" % x, *[(ps[k][:, 0:128], *W3(2), T.dgq[:, c + 20 * d:c + 20 * d + 128], T.dgs[:, c + 20 * d:c + 20 * d + 128]) for d in range(2)])
 
-        act("pr0", "fl", T.pr[:], T.und[:, 1, :], 1024.0, bias=-160.0)
         for e in range(4):
-            scan("inc", "pa16 fl n5", T.inc[:, 4 + e:24:4], T.pa16[:, 1:6], T.und[:, 1, e:20:4], more=e > 0, initial=T.inc[:, e:e + 1])
-        ts("v2p", "uopp kf", T.v2[:, 0, :], T.uop[:, 0, :, 13:64:16], 8.0, Op.mult, T.pf[:, 8:9], Op.add)
+            scan("inc", "pa16 un n5", T.inc[:, 4 + e:24:4], T.pa16[:, 4:9], T.un[:, 16 * e + 15:320:64], more=e > 0, initial=T.inc[:, e:e + 1])
+        ts("v2p", "uopp", T.v2[:, 0, :], T.uop[:, 0, :, 13:64:16], 1 / U, Op.mult, float(MID), Op.add)
         for i in range(5):
-            scan("uopq", "ne ne13 ps4", T.uop[:, 1, i, :], T.ne[:, i, :], ps[4][:, 0:64], more=i > 0)
+            scan("uopq", "ne ne13 ps4", T.uop[:, 1, i, :], T.ne[:, 64 * i:64 * i + 64], ps[4][:, 0:64], more=i > 0)
             if i == 2:
-                tt("pr", "pr0 inc", T.pr[:], T.pr[:], T.inc[:, 0:20], Op.min)
-        tt("v2q", "uopq pr", T.v2[:, 1, :], T.uop[:, 1, :, 15:64:16], T.pr[:], Op.add)
-        digits("p")
-        digits("q")
-        spread("p", (0,))
-        spread("q")
-        spread("p", (1,))
-        form("q", 6)
+                tt("pr", "un inc", T.pr[:], T.un[:, 14:320:16], T.inc[:, 0:20], Op.min)
+                digits("p")
+        list(rest)
+        spread("p", (0, 1))
+        tt("v2q", "uopq pr", T.v2[:, 1, :], T.uop[:, 1, :, 14:64:16], T.pr[:], Op.add)
         spread("p", (2, 3))
-        if t == 0:
-            tt("d16", "d16b d16c", T.d16[:, 0, :], T.d16[:, 0, :], T.d16[:, 1, :], Op.subtract)
-        ts("ofq", "ps6", T.ofq[:], ps[6][:, 0:20], 160.0, Op.add)
+        digits("q")
         form("p", 5)
-        do("v", "ofq phr", "row", lambda: V.tensor_copy(T.row[:].indirect(T.ofq[:]), T.phr[:]))
-        copy("ofp", "ps5", T.ofp[:], ps[5][:, 0:20])
-        for b in (2, 3):
-            act("tq%d" % b, "ofp tp", T.tq[:, 320 * b:320 * b + 320], T.tp[:, 320 * b:320 * b + 320].indirect(T.ofp[:]))
+        spread("q")
+        form("q", 6)
+        ts("ofp", "ps5 r7", T.ofp[:], ps[5][:, 0:20], 8.0, Op.mult, T.pf[:, 0:1], Op.add)
+        for b in range(3):
+            act("tq%d" % b, "ofp gap tp%d" % b, T.tq[:, 320 * b:320 * b + 320], plane(T.tp, b).indirect(T.ofp[:]))
 
         def early(b, h):
-            cs = slice(320 * b + 160 * h, 320 * b + 160 * h + 160)
-            tt("tq%d" % b, "ofp tp tw", T.tq[:, cs], T.tp[:, 320 * b:320 * b + 320].indirect(T.ofp[:, 10 * h:10 * h + 10]), T.tw[:, cs], Op.add, more=h > 0)
+            out, cs = T.tz[:, PL * b + 256 * h:PL * b + 256 * h + 160], slice(320 * b + 160 * h, 320 * b + 160 * h + 160)
+            if b < 3:
+                tt("tz%d" % b, "ps%d tq%d" % (b, b), out, ps[b][:, 160 * h:160 * h + 160], T.tq[:, cs], Op.add, more=h > 0)
+            else:
+                tt("tz3", "ofp gap tp3 tq3", out, plane(T.tp, 3).indirect(T.ofp[:, 10 * h:10 * h + 10]), T.tq[:, cs], Op.add, more=h > 0)
 
+        early(3, 0)
+        ts("ofq", "ps6", T.ofq[:], ps[6][:, 0:20], 160.0, Op.add)
+        early(3, 1)
+        do("v", "ofq phr", "row", lambda: V.tensor_copy(T.row[:].indirect(T.ofq[:]), T.phr[:]))
+        early(0, 0)
+        early(0, 1)
         for i in range(5):
             scan("s5", "d16 row", T.s5[:, i, :], T.d16[:, 0, :], T.row[:, 64 * i:64 * i + 64] if final else T.row[:, i:320:5], more=i > 0, ops=(Op.add, Op.min))
-        early(0, 0)
+        early(1, 0)
         parts = [(slice(0, 20), slice(0, 4))] if final else [(slice(10 * h, 10 * h + 10), slice(2 * h, 2 * h + 2)) for h in range(2)]
         for h, (o, v) in enumerate(parts):
             ts("offa%d" % h, "s5 cb", T.offa[:, o], T.s5[:, :, 15 + 16 * v.start:16 * v.stop:16], T.pf[:, 4:5], Op.add)
-        early(0, 1)
-        early(1, 0)
         early(1, 1)
+        early(2, 0)
+        early(2, 1)
 
-        def picks(h):
-            for b in (2, 3):
-                act("at%d%d" % (h, b), "offa%d tp" % (0 if final else h), T.at[:, 640 * h + b:640 * h + 640:4], T.tp[:, 320 * b:320 * b + 320].indirect(T.offa[:, 10 * h:10 * h + 10]))
-
-        def blend(h):
-            for b in range(4):
-                cs, win = slice(640 * h + b, 640 * h + 640, 4), T.tq[:, 320 * b:320 * b + 320].indirect(T.offa[:, 10 * h:10 * h + 10])
-                rd = "offa%d tq%d" % (0 if final else h, b)
-                if (h, b) == (0, 1):
-                    act("zt0", rd, T.zt[:, cs], win, more=True)
-                elif b < 2:
-                    copy("zt%d" % h, rd, T.zt[:, cs], win, more=b > 0)
-                else:
-                    tt("zt%d" % h, rd + " at%d%d" % (h, b), T.zt[:, cs], win, T.at[:, cs], Op.add, more=True)
+        def blend(h, scalar):
+            for b in (3, 0, 1, 2):
+                cs, win = slice(640 * h + b, 640 * h + 640, 4), plane(T.tz, b).indirect(T.offa[:, 10 * h:10 * h + 10])
+                (act if b in scalar else copy)("zt%d%d" % (h, b), "offa%d tz%d" % (0 if final else h, b), T.zt[:, cs], win)
 
         def kept(h):
             for b in range(4):
-                cs = slice(640 * h + b, 640 * h + 640, 4)
-                if b < 2:
-                    act("ak%d%d" % (h, b), "offa%d tp" % (0 if final else h), T.ak[:, cs], T.tp[:, 320 * b:320 * b + 320].indirect(T.offa[:, 10 * h:10 * h + 10]), 2048.0)
-                else:
-                    act("ak%d%d" % (h, b), "at%d%d" % (h, b), T.ak[:, cs], T.at[:, cs], 2048.0)
+                act("ak%d%d" % (h, b), "offa%d tp%d" % (0 if final else h, b), T.ak[:, 640 * h + b:640 * h + 640:4], plane(T.tp, b).indirect(T.offa[:, 10 * h:10 * h + 10]), 2048.0)
 
         def new(h, b, k, cod):
             mm("ps%d" % k, "wq " + cod[0], (ps[k][:, 0:160], T.wq[:, 128 * b:128 * b + 128], T.wsc[:, 128 * b:128 * b + 128], cod[1], cod[2]))
@@ -600,10 +605,9 @@ def rank_program(g, core, T, topo):
                 act("xt%d" % h, "tm%d%d" % (h, b), T.xt[:, h, :, :, b], T.tm[:, 4 * h + b, :], 2.0 ** -11, more=b > 0)
 
         rc = slice(160 * t, 160 * t + 160)
-        picks(0)
-        blend(0)
-        picks(1)
-        quant("send%d" % t, "zt0", T.sendc[:, rc], T.sendp[:, rc], T.zt[:, 0:640])
+        zs = lambda h: " ".join("zt%d%d" % (h, b) for b in range(4))
+        blend(0, (3, 0))
+        quant("send%d" % t, zs(0), T.sendc[:, rc], T.sendp[:, rc], T.zt[:, 0:640])
         dst = partner_of(t)
         rid, pid, _ = topo.addr(dst)
         pre("p", "send%d" % t, "")
@@ -611,12 +615,12 @@ def rank_program(g, core, T, topo):
             g.remote_dma(a, b, T.sem["arr%d" % t], T.sem["snd%d" % t], pid, rid, topo.mask(core, dst))
         eng = 2 * len(topo.engines(core, dst))
         last["land%d" % t] = {"arr%d" % t: eng}
-        blend(1)
+        blend(1, ())
         kept(1)
         kept(0)
         if final:
             act("pk", "lgr offa0", T.pk[:], T.lgr[:].indirect(T.offa[:]))
-        quant("stay", "zt1", T.lq[:, 0:160], T.lsc[:, 0:160], T.zt[:, 640:1280])
+        quant("stay", zs(1), T.lq[:, 0:160], T.lsc[:, 0:160], T.zt[:, 640:1280])
         for b in range(4):
             new(1, b, 4 + b, ("stay", T.lq[:, 0:160], T.lsc[:, 0:160]))
         if t == 0:

import numpy as np
from concourse.mybir import dt, AluOpType as Op, ActivationFunctionType as AF, AxisListType as AX

F, B, I, U16 = "float32", "bfloat16", "int32", "uint16"
C8, U8 = "float8_e4m3fn_x4", "uint8"
PL = 416


def _sb(t, *s):
    return ("sbuf", [128] + list(s), t)


SCRATCH = {
    "xin": _sb(B, 64, 20), "xt": _sb(B, 2, 5, 32, 4), "ut": _sb(B, 512), "vt": _sb(B, 512),
    "xq": _sb(C8, 320), "xs": _sb(U8, 320), "uq": _sb(C8, 128), "us": _sb(U8, 128), "vq": _sb(C8, 128), "vs": _sb(U8, 128),
    "uq0": _sb(C8, 128), "us0": _sb(U8, 128), "uo": _sb(U16, 8), "uf": _sb(F, 8),
    "wq": _sb(C8, 512), "wsc": _sb(U8, 512), "lq": _sb(C8, 160), "lsc": _sb(U8, 160),
    "sc": _sb(F, 8, 5, 4), "cm": _sb(B, 4, 8, 5), "a2": _sb(B, 7, 40), "hb": _sb(B, 3, 120), "pd": _sb(B, 80),
    "eqr": _sb(B, 5, 80), "prb": _sb(B, 5, 80), "rt": _sb(B, 2, 376), "rq": _sb(C8, 198), "rs": _sb(U8, 198),
    "tbb": _sb(B, 120), "val": _sb(B, 2, 60), "ab": _sb(B, 2, 360), "dt2": _sb(B, 2, 180),
    "so": _sb(B, 28, 180), "tbp": _sb(F, 20), "sqp": _sb(F, 3, 20), "tt4": _sb(F, 2, 4),
    "pe": _sb(F, 64), "pt": _sb(B, 512), "ptq": _sb(C8, 192), "pts": _sb(U8, 192), "pc": _sb(B, 512), "pcq": _sb(C8, 128), "pcs": _sb(U8, 128),
    "ne": _sb(B, 320), "un": _sb(B, 320), "dp": _sb(F, 64), "uop": _sb(F, 2, 5, 64),
    "inc": _sb(F, 24), "pr": _sb(F, 20), "v2": _sb(I, 2, 20), "dgi": _sb(I, 4, 20), "dgp": _sb(B, 15, 5, 2, 4), "dgr": _sb(B, 15, 5, 2, 4),
    "dgq": _sb(C8, 300), "dgs": _sb(U8, 300), "ofp": _sb(U16, 20), "ofq": _sb(U16, 20), "pk": _sb(F, 320), "row": _sb(F, 320),
    "s5": _sb(F, 5, 64), "offa": _sb(U16, 20),
    "tp": _sb(B, 4 * PL), "tq": _sb(B, 1280), "tz": _sb(B, 4 * PL), "zt": _sb(B, 1280), "ak": _sb(B, 1280), "tm": _sb(F, 8, 160),
    "zz": _sb(B, 512), "zf": _sb(F, 4), "wm": _sb(B, 64, 4), "wat": _sb(B, 160, 4), "i16": _sb(B, 64),
    "waq": _sb(C8, 160), "was": _sb(U8, 160), "et": _sb(B, 516), "eqc": _sb(C8, 512), "eqs": _sb(U8, 512),
    "w3": _sb(B, 3, 128, 4), "cq3": _sb(C8, 384), "cs3": _sb(U8, 384),
    "n40": _sb(I, 40), "nb40": _sb(I, 40), "msk": _sb(F, 4, 40), "cg": _sb(F, 20), "grp": _sb(F, 4), "gi": _sb(I, 2, 4),
    "tv": _sb(F, 60), "val1": _sb(B, 2, 60), "pi": _sb(I, 8), "pf": _sb(F, 12), "c0": _sb(F, 2, 10),
    "av": _sb(I, 2, 10), "stv": _sb(F, 3, 12), "stt": _sb(F, 48), "uc": _sb(B, 320),
    "pa": _sb(B, 120), "pa16": _sb(F, 64), "d16i": _sb(I, 64), "d16": _sb(F, 2, 64),
    "phr": _sb(F, 320), "lgr": _sb(F, PL),
}
for _k in ("send", "land"):
    SCRATCH[_k + "c"] = _sb(C8, 480)
    SCRATCH[_k + "p"] = _sb(U8, 480)
for _t in range(8):
    SCRATCH["ps%d" % _t] = ("psum", [128, 512], F)
SEMAPHORES = ["v", "s", "t", "dx0", "dx1", "du", "dw", "dv", "fin"] + ["p%d" % i for i in range(60)] + ["%s%d" % (a, i) for a in ("arr", "snd") for i in range(3)]

EPS = 2.0 ** -24
U = 2.0 ** -10
MID = 248
LOW = 512.0
PARTNER = [1, 2, 3]


def rank_program(g, core, T, topo):
    rank = T.rank_of(core)
    if rank is None:
        return
    queue = {"v": g.vector, "s": g.scalar, "t": g.tensor, "p": g, "y": g.sync}
    count, known, last, reads = {}, {e: {} for e in queue}, {}, {}

    def need(e, sem, val):
        if known[e].get(sem, 0) < val:
            queue[e].wait_ge(T.sem[sem], val)
            known[e][sem] = val

    def pre(e, rd, wr):
        for k in rd.split():
            for s, n in last.get(k, {}).items():
                need(e, s, n)
        for k in wr.split():
            for s, n in list(last.get(k, {}).items()) + list(reads.get(k, {}).items()):
                need(e, s, n)

    def post(sem, n, rd, wr, more=False):
        count[sem] = count.get(sem, 0) + n
        for k in rd.split():
            reads.setdefault(k, {})[sem] = count[sem]
        for k in wr.split():
            old = last.get(k, {}) if more else {}
            last[k] = {**old, sem: count[sem]}
            if not more:
                reads[k] = {}

    open_p = {"up": [], "all": [], "lo": []}

    def do(e, rd, wr, call, sem=None, n=1, more=False, part="all"):
        pre(e, rd, "" if more else wr)
        if e == "p":
            sem = "p%d" % sum(k[0] == "p" for k in count)
            for k in open_p[{"up": "all", "all": "up", "lo": "lo"}[part]]:
                need("p", k, 1)
            if part != "lo":
                open_p[part].append(sem)
        if more:
            for k in wr.split():
                for s, c in reads.get(k, {}).items():
                    if s != e:
                        need(e, s, c)
        sem = sem or e
        call().then_inc(T.sem[sem], n)
        post(sem, n, rd, wr, more)

    V, S, P, Y = g.vector, g.scalar, g, g.sync

    def tt(wr, rd, out, a, b, op, more=False):
        do("v", rd, wr, lambda: V.tensor_tensor(out, a, b, op), more=more)

    def ts(wr, rd, out, a, s1, op0, s2=None, op1=None, more=False):
        if op1 is None:
            do("v", rd, wr, lambda: V.tensor_scalar(out, a, s1, None, op0), more=more)
        else:
            do("v", rd, wr, lambda: V.tensor_scalar(out, a, s1, s2, op0, op1), more=more)

    def scan(wr, rd, out, a, b, more=False, ops=(Op.mult, Op.add), initial=0.0):
        do("v", rd, wr, lambda: V.tensor_tensor_scan(out, a, b, initial, ops[0], ops[1]), more=more)

    def copy(wr, rd, out, a, more=False):
        do("v", rd, wr, lambda: V.tensor_copy(out, a), more=more)

    def fill(wr, out, c, more=False):
        do("v", "", wr, lambda: V.memset(out, c), more=more)

    def quant(wr, rd, q, s, t, more=False):
        do("v", rd, wr, lambda: V.quantize_mx(q, s, t), more=more)

    def act(wr, rd, out, a, scale=1.0, more=False, bias=None, func=None):
        if bias is not None:
            do("s", rd, wr, lambda: S.activation(out, a, func or AF.Identity, bias=bias, scale=scale), more=more)
        else:
            do("s", rd, wr, lambda: S.activation(out, a, func or AF.Copy, scale=scale), more=more)

    def const(wr, out, n, c, more=False, rd=""):
        act(wr, "zz " + rd, out, T.zz[:, 0:n], bias=c, more=more)

    def iota(wr, out, pat, base, cm, more=False, part="all"):
        do("p", "", wr, lambda: P.iota(out, pat, base, cm), more=more, part=part)

    def iotaf(wr, out, pat, base, cm=0, more=False, part="all"):
        do("p", "", wr, lambda: P.iota(out, pat, base, cm, allow_small_or_imprecise_dtypes=True), more=more, part=part)

    def select(wr, rd, out, a, pat, op, c, base, cm, more=False, part="all"):
        do("p", rd, wr, lambda: P.affine_select(out, a, pat, op, c, base, cm), more=more, part=part)

    def mm(wr, rd, *prods, first=True, done=True):
        pre("t", rd, wr if first else "")
        for i, p in enumerate(prods):
            ins = g.tensor.matmul_mx(*p, first and i == 0, done and i == len(prods) - 1)
        ins.then_inc(T.sem.t, 1)
        post("t", 1, rd, wr)

    do("y", "", "xin1", lambda: Y.dma_start(T.xin[:, 32:64, :], T.x[:, 640:1280]), "dx1", 16)
    do("s", "", "ut", lambda: S.dma_start(T.ut[:], T.u[:]), "du", 16)
    do("y", "", "xin0", lambda: Y.dma_start(T.xin[:, 0:32, :], T.x[:, 0:640]), "dx0", 16)

    lo, up = slice(0, 64), slice(64, 128)
    halves, part = ((0, lo), (1, up)), ("lo", "up")
    fill("zz", T.zz[:], 0.0)
    fill("et0", T.et[:], 0.0)
    iota("pi", T.pi[:], [[0, 8]], 0, 1)
    iotaf("uf", T.uf[:], [[0, 4], [-64, 2]], 112)
    iota("av", T.av[:, 0, :], [[-8, 10]], 72, 1)
    select("wm1", "zz", T.wm[lo], T.zz[lo, 0:256], [[-1, 64], [8, 4]], Op.not_equal, 1.0, -56, 1, part="lo")
    iotaf("c0i", T.c0[:, 0, 0:2], [[-1, 2]], 1)
    iotaf("c0i", T.c0[:, 0, 2:10], [[-1, 8]], 7, more=True)
    select("wm", "wm1", T.wm[lo], T.wm[lo], [[-1, 64], [8, 4]], Op.not_equal, 1.0, 8, 1, part="lo")
    iotaf("tv0", T.tv[:, 12:60], [[-64, 8], [0, 6]], 258)
    select("et", "zz et0", T.et[:, 3:515:4], T.zz[:, 0:128], [[-1, 128]], Op.not_equal, 0.5, 0, 1)
    iota("d16i", T.d16i[:], [[1, 64]], 128, -1)
    for j in range(2):
        iotaf("pd0", T.pd[up, j:80:2], [[0, 8], [2 * j - 1, 5]], 0, more=True, part="up")
    for h, sl in halves:
        iotaf("gc", T.grp[sl, :], [[-1, 4]], 8 - 4 * h, more=True, part=part[h])
        iota("n40", T.n40[sl, :], [[0, 10], [-8, 4]], 120 - 32 * h, 1, more=True, part=part[h])
        iota("gi", T.gi[sl, 0, :], [[1, 4]], 4 * h, 0, more=True, part=part[h])

    def orders(j):
        if j == 0:
            for h, sl in halves:
                cs = slice(64 * h, 64 * h + 64)
                select("wt0", "w30", T.w3[sl, 0, cs, 0], T.w3[sl, 0, cs, 0], [[-1, 64]], Op.is_ge, 1.0, 0, 1, more=True, part=part[h])
                select("wt0", "w30", T.w3[sl, 0, cs, 1], T.w3[sl, 0, cs, 1], [[1, 64]], Op.is_gt, 1.0, 0, -1, more=True, part=part[h])
            return
        for step in range(2):
            for h, sl in halves:
                for e in range(4):
                    k0 = 64 - (56 - 32 * h - 8 * e) % 64
                    a, b = T.w3[sl, 1, 64 * h:64 * h + k0, e], T.w3[sl, 1, 64 * h + k0:64 * h + 64, e]
                    name = "wt1%d%d" % (h, e)
                    if step == 0:
                        select(name + "a", "w31", a, a, [[-1, k0]], Op.is_ge, -1.0, 0, 1, part=part[h])
                        if k0 < 64:
                            select(name + "b", "w31", b, b, [[-1, 64 - k0]], Op.is_ge, -1.0, -k0, 1, part=part[h])
                    elif k0 < 64:
                        select(name + "a", name + "a", a, a, [[0, k0]], Op.is_gt, -1.0, k0, -1, part=part[h])
                        select(name + "b", name + "b", b, b, [[0, 64 - k0]], Op.is_ge, 0.0, -k0, 1, part=part[h])
        iotaf("phr", T.phr[:], [[256, 2], [1, 160]], 0)
        for h in range(2):
            iotaf("lgr", T.lgr[:, 256 * h:256 * h + 160], [[1, 5], [5, 32]], 160 * h, more=True)

    def state(h):
        quant("xq%d" % h, "xt%d" % h, T.xq[:, 160 * h:160 * h + 160], T.xs[:, 160 * h:160 * h + 160], T.xt[:, h, :, :, :])

    def places(h):
        for i in range(5):
            (copy if i < 4 else act)("xt%d" % h, "xin%d" % h, T.xt[:, h, i, :, :], T.xin[:, 32 * h:32 * h + 32, 4 * i:4 * i + 4], more=True)

    def turner(sl, c, pieces):
        for a, w in pieces:
            act("wat", "wm", T.wat[sl, a:a + w, :], T.wm[lo, 0:w, :], c, more=True)

    ts("pu0", "pi", T.pi[:, 2:3], T.pi[:, 2:3], 3, Op.bitwise_and)
    ts("pu1", "pi", T.pi[:, 3:4], T.pi[:, 3:4], 12, Op.bitwise_and)
    ts("pj", "pi", T.pi[:, 0:1], T.pi[:, 0:1], 7, Op.bitwise_and)
    ts("pk0", "pi", T.pi[:, 4:5], T.pi[:, 4:5], 63, Op.bitwise_and, 3, Op.logical_shift_right)
    ts("av1", "av", T.av[:, 0, :], T.av[:, 0, :], 63, Op.bitwise_and, 3, Op.logical_shift_right)
    copy("pu2", "pu0", T.pf[:, 6:7], T.pi[:, 2:3])
    ts("pu3", "pu1", T.pf[:, 7:8], T.pi[:, 3:4], -4.0, Op.mult)
    copy("r7", "pj", T.pf[:, 0:1], T.pi[:, 0:1])
    quant("rqz", "zz", T.rq[:, 70:198], T.rs[:, 70:198], T.zz[:])
    ts("av2", "av1", T.av[:, 1, :], T.av[:, 0, :], 4.0, Op.is_ge, 28.0, Op.mult)
    ts("uo", "uf pu2 pu3", T.uo[:], T.uf[:], T.pf[:, 6:7], Op.add, T.pf[:, 7:8], Op.add)
    fill("w30", T.w3[:, 0, :, :], 0.0)
    tt("stv", "av1 av2", T.stv[:, 0, 0:10], T.av[:, 0, :], T.av[:, 1, :], Op.add)
    quant("uq0", "ut", T.uq0[:], T.us0[:], T.ut[:])
    const("pa", T.pa[:], 120, 2.0)
    const("eq0", T.eqr[:, :, 0:80:2], 200, 1.0)
    const("dt0", T.dt2[:], 360, 0.0)
    const("pa", T.pa[:, 0:120:3], 40, 0.0)
    const("tv1", T.tv[:, 0:12], 12, 258.0)
    const("zf", T.zf[:], 4, 0.0)
    const("stz", T.stv[:, 0, 10:11], 1, 0.0)
    const("abk", T.ab[:, :, 0:180:3], 120, 1 / EPS)
    const("dg1", T.dt2[:, 1, 16:180:18], 10, 1 / EPS, rd="dt0")
    places(1)
    ts("c0a", "c0i r7", T.c0[:, 1, :], T.c0[:, 0, :], T.pf[:, 0:1], Op.is_equal)
    places(0)
    do("v", "uq0 uo", "uq", lambda: V.tensor_copy(T.uq[:].bitcast(dt.uint32), T.uq0[:].bitcast(dt.uint32).indirect(T.uo[:])))
    do("s", "uq0 uo", "uq", lambda: S.activation(T.us[:], T.us0[:].indirect(T.uo[:]), AF.Copy), more=True)
    state(1)
    state(0)
    do("y", "xin0", "wq", lambda: Y.dma_start(T.wq[:].bitcast(dt.uint8), T.wc[:]), "dw", 16, more=True)
    do("y", "", "wq", lambda: Y.dma_start(T.wsc[:], T.ws[:]), "dw", 16, more=True)
    do("y", "", "vt", lambda: Y.dma_start(T.vt[:], T.v[:]), "dv", 16)
    const("dg1", T.dt2[:, 1, 34:35], 1, -7 / EPS)
    const("tv", T.tv[:, 5:60:6], 10, -1 / U, rd="tv0 tv1")
    turner(lo, 64 * U, ((0, 64), (64, 64), (128, 32)))
    fill("rt0", T.rt[:], 0.0)
    tt("sg0", "stv stz", T.stv[:, 1, 0:10], T.stv[:, 0, 0:10], T.stv[:, 0, 1:11], Op.subtract)
    tt("st1", "stv c0a", T.stv[:, 2, 0:8], T.stv[:, 0, 2:10], T.c0[:, 1, 2:10], Op.mult)
    orders(0)

    def tables():
        fill("w31", T.w3[:, 1, :, :], 0.0)
        orders(1)
        yield
        turner(up, 4 * U, ((0, 64),))
        yield
        turner(up, 4 * U, ((64, 64),))
        yield
        do("v", "st1", "st2", lambda: V.tensor_reduce(T.pf[:, 1:2], T.stv[:, 2, 0:8], AX.X, Op.add))
        next(big)
        yield
        turner(up, 4 * U, ((128, 32),))
        act("v0", "tv", T.val1[:, 0, :], T.tv[:], U)
        act("v0a", "tv", T.val1[:, 1, :], T.tv[:], U, bias=222 * U)
        yield
        quant("wa", "wat", T.waq[:], T.was[:], T.wat[:])
        ts("st0", "st2", T.pf[:, 2:3], T.pf[:, 1:2], U, Op.mult, -MID * U, Op.add)
        for r in range(6):
            act("stt", "stv", T.stt[:, r:48:6], T.stv[:, 0, 2:10], U, bias=-MID * U if r < 5 else 1.0, more=True)
        act("sig", "sg0 dt0", T.dt2[:, 0, 16:180:18], T.stv[:, 1, 0:10], U / EPS)
        yield
        for j in range(2):
            tt("val1", "v0 v0a c0a", T.val1[:, j, 4:60:6], T.val1[:, j, 4:60:6], T.c0[:, 1, :], Op.subtract, more=j > 0)
        for h, sl in halves:
            for i in range(5):
                act("cg", "stv", T.cg[sl, 4 * i:4 * i + 4], T.stv[sl, 0, 2 + 4 * h:6 + 4 * h], U, bias=(4 * i - MID) * U, more=True)
        const("ne0", T.ne[:, 0:320:16], 20, 0.0)
        const("ne0", T.ne[:, 15:320:16], 20, 1 / 1024, more=True)
        const("dp0", T.dp[:], 64, 0.0)
        fill("pt0", T.pt[:], 0.0)
        const("w32", T.w3[:, 2, :, :], 512, 0.0)
        yield

    def zeros():
        for k, a, b in (("dgp", 0, 8), ("dgp", 8, 15), ("dgr", 0, 8), ("dgr", 8, 15)):
            act("dg0", "zz", T[k][:, a:b, :, :, :], T.zz[:, 0:40 * (b - a)], more=True)
            yield
        const("pc0", T.pc[:], 512, 0.0)
        yield
        const("uc", T.uc[:], 320, 0.0)
        const("pa16", T.pa16[:], 64, 1.0)
        yield
        for b in range(4):
            for k in ("tp", "tz"):
                const("gap", T[k][:, PL * b + 160:PL * b + 256], 96, 0.0, more=True)
            if b == 1:
                const("pa16", T.pa16[:, 3:64:16], 4, 0.0)
            if b % 2:
                yield
        const("uc", T.uc[:, 0:320:16], 20, 1024.0)
        const("uc", T.uc[:, 13:320:16], 20, T.pf[:, 8:9], more=True, rd="kh")
        const("uc", T.uc[:, 14:320:16], 20, T.pf[:, 9:10], more=True, rd="kh")
        const("uc", T.uc[:, 15:320:16], 20, 152 / 1024, more=True)
        const("lgr", T.lgr[:, 160:256], 96, 0.0, more=True)
        yield

    def numbers():
        ts("d16a", "d16i", T.d16i[:], T.d16i[:], 15, Op.bitwise_and)
        ts("n40b", "n40", T.n40[:], T.n40[:], 63, Op.bitwise_and)
        ts("kh", "pk0", T.pf[:, 8:9], T.pi[:, 4:5], -1.0, Op.mult, 8.0, Op.add)
        ts("kh", "pk0", T.pf[:, 9:10], T.pi[:, 4:5], -160.0, Op.add, more=True)
        yield
        ts("i16", "d16a", T.i16[:], T.d16i[:], 0, Op.is_equal)
        yield
        ts("nb40", "n40b", T.nb40[:], T.n40[:], 4, Op.logical_shift_right)
        for h, sl in halves:
            for e in range(4):
                m, c = 16 * (7 - 4 * h - e), 8 * ((e + 1) % 2)
                act("wt2", "i16 w32", T.w3[sl, 2, m:m + 16, e], T.i16[sl, c:c + 16], more=True)
        yield
        tt("gi1", "gi n40b", T.gi[:, 0, :], T.gi[:, 0, :], T.n40[:, 0:4], Op.add)
        yield
        ts("n5a", "n40b", T.pr[:, 0:4], T.n40[:, 0:4], 5.0, Op.mult, -152.0, Op.add)
        yield
        ts("gi2", "gi1", T.gi[:, 1, :], T.gi[:, 0, :], 3, Op.logical_shift_right)
        yield
        ts("d16b", "d16a", T.d16[:, 0, :], T.d16i[:], 0, Op.is_equal, 4 * LOW, Op.mult)
        yield
        ts("d16c", "d16a", T.d16[:, 1, :], T.d16i[:], 1, Op.is_equal, LOW, Op.mult)
        yield
        tt("n5 pr", "n5a gi2", T.inc[:, 0:4], T.pr[:, 0:4], T.gi[:, 1, :], Op.subtract)
        yield
        ts("cb", "d16a", T.pf[:, 4:5], T.d16i[:, 15:16], 0, Op.not_equal, LOW, Op.mult)
        yield
        for nb in range(4):
            ts("msk", "nb40", T.msk[:, nb, :], T.nb40[:], nb, Op.is_equal, more=True)
            yield
        tt("d16", "d16b d16c", T.d16[:, 0, :], T.d16[:, 0, :], T.d16[:, 1, :], Op.subtract)
        yield

    def tiles():
        for b in range(4):
            quant("e%d" % b, "et", T.eqc[:, 128 * b:128 * b + 128], T.eqs[:, 128 * b:128 * b + 128], T.et[:, 3 - b:515 - b])
            yield
        quant("ptqz", "zz", T.ptq[:, 64:192], T.pts[:, 64:192], T.zz[:])
        yield
        for j in (0, 2, 1):
            rd = " ".join(k for k in last if k.startswith("wt%d" % j))
            quant("qwt%d" % j, rd, T.cq3[:, 128 * j:128 * j + 128], T.cs3[:, 128 * j:128 * j + 128], T.w3[:, j, :, :])
            yield

    tab, blank, rest, big = tables(), zeros(), numbers(), tiles()

    def W3(j):
        return T.cq3[:, 128 * j:128 * j + 128], T.cs3[:, 128 * j:128 * j + 128]

    ps = [T["ps%d" % i] for i in range(8)]
    partner_of = lambda t: T.cores[rank ^ PARTNER[t]]

    def scores(h, banks):
        for j, k in enumerate(banks):
            c = 160 * h + 32 * j
            mm("ps%d" % k, "xq%d uq" % h, (ps[k][:, 0:128], T.xq[:, c:c + 128], T.xs[:, c:c + 128], T.uq[:], T.us[:]))

    def bring(h, banks):
        for i in range(5):
            out = T.sc[32 * h:32 * h + 32, :, i, :]
            if i < 3:
                copy("sc%d" % h, "ps%d" % banks[0], out, ps[banks[0]][32 * i:32 * i + 32, 0:32], more=i > 0)
            else:
                act("sc%d" % h, "ps%d" % banks[1], out, ps[banks[1]][32 * i - 32:32 * i, 0:32], more=True)

    def unpack():
        for b in range(4):
            mm("ps%d" % b, "xq0 xq1 e%d" % b, (ps[b][:, 0:320], T.eqc[:, 128 * b:128 * b + 128], T.eqs[:, 128 * b:128 * b + 128], T.xq[:, 0:320], T.xs[:, 0:320]))
        yield
        for b in range(4):
            for h in range(2):
                act("tp%d" % b, "ps%d" % b, T.tp[:, PL * b + 256 * h:PL * b + 256 * h + 160], ps[b][:, 160 * h:160 * h + 160], more=h > 0)
                yield
        act("tq3", "ps3", T.tq[:, 960:1280], ps[3][:, 0:320])
        yield

    plane = lambda buf, b: buf[:, PL * b:PL * b + PL]

    for t in range(3):
        final = t == 2
        if t == 0:
            scores(1, (4, 5))
        scores(0, (6, 7))
        bring(1, (4, 5))
        bring(0, (6, 7))
        next(tab, None)
        planes = unpack()
        if t > 0:
            next(planes)
        key = lambda a, b: T.sc[lo, :, a:b, 3]
        for s in range(1, 5):
            tt("cm%d" % s, "sc0 sc1", T.cm[lo, s - 1, :, 0:5 - s], key(s, 5), key(0, 5 - s), Op.is_gt)
            tt("cm%d" % s, "sc0 sc1", T.cm[lo, s - 1, :, 5 - s:5], key(0, s), key(5 - s, 5), Op.is_ge, more=True)
        for j in range(2):
            for h, sl in halves:
                tt("a2%d" % j, "cm%d cm%d" % (2 * j + 1, 2 * j + 2), T.a2[sl, 5 + j, :], T.cm[lo, 2 * j, :, :], T.cm[lo, 2 * j + 1, :, :], Op.add, more=h > 0)
        act("hb0", "sc0 sc1", T.hb[lo, 0, :], T.sc[lo, :, :, 0:3], func=AF.Sign)
        next(tab, None)
        act("hb1", "hb0", T.hb[lo, 1, :], T.hb[lo, 0, :], func=AF.Relu)
        next(tab, None)
        order = (4, 0, 1, 2, 3)
        for r in order:
            act("ar%d" % r, "a20", T.a2[:, r, :], T.a2[:, 5, :], -1.0, bias=4.0 - r)
        scan("sym", "pa hb1", T.hb[lo, 2, :], T.pa[lo], T.hb[lo, 1, :])
        next(tab, None)
        for j in range(2):
            act("pd", "sym pd0", T.pd[lo, j:80:2], T.hb[lo, 2, 2:120:3], 2.0 * j - 1, more=j > 0)
        for r in order:
            tt("eqr%d" % r, "ar%d a21 eq0" % r, T.eqr[:, r, 1:80:2], T.a2[:, r, :], T.a2[:, 6, :], Op.not_equal)
        for i in range(5):
            act("rtu", "sym rt0", T.rt[lo, :, 196 + 16 * i:212 + 16 * i:5], T.hb[lo, 2, 2 + 3 * i:120:15], more=i > 0)
        next(tab, None)
        for r in order:
            scan("prb%d" % r, "eqr%d pd" % r, T.prb[:, r, :], T.eqr[:, r, :], T.pd[:])
            act("rts", "prb%d rt0" % r, T.rt[:, :, 4 * r:4 * r + 76:25], T.prb[:, r, 9:80:10], more=r != 4)
        for a, c in ((0, 192), (1, 96)):
            tt("rt1", "prb4 c0a rt0", T.rt[:, a, c:c + 4], T.prb[:, 4, 9 + 40 * a:40 + 40 * a:10], T.c0[:, 1, 2 + 4 * a:6 + 4 * a], Op.mult, more=a > 0)
        next(tab, None)
        const("abb1", T.ab[:, 1, 2:180:3], 60, EPS)

        quant("rq", "rts rtu rt1 rqz", T.rq[:, 0:188], T.rs[:, 0:188], T.rt[:])
        mm("ps5", "wa rq", *[(ps[5][:, 0:128], T.waq[:, w:w + 128], T.was[:, w:w + 128], T.rq[:, c:c + 128], T.rs[:, c:c + 128])
                             for w, c in ((0, 0), (32, 70))])
        list(tab)
        next(rest, None)
        next(rest, None)
        tt("tbw", "ps5 stt", T.tbb[:, 72:120], ps[5][:, 0:48], T.stt[:], Op.add)
        ts("tb1", "ps5 dt0", T.dt2[:, 0, 38:180:3], ps[5][:, 0:48], -MID * U, Op.add)
        ts("tk1", "ps5 dt0", T.dt2[:, 0, 36:180:3], ps[5][:, 0:48], -MID * U, Op.add, -1 / EPS, Op.mult)
        act("tbw2", "tbw", T.tbb[:, 60:72], T.tbb[:, 108:120])
        act("tbd", "tbw", T.tbb[:, 0:12], T.tbb[:, 108:120])
        for k, c in (("tb1", 2), ("tk1", 0)):
            act(k + "b", k, T.dt2[:, 0, c:36:3], T.dt2[:, 0, 144 + c:180:3])

        def drew(n):
            s, c = T.so[:, 14 + n, 179:180], 56 - 4 * n
            ts("po%d" % n, "gc pt0 %ssg%d" % ("pe " if n > 11 else "", n), T.pt[:, c:256:64], T.grp[:], s, Op.is_equal)
            if n < 13:
                act("pp%d" % n, "po%d" % n, T.pt[:, c - 3:256:64], T.pt[:, c:256:64])
            else:
                ts("pp13", "gc sg13", T.pt[:, c - 3:256:64], T.grp[:], s, Op.is_equal)
                ts("pq13", "gc sg13", T.pt[:, 256:512:65], T.grp[:], s, Op.is_equal)

        def far(n):
            act("sqp%d" % (n % 3), "tbp so%d" % n, T.sqp[:, n % 3, :], T.tbp[:], -1.0, bias=T.so[:, n, 179:180], func=AF.Square)

        def other(n):
            act("ne", "sqp%d ne0" % (n % 3), T.ne[:, 14 - n:320:16], T.sqp[:, n % 3, :], func=AF.Sign, more=n > 0)

        def steps(n):
            s, so, a = T.so[:, n, 179:180], "so%d" % n, n % 2
            if n == 0:
                act("dp", "zf dp0 " + so, T.dp[:, 13:64:16], T.zf[:], bias=s)
            else:
                act("dp", "tt%d %s" % (1 - a, so), T.dp[:, 13 - n:64:16], T.tt4[:, 1 - a, :], -1.0, bias=s, more=True)
            if n < 13:
                act("tt%d" % a, "zf " + so, T.tt4[:, a, :], T.zf[:], bias=s)

        for n in range(1, 14):
            s, so = T.so[:, n - 1, 179:180], "so%d" % (n - 1)
            j, w = 2 if n < 5 else 1 if n < 10 else 0, n % 2
            vk = "val1" if n < 3 else "vl%d" % w
            old = lambda a, b: T.val1[:, 0, a:b] if n < 3 else T.val[:, w, a:b]

            def marks(a):
                tt("vl%d" % (1 - w), vk + " abb%d" % w, T.val[:, 1 - w, 30 * a:30 * a + 30], old(30 * a, 30 * a + 30), T.ab[:, w, 182 + 90 * a:270 + 90 * a:3], Op.subtract, more=a > 0)

            def search(name, rd, row, d):
                scan(name, "aba%d abb%d %s" % (w, w, rd), T.so[:, row, 18 * j:180], T.ab[:, w, 18 * j:180], T.dt2[:, d, 18 * j:180])

            if n == 1:
                ts("aba1", "val1 abk ps5", T.ab[:, 1, 37:180:3], T.val1[:, 1, 12:60], ps[5][:, 48:49], Op.is_lt, EPS, Op.add)
                ts("so0", "ps5 st0", s, ps[5][:, 48:49], T.pf[:, 2:3], Op.add)
                tt("tbb", "val1 tbw", T.tbb[:, 12:60], T.val1[:, 0, 12:60], T.tbb[:, 72:120], Op.min)
            else:
                ts("abb%d" % w, ("tbb tbw2 " if n < 5 else "tbd ") + so, T.ab[:, w, 18 * j + 2:360:3], T.tbb[:, 6 * j:120], s, Op.is_equal, EPS, Op.add)
                ts("aba%d" % w, vk + " abk " + so, T.ab[:, w, 18 * j + 1:180:3], old(6 * j, 60), s, Op.is_lt, EPS, Op.add)
                drew(n - 1)
                next(rest, None)
            late = range(2) if n == 2 else [n - 1] if n > 2 else []
            for m in late:
                far(m)
            steps(n - 1)
            if t == 0:
                if n == 6:
                    next(planes)
                next(planes if 6 < n < 12 else blank, None)
                if n in (2, 7, 8, 9, 10):
                    next(planes if n > 6 else blank, None)
            elif n > 1:
                next(planes, None)
            for m in late:
                other(m)
            if 2 <= n < 13:
                marks(0)
            if n == 13:
                search("sg13", "dg1", 27, 1)
            search("so%d" % n, "tb1 tk1 sig" if n < 5 else "tb1b tk1b", n, 0)
            if 2 <= n < 13:
                marks(1)
            if n < 13:
                search("sg%d" % n, "dg1", 14 + n, 1)
            if n == 1:
                for h, sl in halves:
                    tt("tbp", "ps5 cg", T.tbp[sl], ps[5][sl, 49 + 24 * h:69 + 24 * h], T.cg[sl], Op.add, more=h > 0)
            elif n < 12:
                next(rest if n in (5, 7, 10) else big, None)
            if n == 12:
                scan("pe", "pa16 " + " ".join("po%d" % m for m in range(1, 12)), T.pe[:], T.pa16[:], T.pt[:, 0:256:4])
        s = T.so[:, 13, 179:180]
        tt("pc", "pe po12 pc0", T.pc[:, 0:256:65], T.pe[:, 15:64:16], T.pt[:, 8:256:64], Op.add)
        list(blank)
        steps(13)
        drew(13)
        ts("ne13", "so13 tbp ne0", T.ne[:, 1:320:16], T.tbp[:], s, Op.not_equal)
        quant("pcq", "pc", T.pcq[:], T.pcs[:], T.pc[:])
        mm("ps4", "pcq qwt1", (ps[4][:, 0:128], *W3(1), T.pcq[:], T.pcs[:]), done=False)
        quant("ptq", "ptqz pq13 " + " ".join("po%d pp%d" % (m, m) for m in range(1, 14)), T.ptq[:, 0:128], T.pts[:, 0:128], T.pt[:])
        mm("ps4", "ptq ptqz qwt0 qwt1", (ps[4][:, 0:128], *W3(0), T.ptq[:, 0:128], T.pts[:, 0:128]),
           (ps[4][:, 0:128], *W3(1), T.ptq[:, 64:192], T.pts[:, 64:192]), first=False)
        scan("un", "ne ne13 uc", T.un[:], T.ne[:], T.uc[:])
        for i in range(5):
            scan("uopp", "ne ne13 dp", T.uop[:, 0, i, :], T.ne[:, 64 * i:64 * i + 64], T.dp[:], more=i > 0)
        form_of = {"p": (0, (3, 60), T.dgp), "q": (1, (15, -16), T.dgr)}

        def digits(x):
            j, masks = form_of[x][:2]
            for d, m in enumerate(masks):
                ts("di" + x, "v2" + x, T.dgi[:, 2 * j + d, :], T.v2[:, j, :], m, Op.bitwise_and, more=d > 0)

        def spread(x, blocks=range(4)):
            j, masks, tile = form_of[x]
            for nb in blocks:
                tt("dg" + x, "di%s msk dg0" % x, tile[:, nb // 2:4:2, :, nb % 2, :], T.dgi[:, 2 * j:2 * j + 2, :], T.msk[:, nb, :], Op.mult, more=nb > 0)

        def form(x, k):
            j, masks, tile = form_of[x]
            c = 150 * j
            quant("dq" + x, "dg" + x, T.dgq[:, c:c + 150], T.dgs[:, c:c + 150], tile[:])
            mm("ps%d" % k, "dq%s qwt2" % x, *[(ps[k][:, 0:128], *W3(2), T.dgq[:, c + 20 * d:c + 20 * d + 128], T.dgs[:, c + 20 * d:c + 20 * d + 128]) for d in range(2)])

        for e in range(4):
            scan("inc", "pa16 un n5", T.inc[:, 4 + e:24:4], T.pa16[:, 4:9], T.un[:, 16 * e + 15:320:64], more=e > 0, initial=T.inc[:, e:e + 1])
        ts("v2p", "uopp", T.v2[:, 0, :], T.uop[:, 0, :, 13:64:16], 1 / U, Op.mult, float(MID), Op.add)
        for i in range(5):
            scan("uopq", "ne ne13 ps4", T.uop[:, 1, i, :], T.ne[:, 64 * i:64 * i + 64], ps[4][:, 0:64], more=i > 0)
            if i == 2:
                tt("pr", "un inc", T.pr[:], T.un[:, 14:320:16], T.inc[:, 0:20], Op.min)
                digits("p")
        list(rest)
        spread("p", (0, 1))
        tt("v2q", "uopq pr", T.v2[:, 1, :], T.uop[:, 1, :, 14:64:16], T.pr[:], Op.add)
        spread("p", (2, 3))
        digits("q")
        form("p", 5)
        spread("q")
        form("q", 6)
        ts("ofp", "ps5 r7", T.ofp[:], ps[5][:, 0:20], 8.0, Op.mult, T.pf[:, 0:1], Op.add)
        for b in range(3):
            act("tq%d" % b, "ofp gap tp%d" % b, T.tq[:, 320 * b:320 * b + 320], plane(T.tp, b).indirect(T.ofp[:]))

        def early(b, h):
            out, cs = T.tz[:, PL * b + 256 * h:PL * b + 256 * h + 160], slice(320 * b + 160 * h, 320 * b + 160 * h + 160)
            if b < 3:
                tt("tz%d" % b, "ps%d tq%d" % (b, b), out, ps[b][:, 160 * h:160 * h + 160], T.tq[:, cs], Op.add, more=h > 0)
            else:
                tt("tz3", "ofp gap tp3 tq3", out, plane(T.tp, 3).indirect(T.ofp[:, 10 * h:10 * h + 10]), T.tq[:, cs], Op.add, more=h > 0)

        early(3, 0)
        ts("ofq", "ps6", T.ofq[:], ps[6][:, 0:20], 160.0, Op.add)
        early(3, 1)
        do("v", "ofq phr", "row", lambda: V.tensor_copy(T.row[:].indirect(T.ofq[:]), T.phr[:]))
        early(0, 0)
        early(0, 1)
        for i in range(5):
            scan("s5", "d16 row", T.s5[:, i, :], T.d16[:, 0, :], T.row[:, 64 * i:64 * i + 64] if final else T.row[:, i:320:5], more=i > 0, ops=(Op.add, Op.min))
        early(1, 0)
        parts = [(slice(0, 20), slice(0, 4))] if final else [(slice(10 * h, 10 * h + 10), slice(2 * h, 2 * h + 2)) for h in range(2)]
        for h, (o, v) in enumerate(parts):
            ts("offa%d" % h, "s5 cb", T.offa[:, o], T.s5[:, :, 15 + 16 * v.start:16 * v.stop:16], T.pf[:, 4:5], Op.add)
        early(1, 1)
        early(2, 0)
        early(2, 1)

        def blend(h, scalar):
            for b in (3, 0, 1, 2):
                cs, win = slice(640 * h + b, 640 * h + 640, 4), plane(T.tz, b).indirect(T.offa[:, 10 * h:10 * h + 10])
                (act if b in scalar else copy)("zt%d%d" % (h, b), "offa%d tz%d" % (0 if final else h, b), T.zt[:, cs], win)

        def kept(h):
            for b in range(4):
                act("ak%d%d" % (h, b), "offa%d tp%d" % (0 if final else h, b), T.ak[:, 640 * h + b:640 * h + 640:4], plane(T.tp, b).indirect(T.offa[:, 10 * h:10 * h + 10]), 2048.0)

        def new(h, b, k, cod):
            mm("ps%d" % k, "wq " + cod[0], (ps[k][:, 0:160], T.wq[:, 128 * b:128 * b + 128], T.wsc[:, 128 * b:128 * b + 128], cod[1], cod[2]))

        def finish(h, b, k):
            tt("tm%d%d" % (h, b), "ps%d ak%d%d" % (k, h, b), T.tm[:, 4 * h + b, :], ps[k][:, 0:160], T.ak[:, 640 * h + b:640 * h + 640:4], Op.add)
            if (h, b) != (0, 3):
                act("xt%d" % h, "tm%d%d" % (h, b), T.xt[:, h, :, :, b], T.tm[:, 4 * h + b, :], 2.0 ** -11, more=b > 0)

        rc = slice(160 * t, 160 * t + 160)
        zs = lambda h: " ".join("zt%d%d" % (h, b) for b in range(4))
        blend(0, (3, 0))
        quant("send%d" % t, zs(0), T.sendc[:, rc], T.sendp[:, rc], T.zt[:, 0:640])
        dst = partner_of(t)
        rid, pid, _ = topo.addr(dst)
        pre("p", "send%d" % t, "")
        for a, b in ((T.landc[:, rc].bitcast(dt.uint8), T.sendc[:, rc].bitcast(dt.uint8)), (T.landp[:, rc], T.sendp[:, rc])):
            g.remote_dma(a, b, T.sem["arr%d" % t], T.sem["snd%d" % t], pid, rid, topo.mask(core, dst))
        eng = 2 * len(topo.engines(core, dst))
        last["land%d" % t] = {"arr%d" % t: eng}
        blend(1, ())
        kept(1)
        kept(0)
        if final:
            act("pk", "lgr offa0", T.pk[:], T.lgr[:].indirect(T.offa[:]))
        quant("stay", zs(1), T.lq[:, 0:160], T.lsc[:, 0:160], T.zt[:, 640:1280])
        for b in range(4):
            new(1, b, 4 + b, ("stay", T.lq[:, 0:160], T.lsc[:, 0:160]))
        if t == 0:
            quant("vq", "vt", T.vq[:], T.vs[:], T.vt[:])
        for b in range(4):
            finish(1, b, 4 + b)
        if final:
            do("y", "pk", "", lambda: Y.dma_start(T.oq[:], T.pk[0:128:16, :]), "fin", 16)
        for b in range(4):
            new(0, b, b, ("land%d" % t, T.landc[:, rc], T.landp[:, rc]))
        for b in range(4):
            finish(0, b, b)
        need("p", "snd%d" % t, eng)
        state(1)
        ts("xt0", "tm03", T.xt[:, 0, :, :, 3], T.tm[:, 3, :], 2.0 ** -11, Op.mult, more=True)
        if final:
            mm("ps4", "xq1 vq", (ps[4][:, 0:160], T.vq[:], T.vs[:], T.xq[:, 160:320], T.xs[:, 160:320]))
            do("y", "xq1", "", lambda: Y.dma_start(T.oc[:, 640:1280], T.xq[:, 160:320].bitcast(dt.uint8)), "fin", 16)
            act("yb1 row", "ps4", T.row[:, 160:320], ps[4][:, 0:160])
            do("y", "yb1", "", lambda: Y.dma_start(T.y[:, 160:320], T.row[:, 160:320]), "fin", 16)
        else:
            scores(1, (4, 5))
        state(0)

    mm("ps5", "xq0 vq", (ps[5][:, 0:160], T.vq[:], T.vs[:], T.xq[:, 0:160], T.xs[:, 0:160]))
    do("y", "xq0", "", lambda: Y.dma_start(T.oc[:, 0:640], T.xq[:, 0:160].bitcast(dt.uint8)), "fin", 16)
    act("yb0", "ps5", T.row[:, 0:160], ps[5][:, 0:160])
    do("s", "yb0", "", lambda: S.dma_start(T.y[:, 0:160], T.row[:, 0:160]), "fin", 16)
    for k in range(4):
        do("y", "xq0 xq1", "", lambda: Y.dma_start(T.osc[4 * k:4 * k + 4, :], T.xs[32 * k:32 * k + 4, :]), "fin", 16)
    for k in count:
        need("y" if k in ("fin", "v", "s", "t") else "p", k, count[k])
